import numpy as np
import ml_dtypes


def mxq(x, axis, fmt="e4m3"):
    dtype, down = {"e4m3": (ml_dtypes.float8_e4m3fn, 7), "e5m2": (ml_dtypes.float8_e5m2, 14)}[fmt]
    v = np.moveaxis(np.asarray(x, np.float32).astype(ml_dtypes.bfloat16).astype(np.float64), axis, -1)
    blocks = v.reshape(v.shape[:-1] + (-1, 32))
    amax = np.abs(blocks).max(-1, keepdims=True)
    byte = np.maximum(np.where(amax > 0, np.frexp(amax)[1] - 1 + 127, 0) - down, 1)
    scale = np.exp2(byte - 127.0)
    codes = (blocks / scale).astype(np.float32).astype(dtype).astype(np.float64)
    return np.moveaxis((codes * scale).reshape(v.shape), -1, axis)


WIDE = False


def mx_kscale(k):
    if not WIDE:
        return np.ones(k)
    levels = np.array([18, -18])
    if k % 512:
        return np.exp2(np.random.permutation(np.resize(levels, k // 32))).repeat(32)
    a = np.empty((k // 512, 16))
    for p in range(k // 512):
        a[p, :8] = np.random.permutation(np.resize(levels, 8))
        for g in range(8):
            far = levels[np.abs(levels - a[p, g]) >= 10]
            a[p, g + 8] = far[np.random.randint(len(far))]
    return np.exp2(a.ravel()).repeat(32)


def f64(x):
    return np.asarray(x).astype(np.float64)


def striped(idx):
    return np.tile(np.asarray(idx).reshape(-1, 16).T, (8, 1)).astype(np.uint16)


def unstriped(offs):
    return offs[:16].T.reshape(-1).astype(np.int64)

def planes(y):
    n, m = y.shape
    v = y.astype(np.float32).astype(ml_dtypes.bfloat16).astype(np.float64).reshape(n // 32, 32, m)
    top = np.abs(v).max(1)
    byte = np.clip(np.where(top > 0, np.frexp(top)[1] - 1 + 127 - 7, 1), 1, 254)
    codes = (v * np.exp2(127.0 - byte)[:, None, :]).reshape(n, m).astype(np.float32).astype(ml_dtypes.float8_e4m3fn).view(np.uint8)
    words = codes.reshape(n // 512, 128, 4, m).transpose(0, 1, 3, 2)
    return np.ascontiguousarray(words), np.ascontiguousarray(byte.astype(np.uint8).reshape(n // 512, 16, m))


def setup_inputs():
    n = np.random.standard_normal
    uni = np.random.uniform
    idx = np.random.permutation(2048)[:512]
    f_d = mx_kscale(512)
    f_r = mx_kscale(512)
    return {
        "xT": (0.5 * n((512, 512)) * f_d[:, None] * f_r[None, :]).astype(np.float32),
        "ws": (n((512, 2048)) / np.sqrt(512) / f_d[:, None]).astype(np.float32),
        "wa": (n((512, 2048)) / np.sqrt(512) / f_d[:, None]).astype(np.float32),
        "wb": (n((512, 2048)) / np.sqrt(512) / f_d[:, None]).astype(np.float32),
        "us": (uni(0.75, 1.3, (512, 1)) / f_r[:, None]).astype(np.float32),
        "ts": np.tile(uni(0.75, 1.3, 2048), (128, 1)).astype(np.float32),
        "la": (uni(0.2, 0.8, (512, 1))).astype(np.float32),
        "wt": (uni(0.75, 1.3, (512, 1))).astype(np.float32),
        "offs": striped(idx),
    }


def reference(xT, ws, wa, wb, us, ts, la, wt, offs):
    idx = unstriped(offs)
    ws_i = f64(ws)[:, idx]
    wa_i = f64(wa)[:, idx]
    wb_i = f64(wb)[:, idx]
    ts_i = f64(ts)[:1][:, idx]
    q_xT = mxq(f64(xT), 0, "e4m3")
    cs = q_xT.T @ mxq(ws_i, 0, "e4m3")
    zs = f64(us) * ts_i * cs
    ms = (zs).max(-1, keepdims=True)
    es = np.exp(zs - ms)
    qs = (es).sum(-1, keepdims=True)
    ca = q_xT.T @ mxq(wa_i, 0, "e4m3")
    za = f64(us) * ts_i * ca
    ma = (za).max(-1, keepdims=True)
    ea = np.exp(za - ma)
    qa = (ea).sum(-1, keepdims=True)
    cb = q_xT.T @ mxq(wb_i, 0, "e4m3")
    zb = f64(us) * ts_i * cb
    mb = (zb).max(-1, keepdims=True)
    eb = np.exp(zb - mb)
    qb = (eb).sum(-1, keepdims=True)
    g = f64(wt) * f64(us) * ts_i * (es / qs - f64(la) * ea / qa - (1.0 - f64(la)) * eb / qb)
    dw = mxq(f64(xT), 1, "e4m3") @ mxq(g, 0, "e5m2")
    out_0 = np.zeros((512, 2048))
    out_0[:, idx] = dw
    return (out_0,) + planes(out_0)

@@ -1,0 +1,274 @@
+from contextlib import ExitStack
+
+import concourse.mybir as mybir
+from concourse.masks import make_identity
+
+F32 = mybir.dt.float32
+BF16 = mybir.dt.bfloat16
+I32 = mybir.dt.int32
+U32 = mybir.dt.uint32
+U16 = mybir.dt.uint16
+U8 = mybir.dt.uint8
+E4M3 = mybir.dt.float8_e4m3fn_x4
+E5M2 = mybir.dt.float8_e5m2_x4
+ALU = mybir.AluOpType
+ACT = mybir.ActivationFunctionType
+
+P = 128
+LANES = 4
+D = 512
+ROWS = 512
+SLOTS = 512
+TOKENS = 2048
+HALF = SLOTS // 2
+CHUNKS = (256, 256, 512, 512, 256, 256)
+WINDOWS = 3
+FLOPS = 4 * 2 * D * ROWS * SLOTS
+
+
+def tile_attend_gkd2_pl_kernel(tc, xT, ws, wa, wb, us, ts, la, wt, offs, out_0, out_1, out_2):
+    nc = tc.nc
+    with ExitStack() as ctx:
+        keep = ctx.enter_context(tc.tile_pool(name="keep", bufs=1))
+        ring = ctx.enter_context(tc.tile_pool(name="ring", bufs=8))
+        work = ctx.enter_context(tc.tile_pool(name="work", bufs=2))
+        quad = ctx.enter_context(tc.tile_pool(name="quad", bufs=4))
+        psum = ctx.enter_context(tc.psum_pool(name="psum", bufs=4))
+
+        offsets = keep.tile([P, SLOTS // 16], U16, name="offsets")
+        nc.sync.dma_start(offsets[:], offs)
+        x_raw = keep.tile([P, LANES, ROWS], F32, name="x_raw")
+        nc.sync.dma_start(x_raw[:], xT.rearrange("(p j) r -> p j r", j=LANES))
+
+        ts_window = keep.tile([P, TOKENS], F32, name="ts_window")
+        nc.vector.memset(ts_window[:], 0.0)
+        us_t = keep.tile([P, LANES], F32, name="us_t")
+        la_t = keep.tile([P, LANES], F32, name="la_t")
+        wt_t = keep.tile([P, LANES], F32, name="wt_t")
+        for dst, src in ((us_t, us), (la_t, la), (wt_t, wt)):
+            nc.scalar.dma_start(dst[:], src.rearrange("(p t) o -> p (t o)", t=LANES))
+        nc.scalar.dma_start(ts_window[0:1, :], ts[0:1, :])
+
+        ident = keep.tile([P, P], F32, name="ident")
+        make_identity(nc, ident[:])
+        warm = keep.tile([P, 1], F32, name="warm")
+        nc.scalar.activation(warm[:], ident[:, 0:1], ACT.Exp)
+
+        planes = []
+        for table in (ws, wa, wb):
+            rows = table.rearrange("(p j) c -> p j c", j=LANES)
+            for j in range(LANES):
+                plane = ring.tile([P, TOKENS], F32, name="plane", tag="ring", align_bytes=64)
+                nc.sync.dma_start(plane[:], rows[:, j, :])
+                planes.append(plane)
+
+        windows = []
+        for j in range(WINDOWS):
+            window = keep.tile([P, TOKENS], F32, name="window%d" % j)
+            nc.vector.memset(window[:], 0.0)
+            windows.append(window)
+
+        g_codes = keep.tile([P, HALF + SLOTS], U32, name="g_codes", align_bytes=64)
+        g_scales = keep.tile([P, HALF + SLOTS], U8, name="g_scales", align_bytes=64)
+        nc.gpsimd.memset(g_codes[:, 0:HALF], 0)
+        nc.gpsimd.memset(g_scales[:, 0:HALF].bitcast(U32), 0)
+
+        neg_us = keep.tile([P, LANES], F32, name="neg_us")
+        factor = keep.tile([P, 3, LANES], F32, name="factor")
+        nc.vector.tensor_scalar(neg_us[:], us_t[:], -1.0, None, ALU.mult)
+        nc.vector.tensor_tensor(factor[:, 0, :], wt_t[:], us_t[:], ALU.mult)
+        nc.vector.scalar_tensor_tensor(factor[:, 1, :], la_t[:], -1.0, factor[:, 0, :], ALU.mult, ALU.mult)
+        nc.vector.scalar_tensor_tensor(factor[:, 2, :], la_t[:], -1.0, factor[:, 0, :], ALU.add, ALU.mult)
+
+        xd_bf = keep.tile([P, ROWS * LANES], BF16, name="xd_bf", align_bytes=64)
+        nc.scalar.copy(
+            xd_bf[:].rearrange("p (c i j) -> p c j i", i=4, j=LANES),
+            x_raw[:].rearrange("p j (c i) -> p c j i", i=4),
+        )
+        xd_codes = keep.tile([P, ROWS], U32, name="xd_codes", align_bytes=64)
+        xd_scales = keep.tile([P, ROWS], U8, name="xd_scales", align_bytes=64)
+        nc.vector.quantize_mx(xd_codes[:].bitcast(E4M3), xd_scales[:], xd_bf[:])
+
+        xr_bf = keep.tile([P, LANES, P, LANES], BF16, name="xr_bf", align_bytes=64)
+        for j in range(LANES):
+            bank = psum.tile([P, LANES, P], F32, name="turned", tag="turned")
+            for t in range(LANES):
+                nc.tensor.transpose(bank[:, t, :], x_raw[:, j, t::LANES], ident[:])
+            nc.scalar.copy(xr_bf[:, j, :, :], bank[:].rearrange("p t q -> p q t"))
+        xr_codes = keep.tile([P, D], U32, name="xr_codes", align_bytes=64)
+        xr_scales = keep.tile([P, D], U8, name="xr_scales", align_bytes=64)
+
+        ts_row = keep.tile([P, SLOTS], F32, name="ts_row")
+        nc.vector.tensor_copy(ts_row[:], ts_window[:].indirect(offsets[:]))
+        bank = psum.tile([P, LANES, P], F32, name="product", tag="product")
+        for k in range(LANES):
+            nc.tensor.transpose(bank[:, k, :], ts_row[:, k * P : (k + 1) * P], ident[:])
+        ts_col = keep.tile([P, LANES], F32, name="ts_col")
+        nc.scalar.copy(ts_col[:], bank[:, :, 0])
+        bank = psum.tile([P, LANES, P], F32, name="product", tag="product")
+        for k in range(LANES):
+            nc.tensor.transpose(bank[:, k, :], ts_col[:, k : k + 1].to_broadcast([P, P]), ident[:])
+        ts_all = keep.tile([P, SLOTS], F32, name="ts_all")
+        nc.scalar.copy(ts_all[:], bank[:].rearrange("p k s -> p (k s)"))
+
+        nc.vector.quantize_mx(xr_codes[:].bitcast(E4M3), xr_scales[:], xr_bf[:].rearrange("p j q t -> p (j q t)"))
+
+        neg_max = keep.tile([P, 3, LANES], F32, name="neg_max")
+        sums = keep.tile([P, 3, LANES], F32, name="sums")
+        inv = keep.tile([P, 3, LANES], F32, name="inv")
+        coef = keep.tile([P, 3, LANES], F32, name="coef")
+        mix = keep.tile([P, LANES, SLOTS], F32, name="mix")
+
+        def half_offsets(h):
+            return offsets[:, h * (HALF // 16) : (h + 1) * (HALF // 16)]
+
+        def scores(n):
+            plain = 2 if n == 2 else LANES
+            dense = work.tile([P, LANES, SLOTS], BF16, name="dense")
+            halves = [work.tile([P, HALF * LANES], BF16, name="w_bf%d" % h, align_bytes=64) for h in range(2)]
+            for j in range(plain):
+                nc.vector.tensor_copy(dense[:, j, :], planes[LANES * n + j][:].indirect(offsets[:]))
+            for h in range(2):
+                nc.scalar.copy(
+                    halves[h][:].rearrange("p (c i j) -> p c j i", i=4, j=LANES)[:, :, 0:plain, :],
+                    dense[:, 0:plain, h * HALF : (h + 1) * HALF].rearrange("p j (c i) -> p c j i", i=4),
+                )
+            for j in range(plain, LANES):
+                for h in range(2):
+                    nc.vector.tensor_copy(halves[h][:, j::LANES], planes[LANES * n + j][:].indirect(half_offsets(h)))
+            scaled = []
+            for h in range(2):
+                codes = work.tile([P, HALF], U32, name="w_codes%d" % h, align_bytes=64)
+                scales = work.tile([P, HALF], U8, name="w_scales%d" % h, align_bytes=64)
+                nc.vector.quantize_mx(codes[:].bitcast(E4M3), scales[:], halves[h][:])
+                for k in range(2):
+                    cols = slice(k * P, (k + 1) * P)
+                    bank = psum.tile([P, ROWS], F32, name="product", tag="product")
+                    nc.tensor.matmul_mx(
+                        bank[:], lhsT=codes[:, cols].bitcast(E4M3), lhsT_scale=scales[:, cols],
+                        rhs=xd_codes[:].bitcast(E4M3), rhs_scale=xd_scales[:], start=True, stop=True,
+                    )
+                    y = quad.tile([P, LANES, P], F32, name="y")
+                    nc.scalar.activation(
+                        y[:], bank[:].rearrange("p (s t) -> p t s", t=LANES), ACT.Copy,
+                        scale=ts_col[:, 2 * h + k : 2 * h + k + 1],
+                    )
+                    scaled.append(y)
+            banks = [psum.tile([P, SLOTS], F32, name="turned", tag="turned") for t in range(LANES)]
+            for k in range(LANES):
+                for t in range(LANES):
+                    nc.tensor.transpose(banks[t][:, k * P : (k + 1) * P], scaled[k][:, t, :], ident[:])
+            return banks
+
+        def exponentials(n, banks, e, tiles):
+            for t in tiles:
+                neg_z = quad.tile([P, SLOTS], F32, name="neg_z")
+                nc.vector.tensor_scalar(
+                    neg_z[:], banks[t][:], neg_us[:, t : t + 1], None, ALU.mult, ALU.min,
+                    accum_out=neg_max[:, n, t : t + 1],
+                )
+                nc.scalar.activation(
+                    e[:, t, :], neg_z[:], ACT.Exp, bias=neg_max[:, n, t : t + 1], scale=-1.0,
+                    accum_out=sums[:, n, t : t + 1],
+                )
+
+        def coefficients(n, lo, hi):
+            nc.vector.reciprocal(inv[:, n, lo:hi], sums[:, n, lo:hi])
+            nc.vector.tensor_tensor(coef[:, n, lo:hi], inv[:, n, lo:hi], factor[:, n, lo:hi], ALU.mult)
+
+        def add_term(n, e, tiles):
+            for t in tiles:
+                nc.vector.scalar_tensor_tensor(
+                    mix[:, t, :], e[:, t, :], coef[:, n, t : t + 1], mix[:, t, :], ALU.mult, ALU.add
+                )
+
+        banks = scores(0)
+        exponentials(0, banks, mix, range(LANES))
+        coefficients(0, 0, LANES)
+        for t in range(LANES):
+            nc.scalar.activation(mix[:, t, :], mix[:, t, :], ACT.Copy, scale=coef[:, 0, t : t + 1])
+
+        e_a = keep.tile([P, LANES, SLOTS], F32, name="e_a")
+        banks = scores(1)
+        exponentials(1, banks, e_a, range(LANES))
+
+        e_b = keep.tile([P, LANES, SLOTS], F32, name="e_b")
+        banks = scores(2)
+        coefficients(1, 0, LANES)
+        add_term(1, e_a, range(LANES))
+        exponentials(2, banks, e_b, range(LANES))
+        for lo in (0, 2):
+            coefficients(2, lo, lo + 2)
+        for lo in (0, 2):
+            add_term(2, e_b, (lo, lo + 1))
+
+        g_bf = keep.tile([P, SLOTS * LANES], BF16, name="g_bf", align_bytes=64)
+        for h in range(2):
+            cols = slice(h * HALF, (h + 1) * HALF)
+            nc.vector.tensor_tensor(
+                g_bf[:, h * HALF * LANES : (h + 1) * HALF * LANES].rearrange("p (c i t) -> p c t i", i=4, t=LANES),
+                mix[:, :, cols].rearrange("p t (c i) -> p c t i", i=4),
+                ts_all[:, cols].rearrange("p (c i) -> p c i", i=4).unsqueeze(2).to_broadcast([P, HALF // 4, LANES, 4]),
+                ALU.mult,
+            )
+        for h in range(2):
+            cols = slice((h + 1) * HALF, (h + 2) * HALF)
+            nc.vector.quantize_mx(
+                g_codes[:, cols].bitcast(E5M2), g_scales[:, cols], g_bf[:, h * HALF * LANES : (h + 1) * HALF * LANES]
+            )
+
+        def gradient(j, first, lo):
+            cols = slice(j * P, (j + 1) * P)
+            moving = slice(first, first + SLOTS)
+            bank = psum.tile([P, SLOTS], F32, name="product", tag="product")
+            nc.tensor.matmul_mx(
+                bank[:], lhsT=xr_codes[:, cols].bitcast(E4M3), lhsT_scale=xr_scales[:, cols],
+                rhs=g_codes[:, moving].bitcast(E5M2), rhs_scale=g_scales[:, moving], start=True, stop=True,
+            )
+            dw = keep.tile([P, SLOTS - lo], F32, name="dw%d_%d" % (j, first))
+            nc.scalar.copy(dw[:], bank[:, lo:SLOTS])
+            return dw
+
+        early = gradient(0, 0, HALF)
+        staged = [gradient(j, HALF, HALF if j == 0 else 0) for j in range(LANES)]
+
+        starts = [sum(CHUNKS[:c]) for c in range(len(CHUNKS))]
+        pairs = [ring.tile([P, 2, w, 2], BF16, name="pairs", tag="ring", align_bytes=64) for w in CHUNKS]
+        out_rows = out_0.rearrange("(q j) c -> q j c", j=LANES)
+        for j in range(LANES):
+            window = windows[j % WINDOWS]
+            if j == 0:
+                nc.vector.tensor_copy(window[:].indirect(half_offsets(0)), early[:])
+                nc.vector.tensor_copy(window[:].indirect(half_offsets(1)), staged[0][:])
+            else:
+                nc.vector.tensor_copy(window[:].indirect(offsets[:]), staged[j][:])
+            nc.sync.dma_start(out_rows[:, j, :], window[:])
+            for c, w in enumerate(CHUNKS):
+                nc.scalar.copy(pairs[c][:, j // 2, :, j % 2], window[:, starts[c] : starts[c] + w])
+
+        o_bf = keep.tile([P, TOKENS * LANES], BF16, name="o_bf", align_bytes=64)
+        o_codes = keep.tile([P, TOKENS], U32, name="o_codes", align_bytes=64)
+        o_scales = keep.tile([P, TOKENS], U8, name="o_scales", align_bytes=64)
+        words = out_1[0].rearrange("p c l -> p (c l)").bitcast(I32)
+
+        def weave(c):
+            src = pairs[c][:].rearrange("p u c e -> p u (c e)").bitcast(F32).rearrange("p u c -> p c u")
+            dst = o_bf[:, starts[c] * LANES : (starts[c] + CHUNKS[c]) * LANES].bitcast(F32).rearrange("p (c u) -> p c u", u=2)
+            if c < len(CHUNKS) - 2:
+                nc.vector.tensor_copy(dst, src)
+            else:
+                nc.scalar.copy(dst, src)
+
+        weave(0)
+        for c, w in enumerate(CHUNKS):
+            if c + 1 < len(CHUNKS):
+                weave(c + 1)
+            cols = slice(starts[c], starts[c] + w)
+            nc.vector.quantize_mx(
+                o_codes[:, cols].bitcast(E4M3), o_scales[:, cols], o_bf[:, starts[c] * LANES : (starts[c] + w) * LANES]
+            )
+            if (starts[c] + w) % 512 == 0:
+                done = slice(starts[c] + w - 512, starts[c] + w)
+                nc.sync.dma_start(words[:, done], o_codes[:, done].bitcast(I32))
+        for q in range(4):
+            nc.scalar.dma_start(out_2[0, 4 * q : 4 * q + 4, :].bitcast(I32), o_scales[32 * q : 32 * q + 4, :].bitcast(I32))

@@ -30,42 +30,39 @@ def tile_attend_gkd2_pl_kernel(tc, xT, ws, wa, wb, us, ts, la, wt, offs, out_0, 
     nc = tc.nc
     with ExitStack() as ctx:
         keep = ctx.enter_context(tc.tile_pool(name="keep", bufs=1))
-        ring = ctx.enter_context(tc.tile_pool(name="ring", bufs=8))
         work = ctx.enter_context(tc.tile_pool(name="work", bufs=2))
         quad = ctx.enter_context(tc.tile_pool(name="quad", bufs=4))
-        psum = ctx.enter_context(tc.psum_pool(name="psum", bufs=4))
+        psum = ctx.enter_context(tc.psum_pool(name="psum", bufs=1))
 
         offsets = keep.tile([P, SLOTS // 16], U16, name="offsets")
         nc.sync.dma_start(offsets[:], offs)
+        ts_window = keep.tile([P, TOKENS], F32, name="ts_window")
+        nc.sync.dma_start(ts_window[P - 1 : P, :], ts[0:1, :])
         x_raw = keep.tile([P, LANES, ROWS], F32, name="x_raw")
         nc.sync.dma_start(x_raw[:], xT.rearrange("(p j) r -> p j r", j=LANES))
 
-        ts_window = keep.tile([P, TOKENS], F32, name="ts_window")
-        nc.vector.memset(ts_window[:], 0.0)
+        nc.vector.memset(ts_window[0 : P - 1, :], 0.0)
         us_t = keep.tile([P, LANES], F32, name="us_t")
         la_t = keep.tile([P, LANES], F32, name="la_t")
         wt_t = keep.tile([P, LANES], F32, name="wt_t")
         for dst, src in ((us_t, us), (la_t, la), (wt_t, wt)):
             nc.scalar.dma_start(dst[:], src.rearrange("(p t) o -> p (t o)", t=LANES))
-        nc.scalar.dma_start(ts_window[0:1, :], ts[0:1, :])
 
         ident = keep.tile([P, P], F32, name="ident")
         make_identity(nc, ident[:])
-        warm = keep.tile([P, 1], F32, name="warm")
-        nc.scalar.activation(warm[:], ident[:, 0:1], ACT.Exp)
 
         planes = []
         for table in (ws, wa, wb):
             rows = table.rearrange("(p j) c -> p j c", j=LANES)
             for j in range(LANES):
-                plane = ring.tile([P, TOKENS], F32, name="plane", tag="ring", align_bytes=64)
+                plane = keep.tile([P, TOKENS], F32, name="plane", tag="plane%d" % (len(planes) % 8), align_bytes=64)
                 nc.sync.dma_start(plane[:], rows[:, j, :])
                 planes.append(plane)
 
         windows = []
         for j in range(WINDOWS):
             window = keep.tile([P, TOKENS], F32, name="window%d" % j)
-            nc.vector.memset(window[:], 0.0)
+            nc.gpsimd.memset(window[:], 0.0)
             windows.append(window)
 
         g_codes = keep.tile([P, HALF + SLOTS], U32, name="g_codes", align_bytes=64)
@@ -74,11 +71,12 @@ def tile_attend_gkd2_pl_kernel(tc, xT, ws, wa, wb, us, ts, la, wt, offs, out_0, 
         nc.gpsimd.memset(g_scales[:, 0:HALF].bitcast(U32), 0)
 
         neg_us = keep.tile([P, LANES], F32, name="neg_us")
-        factor = keep.tile([P, 3, LANES], F32, name="factor")
+        weight = keep.tile([P, LANES], F32, name="weight")
+        share = keep.tile([P, 2, LANES], F32, name="share")
         nc.vector.tensor_scalar(neg_us[:], us_t[:], -1.0, None, ALU.mult)
-        nc.vector.tensor_tensor(factor[:, 0, :], wt_t[:], us_t[:], ALU.mult)
-        nc.vector.scalar_tensor_tensor(factor[:, 1, :], la_t[:], -1.0, factor[:, 0, :], ALU.mult, ALU.mult)
-        nc.vector.scalar_tensor_tensor(factor[:, 2, :], la_t[:], -1.0, factor[:, 0, :], ALU.add, ALU.mult)
+        nc.vector.tensor_tensor(weight[:], wt_t[:], us_t[:], ALU.mult)
+        nc.vector.tensor_scalar(share[:, 0, :], la_t[:], -1.0, None, ALU.mult)
+        nc.vector.tensor_scalar(share[:, 1, :], la_t[:], -1.0, None, ALU.add)
 
         xd_bf = keep.tile([P, ROWS * LANES], BF16, name="xd_bf", align_bytes=64)
         nc.scalar.copy(
@@ -91,7 +89,7 @@ def tile_attend_gkd2_pl_kernel(tc, xT, ws, wa, wb, us, ts, la, wt, offs, out_0, 
 
         xr_bf = keep.tile([P, LANES, P, LANES], BF16, name="xr_bf", align_bytes=64)
         for j in range(LANES):
-            bank = psum.tile([P, LANES, P], F32, name="turned", tag="turned")
+            bank = psum.tile([P, LANES, P], F32, name="turned", tag="bank%d" % (LANES + j))
             for t in range(LANES):
                 nc.tensor.transpose(bank[:, t, :], x_raw[:, j, t::LANES], ident[:])
             nc.scalar.copy(xr_bf[:, j, :, :], bank[:].rearrange("p t q -> p q t"))
@@ -100,12 +98,12 @@ def tile_attend_gkd2_pl_kernel(tc, xT, ws, wa, wb, us, ts, la, wt, offs, out_0, 
 
         ts_row = keep.tile([P, SLOTS], F32, name="ts_row")
         nc.vector.tensor_copy(ts_row[:], ts_window[:].indirect(offsets[:]))
-        bank = psum.tile([P, LANES, P], F32, name="product", tag="product")
+        bank = psum.tile([P, LANES, P], F32, name="product", tag="bank0")
         for k in range(LANES):
             nc.tensor.transpose(bank[:, k, :], ts_row[:, k * P : (k + 1) * P], ident[:])
         ts_col = keep.tile([P, LANES], F32, name="ts_col")
-        nc.scalar.copy(ts_col[:], bank[:, :, 0])
-        bank = psum.tile([P, LANES, P], F32, name="product", tag="product")
+        nc.scalar.copy(ts_col[:], bank[:, :, P - 1])
+        bank = psum.tile([P, LANES, P], F32, name="product", tag="bank1")
         for k in range(LANES):
             nc.tensor.transpose(bank[:, k, :], ts_col[:, k : k + 1].to_broadcast([P, P]), ident[:])
         ts_all = keep.tile([P, SLOTS], F32, name="ts_all")
@@ -116,34 +114,37 @@ def tile_attend_gkd2_pl_kernel(tc, xT, ws, wa, wb, us, ts, la, wt, offs, out_0, 
         neg_max = keep.tile([P, 3, LANES], F32, name="neg_max")
         sums = keep.tile([P, 3, LANES], F32, name="sums")
         inv = keep.tile([P, 3, LANES], F32, name="inv")
-        coef = keep.tile([P, 3, LANES], F32, name="coef")
         mix = keep.tile([P, LANES, SLOTS], F32, name="mix")
 
         def half_offsets(h):
             return offsets[:, h * (HALF // 16) : (h + 1) * (HALF // 16)]
 
-        def scores(n):
-            plain = 2 if n == 2 else LANES
-            dense = work.tile([P, LANES, SLOTS], BF16, name="dense")
-            halves = [work.tile([P, HALF * LANES], BF16, name="w_bf%d" % h, align_bytes=64) for h in range(2)]
-            for j in range(plain):
+        dense = keep.tile([P, LANES, SLOTS], BF16, name="dense")
+        nc.gpsimd.memset(dense[:, LANES - 1, :], 0.0)
+
+        def first_lanes(n):
+            halves = [keep.tile([P, HALF * LANES], BF16, name="w_bf%d" % h, tag="w_bf%d_%d" % (h, n % 2), align_bytes=64) for h in range(2)]
+            for j in range(2):
                 nc.vector.tensor_copy(dense[:, j, :], planes[LANES * n + j][:].indirect(offsets[:]))
             for h in range(2):
+                cols = slice(h * HALF, (h + 1) * HALF)
+                nc.vector.tensor_copy(dense[:, 2, cols], planes[LANES * n + 2][:].indirect(half_offsets(h)))
                 nc.scalar.copy(
-                    halves[h][:].rearrange("p (c i j) -> p c j i", i=4, j=LANES)[:, :, 0:plain, :],
-                    dense[:, 0:plain, h * HALF : (h + 1) * HALF].rearrange("p j (c i) -> p c j i", i=4),
+                    halves[h][:].rearrange("p (c i j) -> p c j i", i=4, j=LANES),
+                    dense[:, :, cols].rearrange("p j (c i) -> p c j i", i=4),
                 )
-            for j in range(plain, LANES):
-                for h in range(2):
-                    nc.vector.tensor_copy(halves[h][:, j::LANES], planes[LANES * n + j][:].indirect(half_offsets(h)))
+            return halves
+
+        def products(n, halves):
             scaled = []
             for h in range(2):
+                nc.vector.tensor_copy(halves[h][:, 3::LANES], planes[LANES * n + 3][:].indirect(half_offsets(h)))
                 codes = work.tile([P, HALF], U32, name="w_codes%d" % h, align_bytes=64)
                 scales = work.tile([P, HALF], U8, name="w_scales%d" % h, align_bytes=64)
                 nc.vector.quantize_mx(codes[:].bitcast(E4M3), scales[:], halves[h][:])
                 for k in range(2):
                     cols = slice(k * P, (k + 1) * P)
-                    bank = psum.tile([P, ROWS], F32, name="product", tag="product")
+                    bank = psum.tile([P, ROWS], F32, name="product", tag="bank%d" % (2 * h + k))
                     nc.tensor.matmul_mx(
                         bank[:], lhsT=codes[:, cols].bitcast(E4M3), lhsT_scale=scales[:, cols],
                         rhs=xd_codes[:].bitcast(E4M3), rhs_scale=xd_scales[:], start=True, stop=True,
@@ -154,73 +155,93 @@ def tile_attend_gkd2_pl_kernel(tc, xT, ws, wa, wb, us, ts, la, wt, offs, out_0, 
                         scale=ts_col[:, 2 * h + k : 2 * h + k + 1],
                     )
                     scaled.append(y)
-            banks = [psum.tile([P, SLOTS], F32, name="turned", tag="turned") for t in range(LANES)]
-            for k in range(LANES):
-                for t in range(LANES):
+            return scaled
+
+        def turn(scaled):
+            banks = [psum.tile([P, SLOTS], F32, name="turned", tag="bank%d" % t) for t in range(LANES)]
+            for t in range(LANES):
+                for k in range(LANES):
                     nc.tensor.transpose(banks[t][:, k * P : (k + 1) * P], scaled[k][:, t, :], ident[:])
             return banks
 
         def exponentials(n, banks, e, tiles):
+            neg_z = keep.tile([P, LANES, SLOTS], F32, name="neg_z", tag=("plane5", "plane1", "plane4")[n], align_bytes=64)
             for t in tiles:
-                neg_z = quad.tile([P, SLOTS], F32, name="neg_z")
                 nc.vector.tensor_scalar(
-                    neg_z[:], banks[t][:], neg_us[:, t : t + 1], None, ALU.mult, ALU.min,
+                    neg_z[:, t, :], banks[t][:], neg_us[:, t : t + 1], None, ALU.mult, ALU.min,
                     accum_out=neg_max[:, n, t : t + 1],
                 )
                 nc.scalar.activation(
-                    e[:, t, :], neg_z[:], ACT.Exp, bias=neg_max[:, n, t : t + 1], scale=-1.0,
+                    e[:, t, :], neg_z[:, t, :], ACT.Exp, bias=neg_max[:, n, t : t + 1], scale=-1.0,
                     accum_out=sums[:, n, t : t + 1],
                 )
 
-        def coefficients(n, lo, hi):
+        def coefficients(n, coef, factor, lo, hi):
             nc.vector.reciprocal(inv[:, n, lo:hi], sums[:, n, lo:hi])
-            nc.vector.tensor_tensor(coef[:, n, lo:hi], inv[:, n, lo:hi], factor[:, n, lo:hi], ALU.mult)
+            nc.vector.tensor_tensor(coef[:, lo:hi], inv[:, n, lo:hi], factor[:, lo:hi], ALU.mult)
 
-        def add_term(n, e, tiles):
-            for t in tiles:
-                nc.vector.scalar_tensor_tensor(
-                    mix[:, t, :], e[:, t, :], coef[:, n, t : t + 1], mix[:, t, :], ALU.mult, ALU.add
-                )
-
-        banks = scores(0)
-        exponentials(0, banks, mix, range(LANES))
-        coefficients(0, 0, LANES)
-        for t in range(LANES):
-            nc.scalar.activation(mix[:, t, :], mix[:, t, :], ACT.Copy, scale=coef[:, 0, t : t + 1])
+        def add_term(coef, e, t):
+            nc.vector.scalar_tensor_tensor(
+                mix[:, t, :], e[:, t, :], coef[:, t : t + 1], mix[:, t, :], ALU.mult, ALU.add
+            )
 
         e_a = keep.tile([P, LANES, SLOTS], F32, name="e_a")
-        banks = scores(1)
-        exponentials(1, banks, e_a, range(LANES))
-
         e_b = keep.tile([P, LANES, SLOTS], F32, name="e_b")
-        banks = scores(2)
-        coefficients(1, 0, LANES)
-        add_term(1, e_a, range(LANES))
-        exponentials(2, banks, e_b, range(LANES))
-        for lo in (0, 2):
-            coefficients(2, lo, lo + 2)
-        for lo in (0, 2):
-            add_term(2, e_b, (lo, lo + 1))
+        banks_s = turn(products(0, first_lanes(0)))
+        halves = first_lanes(1)
+        exponentials(0, banks_s, mix, range(LANES))
+        banks_a = turn(products(1, halves))
+        halves = first_lanes(2)
+        exponentials(1, banks_a, e_a, range(LANES))
+        banks_b = turn(products(2, halves))
+        ratio = keep.tile([P, 2, LANES], F32, name="ratio", tag="w_bf0_0", align_bytes=64)
+        nc.vector.tensor_tensor(ratio[:], share[:], sums[:, 0:1, :].to_broadcast([P, 2, LANES]), ALU.mult)
+        coef_a = keep.tile([P, LANES], F32, name="coef_a", tag="w_bf1_0", align_bytes=64)
+        coefficients(1, coef_a, ratio[:, 0, :], 0, LANES)
+        coef_s = keep.tile([P, LANES], F32, name="coef_s", tag="w_bf1_1", align_bytes=64)
+        coefficients(0, coef_s, weight, 0, LANES)
+        for t in range(LANES):
+            add_term(coef_a, e_a, t)
+        exponentials(2, banks_b, e_b, range(LANES))
+        coef_b = keep.tile([P, LANES], F32, name="coef_b")
+
+        coefficients(2, coef_b, ratio[:, 1, :], 0, 2)
+        add_term(coef_b, e_b, 0)
+        nc.vector.reciprocal(inv[:, 2, 2:4], sums[:, 2, 2:4])
+        add_term(coef_b, e_b, 1)
+        nc.vector.tensor_tensor(coef_b[:, 2:4], inv[:, 2, 2:4], ratio[:, 1, 2:4], ALU.mult)
+        add_term(coef_b, e_b, 2)
+        add_term(coef_b, e_b, 3)
+        outer = keep.tile([P, LANES, SLOTS], F32, name="outer")
+        for t in range(LANES):
+            nc.scalar.activation(outer[:, t, :], ts_all[:], ACT.Copy, scale=coef_s[:, t : t + 1])
 
         g_bf = keep.tile([P, SLOTS * LANES], BF16, name="g_bf", align_bytes=64)
-        for h in range(2):
-            cols = slice(h * HALF, (h + 1) * HALF)
+
+        def round_g(lo, hi):
             nc.vector.tensor_tensor(
-                g_bf[:, h * HALF * LANES : (h + 1) * HALF * LANES].rearrange("p (c i t) -> p c t i", i=4, t=LANES),
-                mix[:, :, cols].rearrange("p t (c i) -> p c t i", i=4),
-                ts_all[:, cols].rearrange("p (c i) -> p c i", i=4).unsqueeze(2).to_broadcast([P, HALF // 4, LANES, 4]),
+                g_bf[:, lo * LANES : hi * LANES].rearrange("p (c i t) -> p c t i", i=4, t=LANES),
+                mix[:, :, lo:hi].rearrange("p t (c i) -> p c t i", i=4),
+                outer[:, :, lo:hi].rearrange("p t (c i) -> p c t i", i=4),
                 ALU.mult,
             )
-        for h in range(2):
+
+        def quantise_g(h):
             cols = slice((h + 1) * HALF, (h + 2) * HALF)
             nc.vector.quantize_mx(
                 g_codes[:, cols].bitcast(E5M2), g_scales[:, cols], g_bf[:, h * HALF * LANES : (h + 1) * HALF * LANES]
             )
 
+        round_g(0, HALF)
+        round_g(HALF, HALF + P)
+        quantise_g(0)
+        round_g(HALF + P, SLOTS)
+        quantise_g(1)
+
         def gradient(j, first, lo):
             cols = slice(j * P, (j + 1) * P)
             moving = slice(first, first + SLOTS)
-            bank = psum.tile([P, SLOTS], F32, name="product", tag="product")
+            bank = psum.tile([P, SLOTS], F32, name="product", tag="bank%d" % (j if first else 6))
             nc.tensor.matmul_mx(
                 bank[:], lhsT=xr_codes[:, cols].bitcast(E4M3), lhsT_scale=xr_scales[:, cols],
                 rhs=g_codes[:, moving].bitcast(E5M2), rhs_scale=g_scales[:, moving], start=True, stop=True,
@@ -233,7 +254,9 @@ def tile_attend_gkd2_pl_kernel(tc, xT, ws, wa, wb, us, ts, la, wt, offs, out_0, 
         staged = [gradient(j, HALF, HALF if j == 0 else 0) for j in range(LANES)]
 
         starts = [sum(CHUNKS[:c]) for c in range(len(CHUNKS))]
-        pairs = [ring.tile([P, 2, w, 2], BF16, name="pairs", tag="ring", align_bytes=64) for w in CHUNKS]
+        pairs = keep.tile([P, 2 * TOKENS * 2], BF16, name="pairs", tag="x_raw")
+        pair_halves = pairs[:].rearrange("p (u c e) -> p u c e", u=2, e=2)
+        pair_words = pairs[:].bitcast(F32).rearrange("p (u c) -> p c u", u=2)
         out_rows = out_0.rearrange("(q j) c -> q j c", j=LANES)
         for j in range(LANES):
             window = windows[j % WINDOWS]
@@ -243,8 +266,8 @@ def tile_attend_gkd2_pl_kernel(tc, xT, ws, wa, wb, us, ts, la, wt, offs, out_0, 
             else:
                 nc.vector.tensor_copy(window[:].indirect(offsets[:]), staged[j][:])
             nc.sync.dma_start(out_rows[:, j, :], window[:])
-            for c, w in enumerate(CHUNKS):
-                nc.scalar.copy(pairs[c][:, j // 2, :, j % 2], window[:, starts[c] : starts[c] + w])
+            for lo, w in zip(starts, CHUNKS) if j == LANES - 1 else [(0, TOKENS)]:
+                nc.scalar.copy(pair_halves[:, j // 2, lo : lo + w, j % 2], window[:, lo : lo + w])
 
         o_bf = keep.tile([P, TOKENS * LANES], BF16, name="o_bf", align_bytes=64)
         o_codes = keep.tile([P, TOKENS], U32, name="o_codes", align_bytes=64)
@@ -252,7 +275,7 @@ def tile_attend_gkd2_pl_kernel(tc, xT, ws, wa, wb, us, ts, la, wt, offs, out_0, 
         words = out_1[0].rearrange("p c l -> p (c l)").bitcast(I32)
 
         def weave(c):
-            src = pairs[c][:].rearrange("p u c e -> p u (c e)").bitcast(F32).rearrange("p u c -> p c u")
+            src = pair_words[:, starts[c] : starts[c] + CHUNKS[c], :]
             dst = o_bf[:, starts[c] * LANES : (starts[c] + CHUNKS[c]) * LANES].bitcast(F32).rearrange("p (c u) -> p c u", u=2)
             if c < len(CHUNKS) - 2:
                 nc.vector.tensor_copy(dst, src)
@@ -267,8 +290,6 @@ def tile_attend_gkd2_pl_kernel(tc, xT, ws, wa, wb, us, ts, la, wt, offs, out_0, 
             nc.vector.quantize_mx(
                 o_codes[:, cols].bitcast(E4M3), o_scales[:, cols], o_bf[:, starts[c] * LANES : (starts[c] + w) * LANES]
             )
-            if (starts[c] + w) % 512 == 0:
-                done = slice(starts[c] + w - 512, starts[c] + w)
-                nc.sync.dma_start(words[:, done], o_codes[:, done].bitcast(I32))
+            nc.sync.dma_start(words[:, cols], o_codes[:, cols].bitcast(I32))
         for q in range(4):
             nc.scalar.dma_start(out_2[0, 4 * q : 4 * q + 4, :].bitcast(I32), o_scales[32 * q : 32 * q + 4, :].bitcast(I32))

@@ -20,9 +20,16 @@ D = 512
 ROWS = 512
 SLOTS = 512
 TOKENS = 2048
+TABLES = 3
 HALF = SLOTS // 2
-CHUNKS = (256, 256, 512, 512, 256, 256)
+RUN = 4
+PLANE_BUFFERS = 8
 WINDOWS = 3
+CHUNK = 512
+CHUNKS = TOKENS // CHUNK
+SCATTER_ORDER = (2, 0, 1, 3)
+LAST_GROUPS = ((0, 1), (1, 3), (3, 4))
+EARLY_BANK = 6
 FLOPS = 4 * 2 * D * ROWS * SLOTS
 
 
@@ -31,7 +38,7 @@ def tile_attend_gkd2_pl_kernel(tc, xT, ws, wa, wb, us, ts, la, wt, offs, out_0, 
     with ExitStack() as ctx:
         keep = ctx.enter_context(tc.tile_pool(name="keep", bufs=1))
         work = ctx.enter_context(tc.tile_pool(name="work", bufs=2))
-        quad = ctx.enter_context(tc.tile_pool(name="quad", bufs=4))
+        quad = ctx.enter_context(tc.tile_pool(name="quad", bufs=LANES))
         psum = ctx.enter_context(tc.psum_pool(name="psum", bufs=1))
 
         offsets = keep.tile([P, SLOTS // 16], U16, name="offsets")
@@ -51,17 +58,20 @@ def tile_attend_gkd2_pl_kernel(tc, xT, ws, wa, wb, us, ts, la, wt, offs, out_0, 
         ident = keep.tile([P, P], F32, name="ident")
         make_identity(nc, ident[:])
 
+        def plane_buffer(i):
+            return "plane%d" % (i % PLANE_BUFFERS)
+
         planes = []
         for table in (ws, wa, wb):
-            rows = table.rearrange("(p j) c -> p j c", j=LANES)
+            table_rows = table.rearrange("(p j) c -> p j c", j=LANES)
             for j in range(LANES):
-                plane = keep.tile([P, TOKENS], F32, name="plane", tag="plane%d" % (len(planes) % 8), align_bytes=64)
-                nc.sync.dma_start(plane[:], rows[:, j, :])
+                plane = keep.tile([P, TOKENS], F32, name="plane", tag=plane_buffer(len(planes)), align_bytes=64)
+                nc.sync.dma_start(plane[:], table_rows[:, j, :])
                 planes.append(plane)
 
         windows = []
-        for j in range(WINDOWS):
-            window = keep.tile([P, TOKENS], F32, name="window%d" % j)
+        for w in range(WINDOWS):
+            window = keep.tile([P, TOKENS], F32, name="window%d" % w)
             nc.gpsimd.memset(window[:], 0.0)
             windows.append(window)
 
@@ -80,8 +90,8 @@ def tile_attend_gkd2_pl_kernel(tc, xT, ws, wa, wb, us, ts, la, wt, offs, out_0, 
 
         xd_bf = keep.tile([P, ROWS * LANES], BF16, name="xd_bf", align_bytes=64)
         nc.scalar.copy(
-            xd_bf[:].rearrange("p (c i j) -> p c j i", i=4, j=LANES),
-            x_raw[:].rearrange("p j (c i) -> p c j i", i=4),
+            xd_bf[:].rearrange("p (c i j) -> p c j i", i=RUN, j=LANES),
+            x_raw[:].rearrange("p j (c i) -> p c j i", i=RUN),
         )
         xd_codes = keep.tile([P, ROWS], U32, name="xd_codes", align_bytes=64)
         xd_scales = keep.tile([P, ROWS], U8, name="xd_scales", align_bytes=64)
@@ -89,7 +99,7 @@ def tile_attend_gkd2_pl_kernel(tc, xT, ws, wa, wb, us, ts, la, wt, offs, out_0, 
 
         xr_bf = keep.tile([P, LANES, P, LANES], BF16, name="xr_bf", align_bytes=64)
         for j in range(LANES):
-            bank = psum.tile([P, LANES, P], F32, name="turned", tag="bank%d" % (LANES + j))
+            bank = psum.tile([P, LANES, P], F32, name="x_turned", tag="bank%d" % (LANES + j))
             for t in range(LANES):
                 nc.tensor.transpose(bank[:, t, :], x_raw[:, j, t::LANES], ident[:])
             nc.scalar.copy(xr_bf[:, j, :, :], bank[:].rearrange("p t q -> p q t"))
@@ -98,12 +108,12 @@ def tile_attend_gkd2_pl_kernel(tc, xT, ws, wa, wb, us, ts, la, wt, offs, out_0, 
 
         ts_row = keep.tile([P, SLOTS], F32, name="ts_row")
         nc.vector.tensor_copy(ts_row[:], ts_window[:].indirect(offsets[:]))
-        bank = psum.tile([P, LANES, P], F32, name="product", tag="bank0")
+        bank = psum.tile([P, LANES, P], F32, name="ts_turned", tag="bank0")
         for k in range(LANES):
             nc.tensor.transpose(bank[:, k, :], ts_row[:, k * P : (k + 1) * P], ident[:])
         ts_col = keep.tile([P, LANES], F32, name="ts_col")
         nc.scalar.copy(ts_col[:], bank[:, :, P - 1])
-        bank = psum.tile([P, LANES, P], F32, name="product", tag="bank1")
+        bank = psum.tile([P, LANES, P], F32, name="ts_spread", tag="bank1")
         for k in range(LANES):
             nc.tensor.transpose(bank[:, k, :], ts_col[:, k : k + 1].to_broadcast([P, P]), ident[:])
         ts_all = keep.tile([P, SLOTS], F32, name="ts_all")
@@ -111,27 +121,33 @@ def tile_attend_gkd2_pl_kernel(tc, xT, ws, wa, wb, us, ts, la, wt, offs, out_0, 
 
         nc.vector.quantize_mx(xr_codes[:].bitcast(E4M3), xr_scales[:], xr_bf[:].rearrange("p j q t -> p (j q t)"))
 
-        neg_max = keep.tile([P, 3, LANES], F32, name="neg_max")
-        sums = keep.tile([P, 3, LANES], F32, name="sums")
-        inv = keep.tile([P, 3, LANES], F32, name="inv")
+        neg_max = keep.tile([P, TABLES, LANES], F32, name="neg_max")
+        sums = keep.tile([P, TABLES, LANES], F32, name="sums")
+        inv = keep.tile([P, TABLES, LANES], F32, name="inv")
         mix = keep.tile([P, LANES, SLOTS], F32, name="mix")
 
         def half_offsets(h):
             return offsets[:, h * (HALF // 16) : (h + 1) * (HALF // 16)]
 
+        def half_buffer(n, h):
+            return "w_bf%d_%d" % (h, n % 2)
+
         dense = keep.tile([P, LANES, SLOTS], BF16, name="dense")
         nc.gpsimd.memset(dense[:, LANES - 1, :], 0.0)
 
         def first_lanes(n):
-            halves = [keep.tile([P, HALF * LANES], BF16, name="w_bf%d" % h, tag="w_bf%d_%d" % (h, n % 2), align_bytes=64) for h in range(2)]
+            halves = [
+                keep.tile([P, HALF * LANES], BF16, name="w_bf%d" % h, tag=half_buffer(n, h), align_bytes=64)
+                for h in range(2)
+            ]
             for j in range(2):
                 nc.vector.tensor_copy(dense[:, j, :], planes[LANES * n + j][:].indirect(offsets[:]))
             for h in range(2):
                 cols = slice(h * HALF, (h + 1) * HALF)
                 nc.vector.tensor_copy(dense[:, 2, cols], planes[LANES * n + 2][:].indirect(half_offsets(h)))
                 nc.scalar.copy(
-                    halves[h][:].rearrange("p (c i j) -> p c j i", i=4, j=LANES),
-                    dense[:, :, cols].rearrange("p j (c i) -> p c j i", i=4),
+                    halves[h][:].rearrange("p (c i j) -> p c j i", i=RUN, j=LANES),
+                    dense[:, :, cols].rearrange("p j (c i) -> p c j i", i=RUN),
                 )
             return halves
 
@@ -142,31 +158,31 @@ def tile_attend_gkd2_pl_kernel(tc, xT, ws, wa, wb, us, ts, la, wt, offs, out_0, 
                 codes = work.tile([P, HALF], U32, name="w_codes%d" % h, align_bytes=64)
                 scales = work.tile([P, HALF], U8, name="w_scales%d" % h, align_bytes=64)
                 nc.vector.quantize_mx(codes[:].bitcast(E4M3), scales[:], halves[h][:])
-                for k in range(2):
-                    cols = slice(k * P, (k + 1) * P)
-                    bank = psum.tile([P, ROWS], F32, name="product", tag="bank%d" % (2 * h + k))
+                for part in range(2):
+                    k = 2 * h + part
+                    cols = slice(part * P, (part + 1) * P)
+                    bank = psum.tile([P, ROWS], F32, name="scores", tag="bank%d" % k)
                     nc.tensor.matmul_mx(
                         bank[:], lhsT=codes[:, cols].bitcast(E4M3), lhsT_scale=scales[:, cols],
                         rhs=xd_codes[:].bitcast(E4M3), rhs_scale=xd_scales[:], start=True, stop=True,
                     )
                     y = quad.tile([P, LANES, P], F32, name="y")
                     nc.scalar.activation(
-                        y[:], bank[:].rearrange("p (s t) -> p t s", t=LANES), ACT.Copy,
-                        scale=ts_col[:, 2 * h + k : 2 * h + k + 1],
+                        y[:], bank[:].rearrange("p (s t) -> p t s", t=LANES), ACT.Copy, scale=ts_col[:, k : k + 1]
                     )
                     scaled.append(y)
             return scaled
 
         def turn(scaled):
-            banks = [psum.tile([P, SLOTS], F32, name="turned", tag="bank%d" % t) for t in range(LANES)]
+            banks = [psum.tile([P, SLOTS], F32, name="row_tile", tag="bank%d" % t) for t in range(LANES)]
             for t in range(LANES):
                 for k in range(LANES):
                     nc.tensor.transpose(banks[t][:, k * P : (k + 1) * P], scaled[k][:, t, :], ident[:])
             return banks
 
-        def exponentials(n, banks, e, tiles):
-            neg_z = keep.tile([P, LANES, SLOTS], F32, name="neg_z", tag=("plane5", "plane1", "plane4")[n], align_bytes=64)
-            for t in tiles:
+        def exponentials(n, banks, e, buffer):
+            neg_z = keep.tile([P, LANES, SLOTS], F32, name="neg_z", tag=buffer, align_bytes=64)
+            for t in range(LANES):
                 nc.vector.tensor_scalar(
                     neg_z[:, t, :], banks[t][:], neg_us[:, t : t + 1], None, ALU.mult, ALU.min,
                     accum_out=neg_max[:, n, t : t + 1],
@@ -180,38 +196,35 @@ def tile_attend_gkd2_pl_kernel(tc, xT, ws, wa, wb, us, ts, la, wt, offs, out_0, 
             nc.vector.reciprocal(inv[:, n, lo:hi], sums[:, n, lo:hi])
             nc.vector.tensor_tensor(coef[:, lo:hi], inv[:, n, lo:hi], factor[:, lo:hi], ALU.mult)
 
-        def add_term(coef, e, t):
-            nc.vector.scalar_tensor_tensor(
-                mix[:, t, :], e[:, t, :], coef[:, t : t + 1], mix[:, t, :], ALU.mult, ALU.add
-            )
+        def add_term(coef, e):
+            for t in range(LANES):
+                nc.vector.scalar_tensor_tensor(
+                    mix[:, t, :], e[:, t, :], coef[:, t : t + 1], mix[:, t, :], ALU.mult, ALU.add
+                )
 
         e_a = keep.tile([P, LANES, SLOTS], F32, name="e_a")
         e_b = keep.tile([P, LANES, SLOTS], F32, name="e_b")
         banks_s = turn(products(0, first_lanes(0)))
-        halves = first_lanes(1)
-        exponentials(0, banks_s, mix, range(LANES))
-        banks_a = turn(products(1, halves))
-        halves = first_lanes(2)
-        exponentials(1, banks_a, e_a, range(LANES))
-        banks_b = turn(products(2, halves))
-        ratio = keep.tile([P, 2, LANES], F32, name="ratio", tag="w_bf0_0", align_bytes=64)
-        nc.vector.tensor_tensor(ratio[:], share[:], sums[:, 0:1, :].to_broadcast([P, 2, LANES]), ALU.mult)
-        coef_a = keep.tile([P, LANES], F32, name="coef_a", tag="w_bf1_0", align_bytes=64)
-        coefficients(1, coef_a, ratio[:, 0, :], 0, LANES)
-        coef_s = keep.tile([P, LANES], F32, name="coef_s", tag="w_bf1_1", align_bytes=64)
-        coefficients(0, coef_s, weight, 0, LANES)
-        for t in range(LANES):
-            add_term(coef_a, e_a, t)
-        exponentials(2, banks_b, e_b, range(LANES))
-        coef_b = keep.tile([P, LANES], F32, name="coef_b")
+        halves_a = first_lanes(1)
+        exponentials(0, banks_s, mix, plane_buffer(LANES + 2))
+        banks_a = turn(products(1, halves_a))
+        halves_b = first_lanes(2)
+        exponentials(1, banks_a, e_a, plane_buffer(2 * LANES + 2))
+        banks_b = turn(products(2, halves_b))
 
-        coefficients(2, coef_b, ratio[:, 1, :], 0, 2)
-        add_term(coef_b, e_b, 0)
-        nc.vector.reciprocal(inv[:, 2, 2:4], sums[:, 2, 2:4])
-        add_term(coef_b, e_b, 1)
-        nc.vector.tensor_tensor(coef_b[:, 2:4], inv[:, 2, 2:4], ratio[:, 1, 2:4], ALU.mult)
-        add_term(coef_b, e_b, 2)
-        add_term(coef_b, e_b, 3)
+        ratio = keep.tile([P, 2, LANES], F32, name="ratio", tag=half_buffer(2, 0), align_bytes=64)
+        nc.vector.tensor_tensor(ratio[:], share[:], sums[:, 0:1, :].to_broadcast([P, 2, LANES]), ALU.mult)
+        coef_a = keep.tile([P, LANES], F32, name="coef_a", tag=half_buffer(2, 1), align_bytes=64)
+        coefficients(1, coef_a, ratio[:, 0, :], 0, LANES)
+        coef_s = keep.tile([P, LANES], F32, name="coef_s", tag=half_buffer(1, 1), align_bytes=64)
+        coefficients(0, coef_s, weight, 0, LANES)
+        add_term(coef_a, e_a)
+        coef_b = keep.tile([P, LANES], F32, name="coef_b")
+        exponentials(2, banks_b, e_b, plane_buffer(LANES))
+        for lo, hi in LAST_GROUPS:
+            coefficients(2, coef_b, ratio[:, 1, :], lo, hi)
+        add_term(coef_b, e_b)
+
         outer = keep.tile([P, LANES, SLOTS], F32, name="outer")
         for t in range(LANES):
             nc.scalar.activation(outer[:, t, :], ts_all[:], ACT.Copy, scale=coef_s[:, t : t + 1])
@@ -220,9 +233,9 @@ def tile_attend_gkd2_pl_kernel(tc, xT, ws, wa, wb, us, ts, la, wt, offs, out_0, 
 
         def round_g(lo, hi):
             nc.vector.tensor_tensor(
-                g_bf[:, lo * LANES : hi * LANES].rearrange("p (c i t) -> p c t i", i=4, t=LANES),
-                mix[:, :, lo:hi].rearrange("p t (c i) -> p c t i", i=4),
-                outer[:, :, lo:hi].rearrange("p t (c i) -> p c t i", i=4),
+                g_bf[:, lo * LANES : hi * LANES].rearrange("p (c i t) -> p c t i", i=RUN, t=LANES),
+                mix[:, :, lo:hi].rearrange("p t (c i) -> p c t i", i=RUN),
+                outer[:, :, lo:hi].rearrange("p t (c i) -> p c t i", i=RUN),
                 ALU.mult,
             )
 
@@ -238,10 +251,10 @@ def tile_attend_gkd2_pl_kernel(tc, xT, ws, wa, wb, us, ts, la, wt, offs, out_0, 
         round_g(HALF + P, SLOTS)
         quantise_g(1)
 
-        def gradient(j, first, lo):
+        def gradient(j, first, lo, bank_number):
             cols = slice(j * P, (j + 1) * P)
             moving = slice(first, first + SLOTS)
-            bank = psum.tile([P, SLOTS], F32, name="product", tag="bank%d" % (j if first else 6))
+            bank = psum.tile([P, SLOTS], F32, name="dw_sums", tag="bank%d" % bank_number)
             nc.tensor.matmul_mx(
                 bank[:], lhsT=xr_codes[:, cols].bitcast(E4M3), lhsT_scale=xr_scales[:, cols],
                 rhs=g_codes[:, moving].bitcast(E5M2), rhs_scale=g_scales[:, moving], start=True, stop=True,
@@ -250,24 +263,31 @@ def tile_attend_gkd2_pl_kernel(tc, xT, ws, wa, wb, us, ts, la, wt, offs, out_0, 
             nc.scalar.copy(dw[:], bank[:, lo:SLOTS])
             return dw
 
-        early = gradient(0, 0, HALF)
-        staged = [gradient(j, HALF, HALF if j == 0 else 0) for j in range(LANES)]
+        early = gradient(SCATTER_ORDER[0], 0, HALF, EARLY_BANK)
+        staged = {j: gradient(j, HALF, HALF if j == SCATTER_ORDER[0] else 0, j) for j in SCATTER_ORDER}
 
-        starts = [sum(CHUNKS[:c]) for c in range(len(CHUNKS))]
-        pairs = keep.tile([P, 2 * TOKENS * 2], BF16, name="pairs", tag="x_raw")
-        pair_halves = pairs[:].rearrange("p (u c e) -> p u c e", u=2, e=2)
+        pairs = keep.tile([P, LANES * TOKENS], BF16, name="pairs", tag="x_raw")
+        pair_lanes = pairs[:].rearrange("p (u c e) -> p u c e", u=2, e=2)
         pair_words = pairs[:].bitcast(F32).rearrange("p (u c) -> p c u", u=2)
         out_rows = out_0.rearrange("(q j) c -> q j c", j=LANES)
-        for j in range(LANES):
-            window = windows[j % WINDOWS]
-            if j == 0:
+        for step, j in enumerate(SCATTER_ORDER):
+            window = windows[step % WINDOWS]
+            if step == 0:
                 nc.vector.tensor_copy(window[:].indirect(half_offsets(0)), early[:])
-                nc.vector.tensor_copy(window[:].indirect(half_offsets(1)), staged[0][:])
+                nc.vector.tensor_copy(window[:].indirect(half_offsets(1)), staged[j][:])
             else:
                 nc.vector.tensor_copy(window[:].indirect(offsets[:]), staged[j][:])
             nc.sync.dma_start(out_rows[:, j, :], window[:])
-            for lo, w in zip(starts, CHUNKS) if j == LANES - 1 else [(0, TOKENS)]:
-                nc.scalar.copy(pair_halves[:, j // 2, lo : lo + w, j % 2], window[:, lo : lo + w])
+            if step < LANES - 1:
+                nc.scalar.copy(pair_lanes[:, j // 2, :, j % 2], window[:])
+
+        last_window = windows[(LANES - 1) % WINDOWS]
+        for c in range(CHUNKS):
+            cols = slice(c * CHUNK, (c + 1) * CHUNK)
+            if c == 0:
+                nc.vector.tensor_copy(pair_lanes[:, 1, cols, 1], last_window[:, cols])
+            else:
+                nc.scalar.copy(pair_lanes[:, 1, cols, 1], last_window[:, cols])
 
         o_bf = keep.tile([P, TOKENS * LANES], BF16, name="o_bf", align_bytes=64)
         o_codes = keep.tile([P, TOKENS], U32, name="o_codes", align_bytes=64)
@@ -275,21 +295,21 @@ def tile_attend_gkd2_pl_kernel(tc, xT, ws, wa, wb, us, ts, la, wt, offs, out_0, 
         words = out_1[0].rearrange("p c l -> p (c l)").bitcast(I32)
 
         def weave(c):
-            src = pair_words[:, starts[c] : starts[c] + CHUNKS[c], :]
-            dst = o_bf[:, starts[c] * LANES : (starts[c] + CHUNKS[c]) * LANES].bitcast(F32).rearrange("p (c u) -> p c u", u=2)
-            if c < len(CHUNKS) - 2:
+            src = pair_words[:, c * CHUNK : (c + 1) * CHUNK, :]
+            dst = o_bf[:, c * CHUNK * LANES : (c + 1) * CHUNK * LANES].bitcast(F32).rearrange("p (c u) -> p c u", u=2)
+            if c < CHUNKS - 1:
                 nc.vector.tensor_copy(dst, src)
             else:
                 nc.scalar.copy(dst, src)
 
         weave(0)
-        for c, w in enumerate(CHUNKS):
-            if c + 1 < len(CHUNKS):
+        for c in range(CHUNKS):
+            if c + 1 < CHUNKS:
                 weave(c + 1)
-            cols = slice(starts[c], starts[c] + w)
+            cols = slice(c * CHUNK, (c + 1) * CHUNK)
             nc.vector.quantize_mx(
-                o_codes[:, cols].bitcast(E4M3), o_scales[:, cols], o_bf[:, starts[c] * LANES : (starts[c] + w) * LANES]
+                o_codes[:, cols].bitcast(E4M3), o_scales[:, cols], o_bf[:, c * CHUNK * LANES : (c + 1) * CHUNK * LANES]
             )
             nc.sync.dma_start(words[:, cols], o_codes[:, cols].bitcast(I32))
-        for q in range(4):
+        for q in range(P // 32):
             nc.scalar.dma_start(out_2[0, 4 * q : 4 * q + 4, :].bitcast(I32), o_scales[32 * q : 32 * q + 4, :].bitcast(I32))

@@ -29,7 +29,7 @@ CHUNK = 512
 CHUNKS = TOKENS // CHUNK
 SCATTER_ORDER = (2, 0, 1, 3)
 LAST_GROUPS = ((0, 1), (1, 3), (3, 4))
-EARLY_BANK = 6
+EARLY_BANK = 0
 FLOPS = 4 * 2 * D * ROWS * SLOTS
 
 
@@ -62,7 +62,7 @@ def tile_attend_gkd2_pl_kernel(tc, xT, ws, wa, wb, us, ts, la, wt, offs, out_0, 
             return "plane%d" % (i % PLANE_BUFFERS)
 
         planes = []
-        for table in (ws, wa, wb):
+        for table in (wa, wb, ws):
             table_rows = table.rearrange("(p j) c -> p j c", j=LANES)
             for j in range(LANES):
                 plane = keep.tile([P, TOKENS], F32, name="plane", tag=plane_buffer(len(planes)), align_bytes=64)
@@ -119,11 +119,14 @@ def tile_attend_gkd2_pl_kernel(tc, xT, ws, wa, wb, us, ts, la, wt, offs, out_0, 
         ts_all = keep.tile([P, SLOTS], F32, name="ts_all")
         nc.scalar.copy(ts_all[:], bank[:].rearrange("p k s -> p (k s)"))
 
+        outer = keep.tile([P, LANES, SLOTS], F32, name="outer")
+        for t in range(LANES):
+            nc.scalar.activation(outer[:, t, :], ts_all[:], ACT.Copy, scale=weight[:, t : t + 1])
+
         nc.vector.quantize_mx(xr_codes[:].bitcast(E4M3), xr_scales[:], xr_bf[:].rearrange("p j q t -> p (j q t)"))
 
         neg_max = keep.tile([P, TABLES, LANES], F32, name="neg_max")
         sums = keep.tile([P, TABLES, LANES], F32, name="sums")
-        inv = keep.tile([P, TABLES, LANES], F32, name="inv")
         mix = keep.tile([P, LANES, SLOTS], F32, name="mix")
 
         def half_offsets(h):
@@ -151,17 +154,18 @@ def tile_attend_gkd2_pl_kernel(tc, xT, ws, wa, wb, us, ts, la, wt, offs, out_0, 
                 )
             return halves
 
-        def products(n, halves):
+        def products(n, halves, first_bank=0):
             scaled = []
             for h in range(2):
                 nc.vector.tensor_copy(halves[h][:, 3::LANES], planes[LANES * n + 3][:].indirect(half_offsets(h)))
+            for h in range(2):
                 codes = work.tile([P, HALF], U32, name="w_codes%d" % h, align_bytes=64)
                 scales = work.tile([P, HALF], U8, name="w_scales%d" % h, align_bytes=64)
                 nc.vector.quantize_mx(codes[:].bitcast(E4M3), scales[:], halves[h][:])
                 for part in range(2):
                     k = 2 * h + part
                     cols = slice(part * P, (part + 1) * P)
-                    bank = psum.tile([P, ROWS], F32, name="scores", tag="bank%d" % k)
+                    bank = psum.tile([P, ROWS], F32, name="scores", tag="bank%d" % (first_bank + k))
                     nc.tensor.matmul_mx(
                         bank[:], lhsT=codes[:, cols].bitcast(E4M3), lhsT_scale=scales[:, cols],
                         rhs=xd_codes[:].bitcast(E4M3), rhs_scale=xd_scales[:], start=True, stop=True,
@@ -173,61 +177,90 @@ def tile_attend_gkd2_pl_kernel(tc, xT, ws, wa, wb, us, ts, la, wt, offs, out_0, 
                     scaled.append(y)
             return scaled
 
-        def turn(scaled):
-            banks = [psum.tile([P, SLOTS], F32, name="row_tile", tag="bank%d" % t) for t in range(LANES)]
+        def turn(scaled, first_bank=0):
+            banks = [psum.tile([P, SLOTS], F32, name="row_tile", tag="bank%d" % (first_bank + t)) for t in range(LANES)]
             for t in range(LANES):
                 for k in range(LANES):
                     nc.tensor.transpose(banks[t][:, k * P : (k + 1) * P], scaled[k][:, t, :], ident[:])
             return banks
 
-        def exponentials(n, banks, e, buffer):
-            neg_z = keep.tile([P, LANES, SLOTS], F32, name="neg_z", tag=buffer, align_bytes=64)
-            for t in range(LANES):
-                nc.vector.tensor_scalar(
-                    neg_z[:, t, :], banks[t][:], neg_us[:, t : t + 1], None, ALU.mult, ALU.min,
-                    accum_out=neg_max[:, n, t : t + 1],
-                )
-                nc.scalar.activation(
-                    e[:, t, :], neg_z[:, t, :], ACT.Exp, bias=neg_max[:, n, t : t + 1], scale=-1.0,
-                    accum_out=sums[:, n, t : t + 1],
-                )
+        def exponential(n, banks, e, neg_z, t):
+            nc.vector.tensor_scalar(
+                neg_z, banks[t][:], neg_us[:, t : t + 1], None, ALU.mult, ALU.min,
+                accum_out=neg_max[:, n, t : t + 1],
+            )
+            nc.scalar.activation(
+                e[:, t, :], neg_z, ACT.Exp, bias=neg_max[:, n, t : t + 1], scale=-1.0,
+                accum_out=sums[:, n, t : t + 1],
+            )
 
-        def coefficients(n, coef, factor, lo, hi):
-            nc.vector.reciprocal(inv[:, n, lo:hi], sums[:, n, lo:hi])
-            nc.vector.tensor_tensor(coef[:, lo:hi], inv[:, n, lo:hi], factor[:, lo:hi], ALU.mult)
+        def add_term(coef, e, t):
+            nc.vector.scalar_tensor_tensor(
+                mix[:, t, :], e[:, t, :], coef[:, t : t + 1], mix[:, t, :], ALU.mult, ALU.add
+            )
 
-        def add_term(coef, e):
-            for t in range(LANES):
-                nc.vector.scalar_tensor_tensor(
-                    mix[:, t, :], e[:, t, :], coef[:, t : t + 1], mix[:, t, :], ALU.mult, ALU.add
-                )
+        def scratch(buffer, tiles):
+            held = keep.tile([P, tiles * SLOTS + 2 * LANES], F32, name="held", tag=buffer, align_bytes=64)
+            rows = held[:, 0 : tiles * SLOTS].rearrange("p (t s) -> p t s", t=tiles)
+            return rows, held[:, tiles * SLOTS :].rearrange("p (a t) -> p a t", a=2)
 
-        e_a = keep.tile([P, LANES, SLOTS], F32, name="e_a")
+        def scale_first(inv, t):
+            nc.gpsimd.tensor_scalar(
+                mix[:, t, :], mix[:, t, :], inv[:, t : t + 1], share[:, 0, t : t + 1], ALU.mult, ALU.mult
+            )
+
         e_b = keep.tile([P, LANES, SLOTS], F32, name="e_b")
-        banks_s = turn(products(0, first_lanes(0)))
-        halves_a = first_lanes(1)
-        exponentials(0, banks_s, mix, plane_buffer(LANES + 2))
-        banks_a = turn(products(1, halves_a))
-        halves_b = first_lanes(2)
-        exponentials(1, banks_a, e_a, plane_buffer(2 * LANES + 2))
-        banks_b = turn(products(2, halves_b))
+        e_s = keep.tile([P, LANES, SLOTS], F32, name="e_s")
+        banks_a = turn(products(0, first_lanes(0)))
 
-        ratio = keep.tile([P, 2, LANES], F32, name="ratio", tag=half_buffer(2, 0), align_bytes=64)
-        nc.vector.tensor_tensor(ratio[:], share[:], sums[:, 0:1, :].to_broadcast([P, 2, LANES]), ALU.mult)
-        coef_a = keep.tile([P, LANES], F32, name="coef_a", tag=half_buffer(2, 1), align_bytes=64)
-        coefficients(1, coef_a, ratio[:, 0, :], 0, LANES)
-        coef_s = keep.tile([P, LANES], F32, name="coef_s", tag=half_buffer(1, 1), align_bytes=64)
-        coefficients(0, coef_s, weight, 0, LANES)
-        add_term(coef_a, e_a)
-        coef_b = keep.tile([P, LANES], F32, name="coef_b")
-        exponentials(2, banks_b, e_b, plane_buffer(LANES))
-        for lo, hi in LAST_GROUPS:
-            coefficients(2, coef_b, ratio[:, 1, :], lo, hi)
-        add_term(coef_b, e_b)
+        halves_b = first_lanes(1)
+        neg_z, coef = scratch(plane_buffer(6), 2)
+        exponential(0, banks_a, mix, neg_z[:, 0, :], 0)
+        exponential(0, banks_a, mix, neg_z[:, 1, :], 1)
+        scaled_b = products(1, halves_b, LANES)
+        neg_z, coef = scratch(half_buffer(1, 1), 2)
+        exponential(0, banks_a, mix, neg_z[:, 0, :], 2)
+        nc.vector.reciprocal(coef[:, 0, 0:2], sums[:, 0, 0:2])
+        exponential(0, banks_a, mix, neg_z[:, 1, :], 3)
+        scale_first(coef[:, 0, :], 0)
+        scale_first(coef[:, 0, :], 1)
+        banks_b = turn(scaled_b, LANES)
 
-        outer = keep.tile([P, LANES, SLOTS], F32, name="outer")
-        for t in range(LANES):
-            nc.scalar.activation(outer[:, t, :], ts_all[:], ACT.Copy, scale=coef_s[:, t : t + 1])
+        halves_s = first_lanes(2)
+        neg_z, coef = scratch(plane_buffer(10), 2)
+        nc.vector.reciprocal(coef[:, 0, 2:4], sums[:, 0, 2:4])
+        scale_first(coef[:, 0, :], 2)
+        scale_first(coef[:, 0, :], 3)
+        exponential(1, banks_b, e_b, neg_z[:, 0, :], 0)
+        exponential(1, banks_b, e_b, neg_z[:, 1, :], 1)
+        scaled_s = products(2, halves_s, 0)
+        neg_z, coef = scratch(half_buffer(2, 1), 2)
+        nc.vector.reciprocal(coef[:, 0, 0:2], sums[:, 1, 0:2])
+        exponential(1, banks_b, e_b, neg_z[:, 0, :], 2)
+        nc.vector.tensor_tensor(coef[:, 1, 0:2], coef[:, 0, 0:2], share[:, 1, 0:2], ALU.mult)
+        exponential(1, banks_b, e_b, neg_z[:, 1, :], 3)
+        add_term(coef[:, 1, :], e_b, 0)
+        add_term(coef[:, 1, :], e_b, 1)
+        banks_s = turn(scaled_s, 0)
+
+        inv_s = keep.tile([P, LANES], F32, name="inv_s")
+        neg_z, late = scratch(plane_buffer(LANES), LANES)
+        exponential(2, banks_s, e_s, neg_z[:, 0, :], 0)
+        nc.vector.reciprocal(late[:, 0, 2:3], sums[:, 1, 2:3])
+        nc.gpsimd.tensor_scalar(e_b[:, 2, :], e_b[:, 2, :], late[:, 0, 2:3], share[:, 1, 2:3], ALU.mult, ALU.mult)
+        nc.gpsimd.tensor_tensor(mix[:, 2, :], mix[:, 2, :], e_b[:, 2, :], ALU.add)
+        exponential(2, banks_s, e_s, neg_z[:, 1, :], 1)
+        exponential(2, banks_s, e_s, neg_z[:, 2, :], 2)
+        nc.vector.reciprocal(late[:, 0, 3:4], sums[:, 1, 3:4])
+        nc.vector.reciprocal(inv_s[:, 0:1], sums[:, 2, 0:1])
+        exponential(2, banks_s, e_s, neg_z[:, 3, :], 3)
+        nc.vector.tensor_tensor(late[:, 1, 3:4], late[:, 0, 3:4], share[:, 1, 3:4], ALU.mult)
+        nc.vector.reciprocal(inv_s[:, 1:2], sums[:, 2, 1:2])
+        add_term(inv_s, e_s, 0)
+        add_term(late[:, 1, :], e_b, 3)
+        nc.vector.reciprocal(inv_s[:, 2:4], sums[:, 2, 2:4])
+        for t in range(1, LANES):
+            add_term(inv_s, e_s, t)
 
         g_bf = keep.tile([P, SLOTS * LANES], BF16, name="g_bf", align_bytes=64)
 
@@ -264,7 +297,7 @@ def tile_attend_gkd2_pl_kernel(tc, xT, ws, wa, wb, us, ts, la, wt, offs, out_0, 
             return dw
 
         early = gradient(SCATTER_ORDER[0], 0, HALF, EARLY_BANK)
-        staged = {j: gradient(j, HALF, HALF if j == SCATTER_ORDER[0] else 0, j) for j in SCATTER_ORDER}
+        staged = {j: gradient(j, HALF, HALF if j == SCATTER_ORDER[0] else 0, LANES + j) for j in SCATTER_ORDER}
 
         pairs = keep.tile([P, LANES * TOKENS], BF16, name="pairs", tag="x_raw")
         pair_lanes = pairs[:].rearrange("p (u c e) -> p u c e", u=2, e=2)

@@ -81,10 +81,8 @@ def tile_attend_gkd2_pl_kernel(tc, xT, ws, wa, wb, us, ts, la, wt, offs, out_0, 
         nc.gpsimd.memset(g_scales[:, 0:HALF].bitcast(U32), 0)
 
         neg_us = keep.tile([P, LANES], F32, name="neg_us")
-        weight = keep.tile([P, LANES], F32, name="weight")
         share = keep.tile([P, 2, LANES], F32, name="share")
         nc.vector.tensor_scalar(neg_us[:], us_t[:], -1.0, None, ALU.mult)
-        nc.vector.tensor_tensor(weight[:], wt_t[:], us_t[:], ALU.mult)
         nc.vector.tensor_scalar(share[:, 0, :], la_t[:], -1.0, None, ALU.mult)
         nc.vector.tensor_scalar(share[:, 1, :], la_t[:], -1.0, None, ALU.add)
 
@@ -118,10 +116,6 @@ def tile_attend_gkd2_pl_kernel(tc, xT, ws, wa, wb, us, ts, la, wt, offs, out_0, 
             nc.tensor.transpose(bank[:, k, :], ts_col[:, k : k + 1].to_broadcast([P, P]), ident[:])
         ts_all = keep.tile([P, SLOTS], F32, name="ts_all")
         nc.scalar.copy(ts_all[:], bank[:].rearrange("p k s -> p (k s)"))
-
-        outer = keep.tile([P, LANES, SLOTS], F32, name="outer")
-        for t in range(LANES):
-            nc.scalar.activation(outer[:, t, :], ts_all[:], ACT.Copy, scale=weight[:, t : t + 1])
 
         nc.vector.quantize_mx(xr_codes[:].bitcast(E4M3), xr_scales[:], xr_bf[:].rearrange("p j q t -> p (j q t)"))
 
@@ -194,9 +188,9 @@ def tile_attend_gkd2_pl_kernel(tc, xT, ws, wa, wb, us, ts, la, wt, offs, out_0, 
                 accum_out=sums[:, n, t : t + 1],
             )
 
-        def add_term(coef, e, t):
+        def add_term(coef, e, t, lo=0, hi=SLOTS):
             nc.vector.scalar_tensor_tensor(
-                mix[:, t, :], e[:, t, :], coef[:, t : t + 1], mix[:, t, :], ALU.mult, ALU.add
+                mix[:, t, lo:hi], e[:, t, lo:hi], coef[:, t : t + 1], mix[:, t, lo:hi], ALU.mult, ALU.add
             )
 
         def scratch(buffer, tiles):
@@ -215,6 +209,10 @@ def tile_attend_gkd2_pl_kernel(tc, xT, ws, wa, wb, us, ts, la, wt, offs, out_0, 
 
         halves_b = first_lanes(1)
         neg_z, coef = scratch(plane_buffer(6), 2)
+        nc.vector.tensor_tensor(coef[:, 0, :], wt_t[:], us_t[:], ALU.mult)
+        outer = keep.tile([P, LANES, SLOTS], F32, name="outer")
+        for t in range(LANES):
+            nc.gpsimd.tensor_scalar(outer[:, t, :], ts_all[:], coef[:, 0, t : t + 1], 0.0, ALU.mult, ALU.add)
         exponential(0, banks_a, mix, neg_z[:, 0, :], 0)
         exponential(0, banks_a, mix, neg_z[:, 1, :], 1)
         scaled_b = products(1, halves_b, LANES)
@@ -236,15 +234,17 @@ def tile_attend_gkd2_pl_kernel(tc, xT, ws, wa, wb, us, ts, la, wt, offs, out_0, 
         scaled_s = products(2, halves_s, 0)
         neg_z, coef = scratch(half_buffer(2, 1), 2)
         nc.vector.reciprocal(coef[:, 0, 0:2], sums[:, 1, 0:2])
+        nc.gpsimd.tensor_scalar(coef[:, 1, 1:2], coef[:, 0, 1:2], share[:, 1, 1:2], 0.0, ALU.mult, ALU.add)
+        nc.gpsimd.tensor_scalar(e_b[:, 0, :], e_b[:, 0, :], coef[:, 0, 0:1], share[:, 1, 0:1], ALU.mult, ALU.mult)
+        nc.gpsimd.tensor_tensor(mix[:, 0, :], mix[:, 0, :], e_b[:, 0, :], ALU.add)
         exponential(1, banks_b, e_b, neg_z[:, 0, :], 2)
-        nc.vector.tensor_tensor(coef[:, 1, 0:2], coef[:, 0, 0:2], share[:, 1, 0:2], ALU.mult)
         exponential(1, banks_b, e_b, neg_z[:, 1, :], 3)
-        add_term(coef[:, 1, :], e_b, 0)
         add_term(coef[:, 1, :], e_b, 1)
         banks_s = turn(scaled_s, 0)
 
         inv_s = keep.tile([P, LANES], F32, name="inv_s")
-        neg_z, late = scratch(plane_buffer(LANES), LANES)
+        neg_z = scratch(plane_buffer(LANES), LANES)[0]
+        late = keep.tile([P, 2, LANES], F32, name="late", tag=plane_buffer(LANES + 1), align_bytes=64)
         exponential(2, banks_s, e_s, neg_z[:, 0, :], 0)
         nc.vector.reciprocal(late[:, 0, 2:3], sums[:, 1, 2:3])
         nc.gpsimd.tensor_scalar(e_b[:, 2, :], e_b[:, 2, :], late[:, 0, 2:3], share[:, 1, 2:3], ALU.mult, ALU.mult)
@@ -259,8 +259,10 @@ def tile_attend_gkd2_pl_kernel(tc, xT, ws, wa, wb, us, ts, la, wt, offs, out_0, 
         add_term(inv_s, e_s, 0)
         add_term(late[:, 1, :], e_b, 3)
         nc.vector.reciprocal(inv_s[:, 2:4], sums[:, 2, 2:4])
-        for t in range(1, LANES):
-            add_term(inv_s, e_s, t)
+        add_term(inv_s, e_s, 1)
+        add_term(inv_s, e_s, 2)
+        add_term(inv_s, e_s, 3, 0, HALF)
+        add_term(inv_s, e_s, 3, HALF, SLOTS)
 
         g_bf = keep.tile([P, SLOTS * LANES], BF16, name="g_bf", align_bytes=64)
 
@@ -272,17 +274,16 @@ def tile_attend_gkd2_pl_kernel(tc, xT, ws, wa, wb, us, ts, la, wt, offs, out_0, 
                 ALU.mult,
             )
 
-        def quantise_g(h):
-            cols = slice((h + 1) * HALF, (h + 2) * HALF)
-            nc.vector.quantize_mx(
-                g_codes[:, cols].bitcast(E5M2), g_scales[:, cols], g_bf[:, h * HALF * LANES : (h + 1) * HALF * LANES]
-            )
+        def quantise_g(lo, hi):
+            cols = slice(HALF + lo, HALF + hi)
+            nc.vector.quantize_mx(g_codes[:, cols].bitcast(E5M2), g_scales[:, cols], g_bf[:, lo * LANES : hi * LANES])
 
         round_g(0, HALF)
         round_g(HALF, HALF + P)
-        quantise_g(0)
+        quantise_g(0, HALF)
         round_g(HALF + P, SLOTS)
-        quantise_g(1)
+        quantise_g(HALF, HALF + P)
+        quantise_g(HALF + P, SLOTS)
 
         def gradient(j, first, lo, bank_number):
             cols = slice(j * P, (j + 1) * P)

@@ -69,16 +69,26 @@ def tile_attend_gkd2_pl_kernel(tc, xT, ws, wa, wb, us, ts, la, wt, offs, out_0, 
                 nc.sync.dma_start(plane[:], table_rows[:, j, :])
                 planes.append(plane)
 
-        windows = []
-        for w in range(WINDOWS):
-            window = keep.tile([P, TOKENS], F32, name="window%d" % w)
-            nc.gpsimd.memset(window[:], 0.0)
-            windows.append(window)
+        ts_row = keep.tile([P, SLOTS], F32, name="ts_row")
+        nc.vector.tensor_copy(ts_row[:], ts_window[:].indirect(offsets[:]))
+        windows = [keep.tile([P, TOKENS], F32, name="window0")]
+        nc.vector.memset(windows[0][:], 0.0)
 
         g_codes = keep.tile([P, HALF + SLOTS], U32, name="g_codes", align_bytes=64)
         g_scales = keep.tile([P, HALF + SLOTS], U8, name="g_scales", align_bytes=64)
-        nc.gpsimd.memset(g_codes[:, 0:HALF], 0)
-        nc.gpsimd.memset(g_scales[:, 0:HALF].bitcast(U32), 0)
+        nc.vector.memset(g_codes[:, 0:HALF], 0)
+        nc.vector.memset(g_scales[:, 0:HALF].bitcast(U32), 0)
+
+        bank = psum.tile([P, LANES, P], F32, name="ts_turned", tag="bank0")
+        for k in range(LANES):
+            nc.tensor.transpose(bank[:, k, :], ts_row[:, k * P : (k + 1) * P], ident[:])
+        ts_col = keep.tile([P, LANES], F32, name="ts_col")
+        nc.scalar.copy(ts_col[:], bank[:, :, P - 1])
+        bank = psum.tile([P, LANES, P], F32, name="ts_spread", tag="bank1")
+        for k in range(LANES):
+            nc.tensor.transpose(bank[:, k, :], ts_col[:, k : k + 1].to_broadcast([P, P]), ident[:])
+        ts_all = keep.tile([P, SLOTS], F32, name="ts_all")
+        nc.scalar.copy(ts_all[:], bank[:].rearrange("p k s -> p (k s)"))
 
         neg_us = keep.tile([P, LANES], F32, name="neg_us")
         share = keep.tile([P, 2, LANES], F32, name="share")
@@ -95,29 +105,33 @@ def tile_attend_gkd2_pl_kernel(tc, xT, ws, wa, wb, us, ts, la, wt, offs, out_0, 
         xd_scales = keep.tile([P, ROWS], U8, name="xd_scales", align_bytes=64)
         nc.vector.quantize_mx(xd_codes[:].bitcast(E4M3), xd_scales[:], xd_bf[:])
 
-        xr_bf = keep.tile([P, LANES, P, LANES], BF16, name="xr_bf", align_bytes=64)
-        for j in range(LANES):
-            bank = psum.tile([P, LANES, P], F32, name="x_turned", tag="bank%d" % (LANES + j))
-            for t in range(LANES):
-                nc.tensor.transpose(bank[:, t, :], x_raw[:, j, t::LANES], ident[:])
-            nc.scalar.copy(xr_bf[:, j, :, :], bank[:].rearrange("p t q -> p q t"))
+        x_pairs = keep.tile([P, LANES * ROWS], BF16, name="x_pairs")
+        nc.vector.tensor_copy(
+            x_pairs[:].rearrange("q (j u p e) -> q j u p e", j=LANES, u=2, e=2),
+            x_raw[:].rearrange("q j (p u e) -> q j u p e", u=2, e=2),
+        )
+        x_words = x_pairs[:].bitcast(F32)
+        xr_bf = keep.tile([P, D * LANES], BF16, name="xr_bf", align_bytes=64)
+        xr_words = xr_bf[:].bitcast(F32).rearrange("p (j q u) -> p j q u", j=LANES, u=2)
+        for half in range(2):
+            bank = psum.tile([P, LANES, P], F32, name="x_turned", tag="bank%d" % (LANES + half))
+            for i in range(LANES):
+                first = (LANES * half + i) * P
+                nc.tensor.transpose(bank[:, i, :], x_words[:, first : first + P], ident[:])
+            nc.scalar.copy(
+                xr_words[:, 2 * half : 2 * half + 2, :, :], bank[:].rearrange("p (j u) q -> p j q u", u=2)
+            )
         xr_codes = keep.tile([P, D], U32, name="xr_codes", align_bytes=64)
         xr_scales = keep.tile([P, D], U8, name="xr_scales", align_bytes=64)
 
-        ts_row = keep.tile([P, SLOTS], F32, name="ts_row")
-        nc.vector.tensor_copy(ts_row[:], ts_window[:].indirect(offsets[:]))
-        bank = psum.tile([P, LANES, P], F32, name="ts_turned", tag="bank0")
-        for k in range(LANES):
-            nc.tensor.transpose(bank[:, k, :], ts_row[:, k * P : (k + 1) * P], ident[:])
-        ts_col = keep.tile([P, LANES], F32, name="ts_col")
-        nc.scalar.copy(ts_col[:], bank[:, :, P - 1])
-        bank = psum.tile([P, LANES, P], F32, name="ts_spread", tag="bank1")
-        for k in range(LANES):
-            nc.tensor.transpose(bank[:, k, :], ts_col[:, k : k + 1].to_broadcast([P, P]), ident[:])
-        ts_all = keep.tile([P, SLOTS], F32, name="ts_all")
-        nc.scalar.copy(ts_all[:], bank[:].rearrange("p k s -> p (k s)"))
+        nc.vector.quantize_mx(xr_codes[:].bitcast(E4M3), xr_scales[:], xr_bf[:])
 
-        nc.vector.quantize_mx(xr_codes[:].bitcast(E4M3), xr_scales[:], xr_bf[:].rearrange("p j q t -> p (j q t)"))
+        def late_window(buffer):
+            window = keep.tile([P, TOKENS], F32, name="window", tag=buffer, align_bytes=64)
+            nc.gpsimd.memset(window[:], 0.0)
+            windows.append(window)
+
+        late_window("xr_bf")
 
         neg_max = keep.tile([P, TABLES, LANES], F32, name="neg_max")
         sums = keep.tile([P, TABLES, LANES], F32, name="sums")
@@ -127,10 +141,10 @@ def tile_attend_gkd2_pl_kernel(tc, xT, ws, wa, wb, us, ts, la, wt, offs, out_0, 
             return offsets[:, h * (HALF // 16) : (h + 1) * (HALF // 16)]
 
         def half_buffer(n, h):
-            return "w_bf%d_%d" % (h, n % 2)
+            return "w_bf%d_%d" % (h, n)
 
         dense = keep.tile([P, LANES, SLOTS], BF16, name="dense")
-        nc.gpsimd.memset(dense[:, LANES - 1, :], 0.0)
+        nc.vector.memset(dense[:, LANES - 1, :], 0.0)
 
         def first_lanes(n):
             halves = [
@@ -207,6 +221,7 @@ def tile_attend_gkd2_pl_kernel(tc, xT, ws, wa, wb, us, ts, la, wt, offs, out_0, 
         e_s = keep.tile([P, LANES, SLOTS], F32, name="e_s")
         banks_a = turn(products(0, first_lanes(0)))
 
+        late_window(half_buffer(0, 1))
         halves_b = first_lanes(1)
         neg_z, coef = scratch(plane_buffer(6), 2)
         nc.vector.tensor_tensor(coef[:, 0, :], wt_t[:], us_t[:], ALU.mult)

@@ -30,6 +30,7 @@ CHUNKS = TOKENS // CHUNK
 SCATTER_ORDER = (2, 0, 1, 3)
 LAST_GROUPS = ((0, 1), (1, 3), (3, 4))
 EARLY_BANK = 0
+WARM_UPS = 3
 FLOPS = 4 * 2 * D * ROWS * SLOTS
 
 
@@ -246,6 +247,12 @@ def tile_attend_gkd2_pl_kernel(tc, xT, ws, wa, wb, us, ts, la, wt, offs, out_0, 
         scale_first(coef[:, 0, :], 3)
         exponential(1, banks_b, e_b, neg_z[:, 0, :], 0)
         exponential(1, banks_b, e_b, neg_z[:, 1, :], 1)
+        for repeat in range(WARM_UPS):
+            bank = psum.tile([P, ROWS], F32, name="warm_up", tag="bank%d" % LANES)
+            nc.tensor.matmul_mx(
+                bank[:], lhsT=xr_codes[:, 0:P].bitcast(E4M3), lhsT_scale=xr_scales[:, 0:P],
+                rhs=xd_codes[:].bitcast(E4M3), rhs_scale=xd_scales[:], start=True, stop=True,
+            )
         scaled_s = products(2, halves_s, 0)
         neg_z, coef = scratch(half_buffer(2, 1), 2)
         nc.vector.reciprocal(coef[:, 0, 0:2], sums[:, 1, 0:2])

@@ -31,6 +31,7 @@ SCATTER_ORDER = (2, 0, 1, 3)
 LAST_GROUPS = ((0, 1), (1, 3), (3, 4))
 EARLY_BANK = 0
 WARM_UPS = 3
+VECTOR_CHUNKS = 2
 FLOPS = 4 * 2 * D * ROWS * SLOTS
 
 
@@ -340,7 +341,7 @@ def tile_attend_gkd2_pl_kernel(tc, xT, ws, wa, wb, us, ts, la, wt, offs, out_0, 
         last_window = windows[(LANES - 1) % WINDOWS]
         for c in range(CHUNKS):
             cols = slice(c * CHUNK, (c + 1) * CHUNK)
-            if c == 0:
+            if c < VECTOR_CHUNKS:
                 nc.vector.tensor_copy(pair_lanes[:, 1, cols, 1], last_window[:, cols])
             else:
                 nc.scalar.copy(pair_lanes[:, 1, cols, 1], last_window[:, cols])
@@ -353,19 +354,19 @@ def tile_attend_gkd2_pl_kernel(tc, xT, ws, wa, wb, us, ts, la, wt, offs, out_0, 
         def weave(c):
             src = pair_words[:, c * CHUNK : (c + 1) * CHUNK, :]
             dst = o_bf[:, c * CHUNK * LANES : (c + 1) * CHUNK * LANES].bitcast(F32).rearrange("p (c u) -> p c u", u=2)
-            if c < CHUNKS - 1:
+            if c < VECTOR_CHUNKS:
                 nc.vector.tensor_copy(dst, src)
             else:
                 nc.scalar.copy(dst, src)
 
-        weave(0)
         for c in range(CHUNKS):
-            if c + 1 < CHUNKS:
-                weave(c + 1)
+            weave(c)
+        for c in range(CHUNKS):
             cols = slice(c * CHUNK, (c + 1) * CHUNK)
             nc.vector.quantize_mx(
                 o_codes[:, cols].bitcast(E4M3), o_scales[:, cols], o_bf[:, c * CHUNK * LANES : (c + 1) * CHUNK * LANES]
             )
             nc.sync.dma_start(words[:, cols], o_codes[:, cols].bitcast(I32))
         for q in range(P // 32):
-            nc.scalar.dma_start(out_2[0, 4 * q : 4 * q + 4, :].bitcast(I32), o_scales[32 * q : 32 * q + 4, :].bitcast(I32))
+            queue = nc.scalar if q % 2 == 0 else nc.sync
+            queue.dma_start(out_2[0, 4 * q : 4 * q + 4, :].bitcast(I32), o_scales[32 * q : 32 * q + 4, :].bitcast(I32))

@@ -32,6 +32,7 @@ LAST_GROUPS = ((0, 1), (1, 3), (3, 4))
 EARLY_BANK = 0
 WARM_UPS = 3
 VECTOR_CHUNKS = 2
+SCALAR_COLUMNS = 3 * CHUNK
 FLOPS = 4 * 2 * D * ROWS * SLOTS
 
 
@@ -336,7 +337,11 @@ def tile_attend_gkd2_pl_kernel(tc, xT, ws, wa, wb, us, ts, la, wt, offs, out_0, 
                 nc.vector.tensor_copy(window[:].indirect(offsets[:]), staged[j][:])
             nc.sync.dma_start(out_rows[:, j, :], window[:])
             if step < LANES - 1:
-                nc.scalar.copy(pair_lanes[:, j // 2, :, j % 2], window[:])
+                lane = pair_lanes[:, j // 2, :, j % 2]
+                nc.scalar.copy(lane[:, 0:SCALAR_COLUMNS], window[:, 0:SCALAR_COLUMNS])
+                nc.gpsimd.tensor_scalar(
+                    lane[:, SCALAR_COLUMNS:], window[:, SCALAR_COLUMNS:], 1.0, 1.0, ALU.mult, ALU.mult
+                )
 
         last_window = windows[(LANES - 1) % WINDOWS]
         for c in range(CHUNKS):

@@ -24,15 +24,8 @@ TABLES = 3
 HALF = SLOTS // 2
 RUN = 4
 PLANE_BUFFERS = 8
-WINDOWS = 3
 CHUNK = 512
 CHUNKS = TOKENS // CHUNK
-SCATTER_ORDER = (2, 0, 1, 3)
-LAST_GROUPS = ((0, 1), (1, 3), (3, 4))
-EARLY_BANK = 0
-WARM_UPS = 3
-VECTOR_CHUNKS = 2
-SCALAR_COLUMNS = 3 * CHUNK
 FLOPS = 4 * 2 * D * ROWS * SLOTS
 
 
@@ -44,11 +37,14 @@ def tile_attend_gkd2_pl_kernel(tc, xT, ws, wa, wb, us, ts, la, wt, offs, out_0, 
         quad = ctx.enter_context(tc.tile_pool(name="quad", bufs=LANES))
         psum = ctx.enter_context(tc.psum_pool(name="psum", bufs=1))
 
+        def bank_tile(number, shape):
+            return psum.tile(shape, F32, name="bank", tag="bank%d" % number)
+
         offsets = keep.tile([P, SLOTS // 16], U16, name="offsets")
         nc.sync.dma_start(offsets[:], offs)
-        ts_window = keep.tile([P, TOKENS], F32, name="ts_window")
+        ts_window = keep.tile([P, TOKENS], F32, name="ts_window", align_bytes=64)
         nc.sync.dma_start(ts_window[P - 1 : P, :], ts[0:1, :])
-        x_raw = keep.tile([P, LANES, ROWS], F32, name="x_raw")
+        x_raw = keep.tile([P, LANES, ROWS], F32, name="x_raw", align_bytes=64)
         nc.sync.dma_start(x_raw[:], xT.rearrange("(p j) r -> p j r", j=LANES))
 
         nc.vector.memset(ts_window[0 : P - 1, :], 0.0)
@@ -72,61 +68,61 @@ def tile_attend_gkd2_pl_kernel(tc, xT, ws, wa, wb, us, ts, la, wt, offs, out_0, 
                 nc.sync.dma_start(plane[:], table_rows[:, j, :])
                 planes.append(plane)
 
-        ts_row = keep.tile([P, SLOTS], F32, name="ts_row")
-        nc.vector.tensor_copy(ts_row[:], ts_window[:].indirect(offsets[:]))
         windows = [keep.tile([P, TOKENS], F32, name="window0")]
         nc.vector.memset(windows[0][:], 0.0)
 
-        g_codes = keep.tile([P, HALF + SLOTS], U32, name="g_codes", align_bytes=64)
-        g_scales = keep.tile([P, HALF + SLOTS], U8, name="g_scales", align_bytes=64)
-        nc.vector.memset(g_codes[:, 0:HALF], 0)
-        nc.vector.memset(g_scales[:, 0:HALF].bitcast(U32), 0)
-
-        bank = psum.tile([P, LANES, P], F32, name="ts_turned", tag="bank0")
-        for k in range(LANES):
-            nc.tensor.transpose(bank[:, k, :], ts_row[:, k * P : (k + 1) * P], ident[:])
-        ts_col = keep.tile([P, LANES], F32, name="ts_col")
-        nc.scalar.copy(ts_col[:], bank[:, :, P - 1])
-        bank = psum.tile([P, LANES, P], F32, name="ts_spread", tag="bank1")
-        for k in range(LANES):
-            nc.tensor.transpose(bank[:, k, :], ts_col[:, k : k + 1].to_broadcast([P, P]), ident[:])
-        ts_all = keep.tile([P, SLOTS], F32, name="ts_all")
-        nc.scalar.copy(ts_all[:], bank[:].rearrange("p k s -> p (k s)"))
-
-        neg_us = keep.tile([P, LANES], F32, name="neg_us")
-        share = keep.tile([P, 2, LANES], F32, name="share")
-        nc.vector.tensor_scalar(neg_us[:], us_t[:], -1.0, None, ALU.mult)
-        nc.vector.tensor_scalar(share[:, 0, :], la_t[:], -1.0, None, ALU.mult)
-        nc.vector.tensor_scalar(share[:, 1, :], la_t[:], -1.0, None, ALU.add)
-
         xd_bf = keep.tile([P, ROWS * LANES], BF16, name="xd_bf", align_bytes=64)
-        nc.scalar.copy(
-            xd_bf[:].rearrange("p (c i j) -> p c j i", i=RUN, j=LANES),
-            x_raw[:].rearrange("p j (c i) -> p c j i", i=RUN),
+        nc.scalar.activation(
+            xd_bf[:].rearrange("p (t q j) -> p q j t", t=LANES, j=LANES),
+            x_raw[:].rearrange("p j (q t) -> p q j t", t=LANES),
+            ACT.Copy,
         )
-        xd_codes = keep.tile([P, ROWS], U32, name="xd_codes", align_bytes=64)
-        xd_scales = keep.tile([P, ROWS], U8, name="xd_scales", align_bytes=64)
-        nc.vector.quantize_mx(xd_codes[:].bitcast(E4M3), xd_scales[:], xd_bf[:])
-
         x_pairs = keep.tile([P, LANES * ROWS], BF16, name="x_pairs")
         nc.vector.tensor_copy(
             x_pairs[:].rearrange("q (j u p e) -> q j u p e", j=LANES, u=2, e=2),
             x_raw[:].rearrange("q j (p u e) -> q j u p e", u=2, e=2),
         )
+        xd_codes = keep.tile([P, ROWS], U32, name="xd_codes", align_bytes=64)
+        xd_scales = keep.tile([P, ROWS], U8, name="xd_scales", align_bytes=64)
+        nc.vector.quantize_mx(xd_codes[:].bitcast(E4M3), xd_scales[:], xd_bf[:])
+
+        windows.append(keep.tile([P, TOKENS], F32, name="window1", tag="xd_bf", align_bytes=64))
+        nc.vector.memset(windows[1][:], 0.0)
+
+        ts_row = keep.tile([P, SLOTS], F32, name="ts_row")
+        nc.vector.tensor_copy(ts_row[:], ts_window[:].indirect(offsets[:]))
+        bank = bank_tile(0, [P, LANES, P])
+        for k in range(LANES):
+            nc.tensor.transpose(bank[:, k, :], ts_row[:, k * P : (k + 1) * P], ident[:])
+        ts_col = keep.tile([P, LANES], F32, name="ts_col")
+        nc.vector.tensor_copy(ts_col[:], bank[:, :, P - 1])
+        bank = bank_tile(1, [P, LANES, P])
+        for k in range(LANES):
+            nc.tensor.transpose(bank[:, k, :], ts_col[:, k : k + 1].to_broadcast([P, P]), ident[:])
+        ts_all = keep.tile([P, SLOTS], F32, name="ts_all")
+        nc.vector.tensor_copy(ts_all[:], bank[:].rearrange("p k s -> p (k s)"))
+
+        neg_us = keep.tile([P, LANES], F32, name="neg_us")
+        share = keep.tile([P, TABLES, LANES], F32, name="share")
+        weight = share[:, 2, :]
+        nc.vector.tensor_scalar(neg_us[:], us_t[:], -1.0, None, ALU.mult)
+        nc.vector.tensor_tensor(weight, wt_t[:], us_t[:], ALU.mult)
+        nc.vector.scalar_tensor_tensor(share[:, 0, :], la_t[:], -1.0, weight, ALU.mult, ALU.mult)
+        nc.vector.scalar_tensor_tensor(share[:, 1, :], la_t[:], -1.0, weight, ALU.add, ALU.mult)
+
         x_words = x_pairs[:].bitcast(F32)
         xr_bf = keep.tile([P, D * LANES], BF16, name="xr_bf", align_bytes=64)
         xr_words = xr_bf[:].bitcast(F32).rearrange("p (j q u) -> p j q u", j=LANES, u=2)
         for half in range(2):
-            bank = psum.tile([P, LANES, P], F32, name="x_turned", tag="bank%d" % (LANES + half))
+            bank = bank_tile(LANES + half, [P, LANES, P])
             for i in range(LANES):
                 first = (LANES * half + i) * P
                 nc.tensor.transpose(bank[:, i, :], x_words[:, first : first + P], ident[:])
-            nc.scalar.copy(
+            nc.vector.tensor_copy(
                 xr_words[:, 2 * half : 2 * half + 2, :, :], bank[:].rearrange("p (j u) q -> p j q u", u=2)
             )
         xr_codes = keep.tile([P, D], U32, name="xr_codes", align_bytes=64)
         xr_scales = keep.tile([P, D], U8, name="xr_scales", align_bytes=64)
-
         nc.vector.quantize_mx(xr_codes[:].bitcast(E4M3), xr_scales[:], xr_bf[:])
 
         def late_window(buffer):
@@ -134,244 +130,344 @@ def tile_attend_gkd2_pl_kernel(tc, xT, ws, wa, wb, us, ts, la, wt, offs, out_0, 
             nc.gpsimd.memset(window[:], 0.0)
             windows.append(window)
 
-        late_window("xr_bf")
-
         neg_max = keep.tile([P, TABLES, LANES], F32, name="neg_max")
-        sums = keep.tile([P, TABLES, LANES], F32, name="sums")
+        sums = {}
+
+        def new_sum(n, t):
+            if n == 2:
+                sums[n, t] = keep.tile([P, 1], F32, name="sum", tag="sum%d" % t)[:]
+            elif t == 3:
+                sums[n, t] = sums[n, "last"][:, 1:2]
+            else:
+                held = keep.tile([P, 2], F32, name="sum", tag=plane_buffer(LANES * (n + 1) + t + 1), align_bytes=64)
+                sums[n, "last"] = held
+                sums[n, t] = held[:, 0:1]
+            return sums[n, t]
+
+        inv = keep.tile([P, TABLES, LANES], F32, name="inv")
         mix = keep.tile([P, LANES, SLOTS], F32, name="mix")
+        e_b = keep.tile([P, LANES, SLOTS], F32, name="e_b")
+        e_s = keep.tile([P, LANES, SLOTS], F32, name="e_s")
+        exps = (mix, e_b, e_s)
 
         def half_offsets(h):
             return offsets[:, h * (HALF // 16) : (h + 1) * (HALF // 16)]
 
+        def half_cols(h):
+            return slice(h * HALF, (h + 1) * HALF)
+
         def half_buffer(n, h):
             return "w_bf%d_%d" % (h, n)
 
-        dense = keep.tile([P, LANES, SLOTS], BF16, name="dense")
-        nc.vector.memset(dense[:, LANES - 1, :], 0.0)
+        def new_dense():
+            return work.tile([P, LANES * HALF], F32, name="dense")
 
-        def first_lanes(n):
+        def lanes_of(dense):
+            return dense[:].bitcast(BF16).rearrange("p (j s) -> p j s", j=LANES)
+
+        def gather(n, j, dense):
+            nc.scalar.activation(lanes_of(dense)[:, j, :], planes[LANES * n + j][:].indirect(offsets[:]), ACT.Copy)
+
+        def last_lane(n, dense):
             halves = [
-                keep.tile([P, HALF * LANES], BF16, name="w_bf%d" % h, tag=half_buffer(n, h), align_bytes=64)
+                keep.tile([P, HALF * LANES], BF16, name="w_bf", tag=half_buffer(n, h), align_bytes=64)
                 for h in range(2)
             ]
-            for j in range(2):
-                nc.vector.tensor_copy(dense[:, j, :], planes[LANES * n + j][:].indirect(offsets[:]))
+            codes = keep.tile([P, SLOTS], U32, name="w_codes%d" % n, align_bytes=64)
+            scales = keep.tile([P, SLOTS], U8, name="w_scales%d" % n, align_bytes=64)
             for h in range(2):
-                cols = slice(h * HALF, (h + 1) * HALF)
-                nc.vector.tensor_copy(dense[:, 2, cols], planes[LANES * n + 2][:].indirect(half_offsets(h)))
-                nc.scalar.copy(
-                    halves[h][:].rearrange("p (c i j) -> p c j i", i=RUN, j=LANES),
-                    dense[:, :, cols].rearrange("p j (c i) -> p c j i", i=RUN),
+                nc.scalar.activation(
+                    lanes_of(dense)[:, 3, half_cols(h)], planes[LANES * n + 3][:].indirect(half_offsets(h)), ACT.Copy
                 )
-            return halves
-
-        def products(n, halves, first_bank=0):
-            scaled = []
+                nc.vector.tensor_copy(
+                    halves[h][:].rearrange("p (c i j) -> p c j i", i=RUN, j=LANES),
+                    lanes_of(dense)[:, :, half_cols(h)].rearrange("p j (c i) -> p c j i", i=RUN),
+                )
             for h in range(2):
-                nc.vector.tensor_copy(halves[h][:, 3::LANES], planes[LANES * n + 3][:].indirect(half_offsets(h)))
-            for h in range(2):
-                codes = work.tile([P, HALF], U32, name="w_codes%d" % h, align_bytes=64)
-                scales = work.tile([P, HALF], U8, name="w_scales%d" % h, align_bytes=64)
-                nc.vector.quantize_mx(codes[:].bitcast(E4M3), scales[:], halves[h][:])
-                for part in range(2):
-                    k = 2 * h + part
-                    cols = slice(part * P, (part + 1) * P)
-                    bank = psum.tile([P, ROWS], F32, name="scores", tag="bank%d" % (first_bank + k))
-                    nc.tensor.matmul_mx(
-                        bank[:], lhsT=codes[:, cols].bitcast(E4M3), lhsT_scale=scales[:, cols],
-                        rhs=xd_codes[:].bitcast(E4M3), rhs_scale=xd_scales[:], start=True, stop=True,
-                    )
-                    y = quad.tile([P, LANES, P], F32, name="y")
-                    nc.scalar.activation(
-                        y[:], bank[:].rearrange("p (s t) -> p t s", t=LANES), ACT.Copy, scale=ts_col[:, k : k + 1]
-                    )
-                    scaled.append(y)
-            return scaled
+                nc.vector.quantize_mx(codes[:, half_cols(h)].bitcast(E4M3), scales[:, half_cols(h)], halves[h][:])
+            return codes, scales
 
-        def turn(scaled, first_bank=0):
-            banks = [psum.tile([P, SLOTS], F32, name="row_tile", tag="bank%d" % (first_bank + t)) for t in range(LANES)]
-            for t in range(LANES):
-                for k in range(LANES):
-                    nc.tensor.transpose(banks[t][:, k * P : (k + 1) * P], scaled[k][:, t, :], ident[:])
-            return banks
+        def product(out, lhs, lhs_cols, rhs, rhs_cols, rhs_format=E4M3):
+            nc.tensor.matmul_mx(
+                out, lhsT=lhs[0][:, lhs_cols].bitcast(E4M3), lhsT_scale=lhs[1][:, lhs_cols],
+                rhs=rhs[0][:, rhs_cols].bitcast(rhs_format), rhs_scale=rhs[1][:, rhs_cols], start=True, stop=True,
+            )
 
-        def exponential(n, banks, e, neg_z, t):
+        xd = (xd_codes, xd_scales)
+        xr = (xr_codes, xr_scales)
+
+        def block(i):
+            return slice(i * P, (i + 1) * P)
+
+        def row_scores(w, t, bank_number):
+            bank = bank_tile(bank_number, [P, SLOTS])
+            if t == 0:
+                for h in range(2):
+                    product(bank[:, half_cols(h)], xd, block(t), w, half_cols(h))
+            else:
+                product(bank[:], xd, block(t), w, slice(0, SLOTS))
+            return bank
+
+        def logits(t, bank, z):
+            nc.vector.scalar_tensor_tensor(z, bank[:], us_t[:, t : t + 1], ts_all[:], ALU.mult, ALU.mult)
+
+        def exponential(n, t, z, bias=None):
+            bias = neg_max[:, n, t : t + 1] if bias is None else bias
+            nc.vector.tensor_reduce(bias, z, mybir.AxisListType.X, ALU.max, negate=True)
+            nc.scalar.activation(
+                exps[n][:, t, :], z, ACT.Exp, bias=bias, scale=1.0,
+                accum_out=new_sum(n, t),
+            )
+
+        def turned_exponential(n, t, neg_z, bank):
             nc.vector.tensor_scalar(
-                neg_z, banks[t][:], neg_us[:, t : t + 1], None, ALU.mult, ALU.min,
-                accum_out=neg_max[:, n, t : t + 1],
+                neg_z, bank[:], neg_us[:, t : t + 1], None, ALU.mult, ALU.min, accum_out=neg_max[:, n, t : t + 1]
             )
             nc.scalar.activation(
-                e[:, t, :], neg_z, ACT.Exp, bias=neg_max[:, n, t : t + 1], scale=-1.0,
-                accum_out=sums[:, n, t : t + 1],
+                exps[n][:, t, :], neg_z, ACT.Exp, bias=neg_max[:, n, t : t + 1], scale=-1.0,
+                accum_out=new_sum(n, t),
             )
 
-        def add_term(coef, e, t, lo=0, hi=SLOTS):
+        def invert(n, t):
+            nc.vector.reciprocal(inv[:, n, t : t + 1], sums[n, t])
+
+        coef = keep.tile([P, TABLES, LANES], F32, name="coef")
+
+        def factor(n, t):
+            invert(n, t)
+            nc.scalar.activation(coef[:, n, t : t + 1], inv[:, n, t : t + 1], ACT.Copy, scale=share[:, n, t : t + 1])
+
+        def add_term(n, t, lo=0, hi=SLOTS):
             nc.vector.scalar_tensor_tensor(
-                mix[:, t, lo:hi], e[:, t, lo:hi], coef[:, t : t + 1], mix[:, t, lo:hi], ALU.mult, ALU.add
+                mix[:, t, lo:hi], exps[n][:, t, lo:hi], coef[:, n, t : t + 1], mix[:, t, lo:hi], ALU.mult, ALU.add
             )
 
-        def scratch(buffer, tiles):
-            held = keep.tile([P, tiles * SLOTS + 2 * LANES], F32, name="held", tag=buffer, align_bytes=64)
-            rows = held[:, 0 : tiles * SLOTS].rearrange("p (t s) -> p t s", t=tiles)
-            return rows, held[:, tiles * SLOTS :].rearrange("p (a t) -> p a t", a=2)
+        def scale_term(engine, n, t, inverse):
+            e = exps[n]
+            engine.tensor_scalar(e[:, t, :], e[:, t, :], inverse, share[:, n, t : t + 1], ALU.mult, ALU.mult)
 
-        def scale_first(inv, t):
-            nc.gpsimd.tensor_scalar(
-                mix[:, t, :], mix[:, t, :], inv[:, t : t + 1], share[:, 0, t : t + 1], ALU.mult, ALU.mult
+        def finish_teacher(n):
+            late = keep.tile([P, LANES], F32, name="late", tag=half_buffer(n + 1, 1), align_bytes=64)
+            nc.vector.reciprocal(late[:, 1:2], sums[n, 1])
+            nc.vector.reciprocal(late[:, 2:4], sums[n, "last"][:])
+            if n == 1:
+                nc.vector.tensor_tensor(late[:, 0:1], late[:, 1:2], share[:, n, 1:2], ALU.mult)
+                nc.vector.scalar_tensor_tensor(
+                    mix[:, 1, :], e_b[:, 1, :], late[:, 0:1], mix[:, 1, :], ALU.mult, ALU.add
+                )
+            for t in range(1 + n, LANES):
+                scale_term(nc.gpsimd, n, t, late[:, t : t + 1])
+                if n == 1:
+                    nc.gpsimd.tensor_tensor(mix[:, t, :], mix[:, t, :], e_b[:, t, :], ALU.add)
+
+        def maximum(z, bias):
+            nc.vector.tensor_reduce(bias, z, mybir.AxisListType.X, ALU.max, negate=True)
+
+        def exp_of(n, t, z, bias):
+            nc.scalar.activation(exps[n][:, t, :], z, ACT.Exp, bias=bias, scale=1.0, accum_out=new_sum(n, t))
+
+        dense = new_dense()
+        for j in range(LANES - 1):
+            gather(0, j, dense)
+        w = last_lane(0, dense)
+        for n in range(2):
+            late_window(half_buffer(n, 1))
+            dense = new_dense()
+            gather(n + 1, 0, dense)
+            gather(n + 1, 1, dense)
+            banks = [row_scores(w, t, LANES * n + t) for t in range(LANES)]
+            z = [quad.tile([P, SLOTS], F32, name="z") for t in range(LANES)]
+            logits(0, banks[0], z[0][:])
+            logits(1, banks[1], z[1][:])
+            exponential(n, 0, z[0][:], dense[:, 2 * HALF : 2 * HALF + 1])
+            gather(n + 1, 2, dense)
+            logits(2, banks[2], z[2][:])
+            exponential(n, 1, z[1][:], dense[:, 3 * HALF : 3 * HALF + 1])
+            logits(3, banks[3], z[3][:])
+            maximum(z[2][:], neg_max[:, n, 2:3])
+            invert(n, 0)
+            last_max = keep.tile([P, 1], F32, name="last_max", tag=plane_buffer(LANES * (n + 1) + 1), align_bytes=64)
+            maximum(z[3][:], last_max[:])
+            if n == 0:
+                scale_term(nc.gpsimd, n, 0, inv[:, n, 0:1])
+            else:
+                nc.vector.tensor_tensor(coef[:, n, 0:1], inv[:, n, 0:1], share[:, n, 0:1], ALU.mult)
+                add_term(n, 0)
+            w = last_lane(n + 1, dense)
+            exp_of(n, 2, z[2][:], neg_max[:, n, 2:3])
+            exp_of(n, 3, z[3][:], last_max[:])
+            finish_teacher(n)
+
+        banks = [row_scores(w, t, t) for t in range(2)]
+        turned_in = []
+        for pair in range(2):
+            bank = bank_tile(2 + pair, [P, 2, HALF])
+            for i in range(2):
+                product(bank[:, i, :], w, block(2 * pair + i), xd, slice(HALF, ROWS))
+            for i in range(2):
+                k = 2 * pair + i
+                scaled = quad.tile([P, HALF], F32, name="scaled")
+                nc.scalar.activation(scaled[:], bank[:, i, :], ACT.Copy, scale=ts_col[:, k : k + 1])
+                turned_in.append(scaled)
+        for t in range(2, LANES):
+            bank = bank_tile(2 + t, [P, SLOTS])
+            for k in range(LANES):
+                nc.tensor.transpose(bank[:, block(k)], turned_in[k][:, block(t - 2)], ident[:])
+            banks.append(bank)
+        z = [quad.tile([P, SLOTS], F32, name="z") for t in range(LANES)]
+        logits(0, banks[0], z[0][:])
+        logits(1, banks[1], z[1][:])
+        exponential(2, 0, z[0][:])
+        exponential(2, 1, z[1][:])
+        turned_exponential(2, 2, z[2][:], banks[2])
+        factor(2, 0)
+        turned_exponential(2, 3, z[3][:], banks[3])
+        factor(2, 1)
+        add_term(2, 0, 0, HALF)
+        factor(2, 2)
+        add_term(2, 1, 0, HALF)
+        factor(2, 3)
+        add_term(2, 2, 0, HALF)
+        add_term(2, 3, 0, HALF)
+        coef_late = keep.tile([P, LANES], F32, name="coef_late")
+        nc.scalar.copy(coef_late[:], coef[:, 2, :])
+
+        def late_term(t):
+            nc.vector.scalar_tensor_tensor(
+                mix[:, t, HALF:], e_s[:, t, HALF:], coef_late[:, t : t + 1], mix[:, t, HALF:], ALU.mult, ALU.add
             )
 
-        e_b = keep.tile([P, LANES, SLOTS], F32, name="e_b")
-        e_s = keep.tile([P, LANES, SLOTS], F32, name="e_s")
-        banks_a = turn(products(0, first_lanes(0)))
-
-        late_window(half_buffer(0, 1))
-        halves_b = first_lanes(1)
-        neg_z, coef = scratch(plane_buffer(6), 2)
-        nc.vector.tensor_tensor(coef[:, 0, :], wt_t[:], us_t[:], ALU.mult)
-        outer = keep.tile([P, LANES, SLOTS], F32, name="outer")
-        for t in range(LANES):
-            nc.gpsimd.tensor_scalar(outer[:, t, :], ts_all[:], coef[:, 0, t : t + 1], 0.0, ALU.mult, ALU.add)
-        exponential(0, banks_a, mix, neg_z[:, 0, :], 0)
-        exponential(0, banks_a, mix, neg_z[:, 1, :], 1)
-        scaled_b = products(1, halves_b, LANES)
-        neg_z, coef = scratch(half_buffer(1, 1), 2)
-        exponential(0, banks_a, mix, neg_z[:, 0, :], 2)
-        nc.vector.reciprocal(coef[:, 0, 0:2], sums[:, 0, 0:2])
-        exponential(0, banks_a, mix, neg_z[:, 1, :], 3)
-        scale_first(coef[:, 0, :], 0)
-        scale_first(coef[:, 0, :], 1)
-        banks_b = turn(scaled_b, LANES)
-
-        halves_s = first_lanes(2)
-        neg_z, coef = scratch(plane_buffer(10), 2)
-        nc.vector.reciprocal(coef[:, 0, 2:4], sums[:, 0, 2:4])
-        scale_first(coef[:, 0, :], 2)
-        scale_first(coef[:, 0, :], 3)
-        exponential(1, banks_b, e_b, neg_z[:, 0, :], 0)
-        exponential(1, banks_b, e_b, neg_z[:, 1, :], 1)
-        for repeat in range(WARM_UPS):
-            bank = psum.tile([P, ROWS], F32, name="warm_up", tag="bank%d" % LANES)
-            nc.tensor.matmul_mx(
-                bank[:], lhsT=xr_codes[:, 0:P].bitcast(E4M3), lhsT_scale=xr_scales[:, 0:P],
-                rhs=xd_codes[:].bitcast(E4M3), rhs_scale=xd_scales[:], start=True, stop=True,
-            )
-        scaled_s = products(2, halves_s, 0)
-        neg_z, coef = scratch(half_buffer(2, 1), 2)
-        nc.vector.reciprocal(coef[:, 0, 0:2], sums[:, 1, 0:2])
-        nc.gpsimd.tensor_scalar(coef[:, 1, 1:2], coef[:, 0, 1:2], share[:, 1, 1:2], 0.0, ALU.mult, ALU.add)
-        nc.gpsimd.tensor_scalar(e_b[:, 0, :], e_b[:, 0, :], coef[:, 0, 0:1], share[:, 1, 0:1], ALU.mult, ALU.mult)
-        nc.gpsimd.tensor_tensor(mix[:, 0, :], mix[:, 0, :], e_b[:, 0, :], ALU.add)
-        exponential(1, banks_b, e_b, neg_z[:, 0, :], 2)
-        exponential(1, banks_b, e_b, neg_z[:, 1, :], 3)
-        add_term(coef[:, 1, :], e_b, 1)
-        banks_s = turn(scaled_s, 0)
-
-        inv_s = keep.tile([P, LANES], F32, name="inv_s")
-        neg_z = scratch(plane_buffer(LANES), LANES)[0]
-        late = keep.tile([P, 2, LANES], F32, name="late", tag=plane_buffer(LANES + 1), align_bytes=64)
-        exponential(2, banks_s, e_s, neg_z[:, 0, :], 0)
-        nc.vector.reciprocal(late[:, 0, 2:3], sums[:, 1, 2:3])
-        nc.gpsimd.tensor_scalar(e_b[:, 2, :], e_b[:, 2, :], late[:, 0, 2:3], share[:, 1, 2:3], ALU.mult, ALU.mult)
-        nc.gpsimd.tensor_tensor(mix[:, 2, :], mix[:, 2, :], e_b[:, 2, :], ALU.add)
-        exponential(2, banks_s, e_s, neg_z[:, 1, :], 1)
-        exponential(2, banks_s, e_s, neg_z[:, 2, :], 2)
-        nc.vector.reciprocal(late[:, 0, 3:4], sums[:, 1, 3:4])
-        nc.vector.reciprocal(inv_s[:, 0:1], sums[:, 2, 0:1])
-        exponential(2, banks_s, e_s, neg_z[:, 3, :], 3)
-        nc.vector.tensor_tensor(late[:, 1, 3:4], late[:, 0, 3:4], share[:, 1, 3:4], ALU.mult)
-        nc.vector.reciprocal(inv_s[:, 1:2], sums[:, 2, 1:2])
-        add_term(inv_s, e_s, 0)
-        add_term(late[:, 1, :], e_b, 3)
-        nc.vector.reciprocal(inv_s[:, 2:4], sums[:, 2, 2:4])
-        add_term(inv_s, e_s, 1)
-        add_term(inv_s, e_s, 2)
-        add_term(inv_s, e_s, 3, 0, HALF)
-        add_term(inv_s, e_s, 3, HALF, SLOTS)
+        late_term(0)
 
         g_bf = keep.tile([P, SLOTS * LANES], BF16, name="g_bf", align_bytes=64)
+        g_codes = keep.tile([P, SLOTS], U32, name="g_codes", align_bytes=64)
+        g_scales = keep.tile([P, SLOTS], U8, name="g_scales", align_bytes=64)
+        g = (g_codes, g_scales)
 
         def round_g(lo, hi):
             nc.vector.tensor_tensor(
                 g_bf[:, lo * LANES : hi * LANES].rearrange("p (c i t) -> p c t i", i=RUN, t=LANES),
                 mix[:, :, lo:hi].rearrange("p t (c i) -> p c t i", i=RUN),
-                outer[:, :, lo:hi].rearrange("p t (c i) -> p c t i", i=RUN),
+                ts_all[:, lo:hi].rearrange("p (c i) -> p c i", i=RUN).unsqueeze(2).to_broadcast(
+                    [P, (hi - lo) // RUN, LANES, RUN]
+                ),
                 ALU.mult,
             )
 
         def quantise_g(lo, hi):
-            cols = slice(HALF + lo, HALF + hi)
-            nc.vector.quantize_mx(g_codes[:, cols].bitcast(E5M2), g_scales[:, cols], g_bf[:, lo * LANES : hi * LANES])
+            nc.vector.quantize_mx(
+                g_codes[:, lo:hi].bitcast(E5M2), g_scales[:, lo:hi], g_bf[:, lo * LANES : hi * LANES]
+            )
 
         round_g(0, HALF)
-        round_g(HALF, HALF + P)
+        late_term(1)
         quantise_g(0, HALF)
+        late_term(2)
+        late_term(3)
+        round_g(HALF, HALF + P)
         round_g(HALF + P, SLOTS)
         quantise_g(HALF, HALF + P)
         quantise_g(HALF + P, SLOTS)
 
-        def gradient(j, first, lo, bank_number):
-            cols = slice(j * P, (j + 1) * P)
-            moving = slice(first, first + SLOTS)
-            bank = psum.tile([P, SLOTS], F32, name="dw_sums", tag="bank%d" % bank_number)
+        def gradient(j, cols, bank_number, engine, buffer=None):
+            width = cols.stop - cols.start
+            bank = psum.tile([P, width], F32, name="dw_sums", tag="bank%d" % bank_number)
             nc.tensor.matmul_mx(
-                bank[:], lhsT=xr_codes[:, cols].bitcast(E4M3), lhsT_scale=xr_scales[:, cols],
-                rhs=g_codes[:, moving].bitcast(E5M2), rhs_scale=g_scales[:, moving], start=True, stop=True,
+                bank[:], lhsT=xr_codes[:, j * P : (j + 1) * P].bitcast(E4M3), lhsT_scale=xr_scales[:, j * P : (j + 1) * P],
+                rhs=g_codes[:, cols].bitcast(E5M2), rhs_scale=g_scales[:, cols], start=True, stop=True,
             )
-            dw = keep.tile([P, SLOTS - lo], F32, name="dw%d_%d" % (j, first))
-            nc.scalar.copy(dw[:], bank[:, lo:SLOTS])
+            dw = keep.tile([P, width], F32, name="dw", tag=buffer or "dw%d_%d" % (j, cols.start))
+            if engine == "vector":
+                nc.vector.tensor_copy(dw[:], bank[:])
+            else:
+                nc.scalar.copy(dw[:], bank[:])
             return dw
 
-        early = gradient(SCATTER_ORDER[0], 0, HALF, EARLY_BANK)
-        staged = {j: gradient(j, HALF, HALF if j == SCATTER_ORDER[0] else 0, LANES + j) for j in SCATTER_ORDER}
-
-        pairs = keep.tile([P, LANES * TOKENS], BF16, name="pairs", tag="x_raw")
-        pair_lanes = pairs[:].rearrange("p (u c e) -> p u c e", u=2, e=2)
-        pair_words = pairs[:].bitcast(F32).rearrange("p (u c) -> p c u", u=2)
         out_rows = out_0.rearrange("(q j) c -> q j c", j=LANES)
-        for step, j in enumerate(SCATTER_ORDER):
-            window = windows[step % WINDOWS]
-            if step == 0:
-                nc.vector.tensor_copy(window[:].indirect(half_offsets(0)), early[:])
-                nc.vector.tensor_copy(window[:].indirect(half_offsets(1)), staged[j][:])
-            else:
-                nc.vector.tensor_copy(window[:].indirect(offsets[:]), staged[j][:])
-            nc.sync.dma_start(out_rows[:, j, :], window[:])
-            if step < LANES - 1:
-                lane = pair_lanes[:, j // 2, :, j % 2]
-                nc.scalar.copy(lane[:, 0:SCALAR_COLUMNS], window[:, 0:SCALAR_COLUMNS])
-                nc.gpsimd.tensor_scalar(
-                    lane[:, SCALAR_COLUMNS:], window[:, SCALAR_COLUMNS:], 1.0, 1.0, ALU.mult, ALU.mult
-                )
+        sides = [
+            keep.tile([P, 2, LANES, CHUNK], BF16, name="rounded", tag=plane_buffer(4 * s), align_bytes=64)
+            for s in range(2)
+        ]
 
-        last_window = windows[(LANES - 1) % WINDOWS]
-        for c in range(CHUNKS):
-            cols = slice(c * CHUNK, (c + 1) * CHUNK)
-            if c < VECTOR_CHUNKS:
-                nc.vector.tensor_copy(pair_lanes[:, 1, cols, 1], last_window[:, cols])
-            else:
-                nc.scalar.copy(pair_lanes[:, 1, cols, 1], last_window[:, cols])
+        def scalar_scatter(j, h, dw):
+            nc.scalar.activation(windows[j][:].indirect(half_offsets(h)), dw, ACT.Copy)
 
-        o_bf = keep.tile([P, TOKENS * LANES], BF16, name="o_bf", align_bytes=64)
+        def store(j):
+            nc.sync.dma_start(out_rows[:, j, :], windows[j][:])
+
+        def side_of(j, s):
+            return windows[j][:, 2 * s * CHUNK : 2 * (s + 1) * CHUNK].rearrange("p (c k) -> p c k", c=2)
+
+        def early_round(j, s):
+            nc.gpsimd.tensor_scalar(sides[s][:, :, j, :], side_of(j, s), 1.0, 1.0, ALU.mult, ALU.mult)
+
+        left, right, every = slice(0, HALF), slice(HALF, SLOTS), slice(0, SLOTS)
+        scalar_scatter(0, 0, gradient(0, left, 4, "scalar", "dw_chain")[:])
+        dw_1_left = gradient(1, left, 5, "scalar", "dw_chain")
+        dw_0_right = gradient(0, right, 6, "vector")
+        dw_2 = gradient(2, every, 7, "vector", "dw0_256")
+        dw_1_right = gradient(1, right, 0, "scalar")
+        nc.vector.tensor_copy(windows[0][:].indirect(half_offsets(1)), dw_0_right[:])
+        store(0)
+        scalar_scatter(1, 0, dw_1_left[:])
+        scalar_scatter(1, 1, dw_1_right[:])
+        store(1)
+        early_round(0, 0)
+        early_round(0, 1)
+        early_round(1, 0)
+        nc.vector.tensor_copy(windows[2][:].indirect(offsets[:]), dw_2[:])
+        store(2)
+        dw_3 = gradient(3, every, 1, "scalar", "dw_chain")
+        scalar_scatter(3, 0, dw_3[:, left])
+        scalar_scatter(3, 1, dw_3[:, right])
+        store(3)
+
+        def rounded(c):
+            return sides[c // 2][:, c % 2, :, :]
+
+        for s in range(2):
+            nc.vector.tensor_copy(sides[s][:, :, 2, :], side_of(2, s))
+        nc.vector.tensor_copy(sides[1][:, :, 1, :], side_of(1, 1))
+        nc.vector.tensor_copy(rounded(0)[:, 3, :], windows[3][:, 0:CHUNK])
+        nc.scalar.copy(rounded(1)[:, 3, :], windows[3][:, CHUNK : 2 * CHUNK])
+        nc.scalar.copy(sides[1][:, :, 3, :], side_of(3, 1))
+
+        woven = [
+            keep.tile([P, TOKENS // 2 * LANES], BF16, name="woven", tag=tag, align_bytes=64)
+            for tag in ("x_raw", "ts_window")
+        ]
         o_codes = keep.tile([P, TOKENS], U32, name="o_codes", align_bytes=64)
         o_scales = keep.tile([P, TOKENS], U8, name="o_scales", align_bytes=64)
         words = out_1[0].rearrange("p c l -> p (c l)").bitcast(I32)
 
-        def weave(c):
-            src = pair_words[:, c * CHUNK : (c + 1) * CHUNK, :]
-            dst = o_bf[:, c * CHUNK * LANES : (c + 1) * CHUNK * LANES].bitcast(F32).rearrange("p (c u) -> p c u", u=2)
-            if c < VECTOR_CHUNKS:
+        def weave(engine, lo, hi):
+            c = lo // CHUNK
+            first = lo - c // 2 * 2 * CHUNK
+            dst = woven[c // 2][:, first * LANES : (first + hi - lo) * LANES].rearrange("p (c i j) -> p c j i", i=RUN, j=LANES)
+            src = rounded(c)[:, :, lo - c * CHUNK : hi - c * CHUNK].rearrange("p j (c i) -> p c j i", i=RUN)
+            if engine == "vector":
                 nc.vector.tensor_copy(dst, src)
             else:
                 nc.scalar.copy(dst, src)
 
-        for c in range(CHUNKS):
-            weave(c)
-        for c in range(CHUNKS):
+        def quantise_out(c):
             cols = slice(c * CHUNK, (c + 1) * CHUNK)
             nc.vector.quantize_mx(
-                o_codes[:, cols].bitcast(E4M3), o_scales[:, cols], o_bf[:, c * CHUNK * LANES : (c + 1) * CHUNK * LANES]
+                o_codes[:, cols].bitcast(E4M3), o_scales[:, cols],
+                woven[c // 2][:, c % 2 * CHUNK * LANES : (c % 2 + 1) * CHUNK * LANES],
             )
             nc.sync.dma_start(words[:, cols], o_codes[:, cols].bitcast(I32))
+
+        shared = 2 * CHUNK + CHUNK // 2
+        weave("vector", 0, CHUNK)
+        weave("vector", CHUNK, 2 * CHUNK)
+        weave("scalar", shared, 3 * CHUNK)
+        weave("scalar", 3 * CHUNK, 4 * CHUNK)
+        quantise_out(0)
+        weave("vector", 2 * CHUNK, shared)
+        quantise_out(1)
+        quantise_out(2)
+        quantise_out(3)
         for q in range(P // 32):
             queue = nc.scalar if q % 2 == 0 else nc.sync
             queue.dma_start(out_2[0, 4 * q : 4 * q + 4, :].bitcast(I32), o_scales[32 * q : 32 * q + 4, :].bitcast(I32))

@@ -68,8 +68,11 @@ def tile_attend_gkd2_pl_kernel(tc, xT, ws, wa, wb, us, ts, la, wt, offs, out_0, 
                 nc.sync.dma_start(plane[:], table_rows[:, j, :])
                 planes.append(plane)
 
-        windows = [keep.tile([P, TOKENS], F32, name="window0")]
-        nc.vector.memset(windows[0][:], 0.0)
+        windows = []
+        for w in range(LANES - 1):
+            window = keep.tile([P, TOKENS], F32, name="window%d" % w)
+            nc.vector.memset(window[:], 0.0)
+            windows.append(window)
 
         xd_bf = keep.tile([P, ROWS * LANES], BF16, name="xd_bf", align_bytes=64)
         nc.scalar.activation(
@@ -86,8 +89,8 @@ def tile_attend_gkd2_pl_kernel(tc, xT, ws, wa, wb, us, ts, la, wt, offs, out_0, 
         xd_scales = keep.tile([P, ROWS], U8, name="xd_scales", align_bytes=64)
         nc.vector.quantize_mx(xd_codes[:].bitcast(E4M3), xd_scales[:], xd_bf[:])
 
-        windows.append(keep.tile([P, TOKENS], F32, name="window1", tag="xd_bf", align_bytes=64))
-        nc.vector.memset(windows[1][:], 0.0)
+        windows.append(keep.tile([P, TOKENS], F32, name="window", tag="xd_bf", align_bytes=64))
+        nc.vector.memset(windows[LANES - 1][:], 0.0)
 
         ts_row = keep.tile([P, SLOTS], F32, name="ts_row")
         nc.vector.tensor_copy(ts_row[:], ts_window[:].indirect(offsets[:]))
@@ -124,11 +127,6 @@ def tile_attend_gkd2_pl_kernel(tc, xT, ws, wa, wb, us, ts, la, wt, offs, out_0, 
         xr_codes = keep.tile([P, D], U32, name="xr_codes", align_bytes=64)
         xr_scales = keep.tile([P, D], U8, name="xr_scales", align_bytes=64)
         nc.vector.quantize_mx(xr_codes[:].bitcast(E4M3), xr_scales[:], xr_bf[:])
-
-        def late_window(buffer):
-            window = keep.tile([P, TOKENS], F32, name="window", tag=buffer, align_bytes=64)
-            nc.gpsimd.memset(window[:], 0.0)
-            windows.append(window)
 
         neg_max = keep.tile([P, TABLES, LANES], F32, name="neg_max")
         sums = {}
@@ -271,7 +269,6 @@ def tile_attend_gkd2_pl_kernel(tc, xT, ws, wa, wb, us, ts, la, wt, offs, out_0, 
             gather(0, j, dense)
         w = last_lane(0, dense)
         for n in range(2):
-            late_window(half_buffer(n, 1))
             dense = new_dense()
             gather(n + 1, 0, dense)
             gather(n + 1, 1, dense)

@@ -24,6 +24,7 @@ TABLES = 3
 HALF = SLOTS // 2
 RUN = 4
 PLANE_BUFFERS = 8
+BESIDE = 64
 CHUNK = 512
 CHUNKS = TOKENS // CHUNK
 FLOPS = 4 * 2 * D * ROWS * SLOTS
@@ -40,19 +41,18 @@ def tile_attend_gkd2_pl_kernel(tc, xT, ws, wa, wb, us, ts, la, wt, offs, out_0, 
         def bank_tile(number, shape):
             return psum.tile(shape, F32, name="bank", tag="bank%d" % number)
 
+        x_raw = keep.tile([P, LANES, ROWS], F32, name="x_raw", align_bytes=64)
+        nc.sync.dma_start(x_raw[:], xT.rearrange("(p j) r -> p j r", j=LANES))
         offsets = keep.tile([P, SLOTS // 16], U16, name="offsets")
         nc.sync.dma_start(offsets[:], offs)
         ts_window = keep.tile([P, TOKENS], F32, name="ts_window", align_bytes=64)
         nc.sync.dma_start(ts_window[P - 1 : P, :], ts[0:1, :])
-        x_raw = keep.tile([P, LANES, ROWS], F32, name="x_raw", align_bytes=64)
-        nc.sync.dma_start(x_raw[:], xT.rearrange("(p j) r -> p j r", j=LANES))
 
         nc.vector.memset(ts_window[0 : P - 1, :], 0.0)
-        us_t = keep.tile([P, LANES], F32, name="us_t")
-        la_t = keep.tile([P, LANES], F32, name="la_t")
-        wt_t = keep.tile([P, LANES], F32, name="wt_t")
-        for dst, src in ((us_t, us), (la_t, la), (wt_t, wt)):
-            nc.scalar.dma_start(dst[:], src.rearrange("(p t) o -> p (t o)", t=LANES))
+        vectors = keep.tile([P, ROWS], F32, name="vectors")
+        nc.vector.memset(vectors[0 : P - 3, :], 0.0)
+        for i, src in enumerate((us, la, wt)):
+            nc.sync.dma_start(vectors[P - 3 + i : P - 2 + i, :], src.rearrange("r o -> o r"))
 
         ident = keep.tile([P, P], F32, name="ident")
         make_identity(nc, ident[:])
@@ -99,19 +99,26 @@ def tile_attend_gkd2_pl_kernel(tc, xT, ws, wa, wb, us, ts, la, wt, offs, out_0, 
             nc.tensor.transpose(bank[:, k, :], ts_row[:, k * P : (k + 1) * P], ident[:])
         ts_col = keep.tile([P, LANES], F32, name="ts_col")
         nc.vector.tensor_copy(ts_col[:], bank[:, :, P - 1])
-        bank = bank_tile(1, [P, LANES, P])
+        ts_bank = bank_tile(7, [P, SLOTS])
         for k in range(LANES):
-            nc.tensor.transpose(bank[:, k, :], ts_col[:, k : k + 1].to_broadcast([P, P]), ident[:])
+            nc.tensor.transpose(ts_bank[:, k * P : (k + 1) * P], ts_col[:, k : k + 1].to_broadcast([P, P]), ident[:])
         ts_all = keep.tile([P, SLOTS], F32, name="ts_all")
-        nc.vector.tensor_copy(ts_all[:], bank[:].rearrange("p k s -> p (k s)"))
+        nc.vector.tensor_copy(ts_all[:], ts_bank[:])
+
+        bank = bank_tile(1, [P, LANES, P])
+        for t in range(LANES):
+            nc.tensor.transpose(bank[:, t, :], vectors[:, t::LANES], ident[:])
+        by_row = keep.tile([P, 3, LANES], F32, name="by_row")
+        nc.vector.tensor_copy(by_row[:], bank[:, :, P - 3 :].rearrange("p t i -> p i t"))
+        us_t, la_t, wt_t = (by_row[:, i, :] for i in range(3))
 
         neg_us = keep.tile([P, LANES], F32, name="neg_us")
         share = keep.tile([P, TABLES, LANES], F32, name="share")
         weight = share[:, 2, :]
-        nc.vector.tensor_scalar(neg_us[:], us_t[:], -1.0, None, ALU.mult)
-        nc.vector.tensor_tensor(weight, wt_t[:], us_t[:], ALU.mult)
-        nc.vector.scalar_tensor_tensor(share[:, 0, :], la_t[:], -1.0, weight, ALU.mult, ALU.mult)
-        nc.vector.scalar_tensor_tensor(share[:, 1, :], la_t[:], -1.0, weight, ALU.add, ALU.mult)
+        nc.vector.tensor_scalar(neg_us[:], us_t, -1.0, None, ALU.mult)
+        nc.vector.tensor_tensor(weight, wt_t, us_t, ALU.mult)
+        nc.vector.scalar_tensor_tensor(share[:, 0, :], la_t, -1.0, weight, ALU.mult, ALU.mult)
+        nc.vector.scalar_tensor_tensor(share[:, 1, :], la_t, -1.0, weight, ALU.add, ALU.mult)
 
         x_words = x_pairs[:].bitcast(F32)
         xr_bf = keep.tile([P, D * LANES], BF16, name="xr_bf", align_bytes=64)
@@ -246,16 +253,17 @@ def tile_attend_gkd2_pl_kernel(tc, xT, ws, wa, wb, us, ts, la, wt, offs, out_0, 
 
         def finish_teacher(n):
             late = keep.tile([P, LANES], F32, name="late", tag=half_buffer(n + 1, 1), align_bytes=64)
-            nc.vector.reciprocal(late[:, 1:2], sums[n, 1])
+            if n == 0:
+                nc.vector.reciprocal(late[:, 1:2], sums[n, 1])
             nc.vector.reciprocal(late[:, 2:4], sums[n, "last"][:])
-            if n == 1:
-                nc.vector.tensor_tensor(late[:, 0:1], late[:, 1:2], share[:, n, 1:2], ALU.mult)
-                nc.vector.scalar_tensor_tensor(
-                    mix[:, 1, :], e_b[:, 1, :], late[:, 0:1], mix[:, 1, :], ALU.mult, ALU.add
-                )
-            for t in range(1 + n, LANES):
-                scale_term(nc.gpsimd, n, t, late[:, t : t + 1])
-                if n == 1:
+            if n == 0:
+                for t in range(1, LANES):
+                    scale_term(nc.gpsimd, n, t, late[:, t : t + 1])
+            else:
+                scale_term(nc.gpsimd, n, 2, late[:, 2:3])
+                nc.scalar.activation(coef[:, n, 3:4], late[:, 3:4], ACT.Copy, scale=share[:, n, 3:4])
+                nc.scalar.activation(e_b[:, 3, :], e_b[:, 3, :], ACT.Copy, scale=coef[:, n, 3:4])
+                for t in (2, 3):
                     nc.gpsimd.tensor_tensor(mix[:, t, :], mix[:, t, :], e_b[:, t, :], ALU.add)
 
         def maximum(z, bias):
@@ -272,53 +280,59 @@ def tile_attend_gkd2_pl_kernel(tc, xT, ws, wa, wb, us, ts, la, wt, offs, out_0, 
             dense = new_dense()
             gather(n + 1, 0, dense)
             gather(n + 1, 1, dense)
-            banks = [row_scores(w, t, LANES * n + t) for t in range(LANES)]
-            z = [quad.tile([P, SLOTS], F32, name="z") for t in range(LANES)]
+            banks = [row_scores(w, t, t) for t in range(LANES)]
+            z = [quad.tile([P, SLOTS], F32, name="z") for t in range(LANES - 1)]
             logits(0, banks[0], z[0][:])
             logits(1, banks[1], z[1][:])
             exponential(n, 0, z[0][:], dense[:, 2 * HALF : 2 * HALF + 1])
             gather(n + 1, 2, dense)
             logits(2, banks[2], z[2][:])
             exponential(n, 1, z[1][:], dense[:, 3 * HALF : 3 * HALF + 1])
+            invert(n, 0)
+            scale_term(nc.gpsimd, n, 0, inv[:, n, 0:1])
+            if n == 1:
+                nc.gpsimd.tensor_tensor(mix[:, 0, :], mix[:, 0, :], e_b[:, 0, :], ALU.add)
+            z.append(keep.tile([P, SLOTS], F32, name="z", tag=plane_buffer(LANES * (n + 1) + 1), align_bytes=64))
             logits(3, banks[3], z[3][:])
             maximum(z[2][:], neg_max[:, n, 2:3])
-            invert(n, 0)
-            last_max = keep.tile([P, 1], F32, name="last_max", tag=plane_buffer(LANES * (n + 1) + 1), align_bytes=64)
-            maximum(z[3][:], last_max[:])
-            if n == 0:
-                scale_term(nc.gpsimd, n, 0, inv[:, n, 0:1])
-            else:
-                nc.vector.tensor_tensor(coef[:, n, 0:1], inv[:, n, 0:1], share[:, n, 0:1], ALU.mult)
-                add_term(n, 0)
+            last_max = neg_max[:, n, 3:4]
+            maximum(z[3][:], last_max)
+            if n == 1:
+                invert(n, 1)
+                nc.vector.tensor_tensor(coef[:, n, 1:2], inv[:, n, 1:2], share[:, n, 1:2], ALU.mult)
+                add_term(n, 1)
             w = last_lane(n + 1, dense)
             exp_of(n, 2, z[2][:], neg_max[:, n, 2:3])
-            exp_of(n, 3, z[3][:], last_max[:])
+            exp_of(n, 3, z[3][:], last_max)
             finish_teacher(n)
 
-        banks = [row_scores(w, t, t) for t in range(2)]
+        z = [quad.tile([P, SLOTS], F32, name="z") for t in range(LANES)]
+        for h in range(2):
+            for t in range(2):
+                bank = bank_tile(LANES * (1 - h) + t, [P, HALF])
+                product(bank[:], xd, block(t), w, half_cols(h))
+                nc.vector.scalar_tensor_tensor(
+                    z[t][:, half_cols(h)], bank[:], us_t[:, t : t + 1], ts_all[:, half_cols(h)], ALU.mult, ALU.mult
+                )
+        logits(2, row_scores(w, 2, 2), z[2][:])
         turned_in = []
         for pair in range(2):
-            bank = bank_tile(2 + pair, [P, 2, HALF])
+            bank = bank_tile(3 + 3 * pair, [P, 2, P])
             for i in range(2):
-                product(bank[:, i, :], w, block(2 * pair + i), xd, slice(HALF, ROWS))
+                product(bank[:, i, :], w, block(2 * pair + i), xd, block(3))
             for i in range(2):
                 k = 2 * pair + i
-                scaled = quad.tile([P, HALF], F32, name="scaled")
+                scaled = quad.tile([P, P], F32, name="scaled")
                 nc.scalar.activation(scaled[:], bank[:, i, :], ACT.Copy, scale=ts_col[:, k : k + 1])
                 turned_in.append(scaled)
-        for t in range(2, LANES):
-            bank = bank_tile(2 + t, [P, SLOTS])
-            for k in range(LANES):
-                nc.tensor.transpose(bank[:, block(k)], turned_in[k][:, block(t - 2)], ident[:])
-            banks.append(bank)
-        z = [quad.tile([P, SLOTS], F32, name="z") for t in range(LANES)]
-        logits(0, banks[0], z[0][:])
-        logits(1, banks[1], z[1][:])
+        turned = bank_tile(5, [P, SLOTS])
+        for k in range(LANES):
+            nc.tensor.transpose(turned[:, block(k)], turned_in[k][:], ident[:])
         exponential(2, 0, z[0][:])
         exponential(2, 1, z[1][:])
-        turned_exponential(2, 2, z[2][:], banks[2])
+        exponential(2, 2, z[2][:])
         factor(2, 0)
-        turned_exponential(2, 3, z[3][:], banks[3])
+        turned_exponential(2, 3, z[3][:], turned)
         factor(2, 1)
         add_term(2, 0, 0, HALF)
         factor(2, 2)
@@ -345,9 +359,17 @@ def tile_attend_gkd2_pl_kernel(tc, xT, ws, wa, wb, us, ts, la, wt, offs, out_0, 
             nc.vector.tensor_tensor(
                 g_bf[:, lo * LANES : hi * LANES].rearrange("p (c i t) -> p c t i", i=RUN, t=LANES),
                 mix[:, :, lo:hi].rearrange("p t (c i) -> p c t i", i=RUN),
-                ts_all[:, lo:hi].rearrange("p (c i) -> p c i", i=RUN).unsqueeze(2).to_broadcast(
+                ts_bank[:, lo:hi].rearrange("p (c i) -> p c i", i=RUN).unsqueeze(2).to_broadcast(
                     [P, (hi - lo) // RUN, LANES, RUN]
                 ),
+                ALU.mult,
+            )
+
+        def round_g_beside(lo, hi):
+            nc.gpsimd.tensor_tensor(
+                g_bf[:, lo * LANES : hi * LANES].rearrange("p (s t) -> p s t", t=LANES),
+                mix[:, :, lo:hi].rearrange("p t s -> p s t"),
+                ts_all[:, lo:hi].unsqueeze(2).to_broadcast([P, hi - lo, LANES]),
                 ALU.mult,
             )
 
@@ -356,13 +378,15 @@ def tile_attend_gkd2_pl_kernel(tc, xT, ws, wa, wb, us, ts, la, wt, offs, out_0, 
                 g_codes[:, lo:hi].bitcast(E5M2), g_scales[:, lo:hi], g_bf[:, lo * LANES : hi * LANES]
             )
 
-        round_g(0, HALF)
+        round_g(0, HALF - BESIDE)
+        round_g_beside(HALF - BESIDE, HALF)
         late_term(1)
         quantise_g(0, HALF)
         late_term(2)
         late_term(3)
         round_g(HALF, HALF + P)
-        round_g(HALF + P, SLOTS)
+        round_g(HALF + P, SLOTS - BESIDE)
+        round_g_beside(SLOTS - BESIDE, SLOTS)
         quantise_g(HALF, HALF + P)
         quantise_g(HALF + P, SLOTS)
 
@@ -382,9 +406,12 @@ def tile_attend_gkd2_pl_kernel(tc, xT, ws, wa, wb, us, ts, la, wt, offs, out_0, 
 
         out_rows = out_0.rearrange("(q j) c -> q j c", j=LANES)
         sides = [
-            keep.tile([P, 2, LANES, CHUNK], BF16, name="rounded", tag=plane_buffer(4 * s), align_bytes=64)
+            keep.tile([P, 2, 2, CHUNK, 2], BF16, name="rounded", tag=plane_buffer(4 * s), align_bytes=64)
             for s in range(2)
         ]
+
+        def lane_of(j, s):
+            return sides[s][:, :, j // 2, :, j % 2]
 
         def scalar_scatter(j, h, dw):
             nc.scalar.activation(windows[j][:].indirect(half_offsets(h)), dw, ACT.Copy)
@@ -395,23 +422,24 @@ def tile_attend_gkd2_pl_kernel(tc, xT, ws, wa, wb, us, ts, la, wt, offs, out_0, 
         def side_of(j, s):
             return windows[j][:, 2 * s * CHUNK : 2 * (s + 1) * CHUNK].rearrange("p (c k) -> p c k", c=2)
 
-        def early_round(j, s):
-            nc.gpsimd.tensor_scalar(sides[s][:, :, j, :], side_of(j, s), 1.0, 1.0, ALU.mult, ALU.mult)
+        one = keep.tile([P, 1], F32, name="one")
+        nc.gpsimd.memset(one[:], 1.0)
 
         left, right, every = slice(0, HALF), slice(HALF, SLOTS), slice(0, SLOTS)
         scalar_scatter(0, 0, gradient(0, left, 4, "scalar", "dw_chain")[:])
         dw_1_left = gradient(1, left, 5, "scalar", "dw_chain")
         dw_0_right = gradient(0, right, 6, "vector")
-        dw_2 = gradient(2, every, 7, "vector", "dw0_256")
-        dw_1_right = gradient(1, right, 0, "scalar")
+        dw_1_right = gradient(1, right, 0, "vector")
+        dw_2 = gradient(2, every, 2, "vector", "dw0_256")
         nc.vector.tensor_copy(windows[0][:].indirect(half_offsets(1)), dw_0_right[:])
         store(0)
         scalar_scatter(1, 0, dw_1_left[:])
         scalar_scatter(1, 1, dw_1_right[:])
         store(1)
-        early_round(0, 0)
-        early_round(0, 1)
-        early_round(1, 0)
+        for s in range(2):
+            nc.gpsimd.tensor_scalar(lane_of(0, s), side_of(0, s), one[:], one[:], ALU.mult, ALU.mult)
+        one = keep.tile([P, 1], F32, name="one")
+        nc.gpsimd.memset(one[:], 1.0)
         nc.vector.tensor_copy(windows[2][:].indirect(offsets[:]), dw_2[:])
         store(2)
         dw_3 = gradient(3, every, 1, "scalar", "dw_chain")
@@ -419,52 +447,54 @@ def tile_attend_gkd2_pl_kernel(tc, xT, ws, wa, wb, us, ts, la, wt, offs, out_0, 
         scalar_scatter(3, 1, dw_3[:, right])
         store(3)
 
-        def rounded(c):
-            return sides[c // 2][:, c % 2, :, :]
-
         for s in range(2):
-            nc.vector.tensor_copy(sides[s][:, :, 2, :], side_of(2, s))
-        nc.vector.tensor_copy(sides[1][:, :, 1, :], side_of(1, 1))
-        nc.vector.tensor_copy(rounded(0)[:, 3, :], windows[3][:, 0:CHUNK])
-        nc.scalar.copy(rounded(1)[:, 3, :], windows[3][:, CHUNK : 2 * CHUNK])
-        nc.scalar.copy(sides[1][:, :, 3, :], side_of(3, 1))
+            nc.vector.tensor_scalar(lane_of(1, s), side_of(1, s), one[:], None, ALU.mult)
+        nc.vector.tensor_scalar(lane_of(2, 0), side_of(2, 0), one[:], None, ALU.mult)
+        last_one = keep.tile([P, 1], F32, name="last_one", tag="dw_chain")
+        nc.vector.tensor_copy(last_one[:], one[:])
+        for c in range(2):
+            nc.vector.tensor_scalar(lane_of(3, 0)[:, c, :], side_of(3, 0)[:, c, :], one[:], None, ALU.mult)
+        for c in range(2):
+            nc.scalar.copy(lane_of(3, 1)[:, c, :], side_of(3, 1)[:, c, :])
+            nc.scalar.activation(lane_of(2, 1)[:, c, :], side_of(2, 1)[:, c, :], ACT.Copy, scale=last_one[:])
 
         woven = [
             keep.tile([P, TOKENS // 2 * LANES], BF16, name="woven", tag=tag, align_bytes=64)
             for tag in ("x_raw", "ts_window")
         ]
         o_codes = keep.tile([P, TOKENS], U32, name="o_codes", align_bytes=64)
-        o_scales = keep.tile([P, TOKENS], U8, name="o_scales", align_bytes=64)
+        o_scales = keep.tile([P, CHUNK], U8, name="o_scales", align_bytes=64)
         words = out_1[0].rearrange("p c l -> p (c l)").bitcast(I32)
 
-        def weave(engine, lo, hi):
-            c = lo // CHUNK
-            first = lo - c // 2 * 2 * CHUNK
-            dst = woven[c // 2][:, first * LANES : (first + hi - lo) * LANES].rearrange("p (c i j) -> p c j i", i=RUN, j=LANES)
-            src = rounded(c)[:, :, lo - c * CHUNK : hi - c * CHUNK].rearrange("p j (c i) -> p c j i", i=RUN)
+        def weave(engine, c):
+            dst = woven[c // 2][:].bitcast(F32).rearrange("p (c k u) -> p c k u", c=2, u=2)[:, c % 2]
+            src = sides[c // 2][:].rearrange("p c u k e -> p (c u k e)").bitcast(F32)
+            src = src.rearrange("p (c u k) -> p c k u", c=2, u=2)[:, c % 2]
             if engine == "vector":
                 nc.vector.tensor_copy(dst, src)
             else:
                 nc.scalar.copy(dst, src)
 
-        def quantise_out(c):
-            cols = slice(c * CHUNK, (c + 1) * CHUNK)
+        def quantise_out(c, lo=0, hi=CHUNK):
+            cols = slice(c * CHUNK + lo, c * CHUNK + hi)
+            first = c % 2 * CHUNK
             nc.vector.quantize_mx(
-                o_codes[:, cols].bitcast(E4M3), o_scales[:, cols],
-                woven[c // 2][:, c % 2 * CHUNK * LANES : (c % 2 + 1) * CHUNK * LANES],
+                o_codes[:, cols].bitcast(E4M3), o_scales[LANES * c :, lo:hi],
+                woven[c // 2][:, (first + lo) * LANES : (first + hi) * LANES],
             )
             nc.sync.dma_start(words[:, cols], o_codes[:, cols].bitcast(I32))
 
-        shared = 2 * CHUNK + CHUNK // 2
-        weave("vector", 0, CHUNK)
-        weave("vector", CHUNK, 2 * CHUNK)
-        weave("scalar", shared, 3 * CHUNK)
-        weave("scalar", 3 * CHUNK, 4 * CHUNK)
+        weave("vector", 0)
+        weave("vector", 1)
         quantise_out(0)
-        weave("vector", 2 * CHUNK, shared)
+        weave("vector", 2)
+        weave("scalar", 3)
         quantise_out(1)
         quantise_out(2)
         quantise_out(3)
         for q in range(P // 32):
             queue = nc.scalar if q % 2 == 0 else nc.sync
-            queue.dma_start(out_2[0, 4 * q : 4 * q + 4, :].bitcast(I32), o_scales[32 * q : 32 * q + 4, :].bitcast(I32))
+            queue.dma_start(
+                out_2[0, 4 * q : 4 * q + 4, :].bitcast(I32).rearrange("r (c k) -> c r k", c=CHUNKS),
+                o_scales[32 * q : 32 * q + 16, :].bitcast(I32),
+            )

@@ -21,12 +21,15 @@ ROWS = 512
 SLOTS = 512
 TOKENS = 2048
 TABLES = 3
+STUDENT = 2
+VECTORS = 3
 HALF = SLOTS // 2
 RUN = 4
 PLANE_BUFFERS = 8
 BESIDE = 64
 CHUNK = 512
 CHUNKS = TOKENS // CHUNK
+TS_BANK = 7
 FLOPS = 4 * 2 * D * ROWS * SLOTS
 
 
@@ -50,9 +53,11 @@ def tile_attend_gkd2_pl_kernel(tc, xT, ws, wa, wb, us, ts, la, wt, offs, out_0, 
 
         nc.vector.memset(ts_window[0 : P - 1, :], 0.0)
         vectors = keep.tile([P, ROWS], F32, name="vectors")
-        nc.vector.memset(vectors[0 : P - 3, :], 0.0)
+        first = P // 2 - VECTORS
+        nc.vector.memset(vectors[0:first, :], 0.0)
+        nc.vector.memset(vectors[P // 2 :, :], 0.0)
         for i, src in enumerate((us, la, wt)):
-            nc.sync.dma_start(vectors[P - 3 + i : P - 2 + i, :], src.rearrange("r o -> o r"))
+            nc.sync.dma_start(vectors[first + i : first + i + 1, :], src.rearrange("r o -> o r"))
 
         ident = keep.tile([P, P], F32, name="ident")
         make_identity(nc, ident[:])
@@ -69,8 +74,8 @@ def tile_attend_gkd2_pl_kernel(tc, xT, ws, wa, wb, us, ts, la, wt, offs, out_0, 
                 planes.append(plane)
 
         windows = []
-        for w in range(LANES - 1):
-            window = keep.tile([P, TOKENS], F32, name="window%d" % w)
+        for j in range(LANES - 1):
+            window = keep.tile([P, TOKENS], F32, name="window%d" % j)
             nc.vector.memset(window[:], 0.0)
             windows.append(window)
 
@@ -92,29 +97,32 @@ def tile_attend_gkd2_pl_kernel(tc, xT, ws, wa, wb, us, ts, la, wt, offs, out_0, 
         windows.append(keep.tile([P, TOKENS], F32, name="window", tag="xd_bf", align_bytes=64))
         nc.vector.memset(windows[LANES - 1][:], 0.0)
 
+        def block(i):
+            return slice(i * P, (i + 1) * P)
+
         ts_row = keep.tile([P, SLOTS], F32, name="ts_row")
         nc.vector.tensor_copy(ts_row[:], ts_window[:].indirect(offsets[:]))
         bank = bank_tile(0, [P, LANES, P])
         for k in range(LANES):
-            nc.tensor.transpose(bank[:, k, :], ts_row[:, k * P : (k + 1) * P], ident[:])
+            nc.tensor.transpose(bank[:, k, :], ts_row[:, block(k)], ident[:])
         ts_col = keep.tile([P, LANES], F32, name="ts_col")
         nc.vector.tensor_copy(ts_col[:], bank[:, :, P - 1])
-        ts_bank = bank_tile(7, [P, SLOTS])
+        ts_bank = bank_tile(TS_BANK, [P, SLOTS])
         for k in range(LANES):
-            nc.tensor.transpose(ts_bank[:, k * P : (k + 1) * P], ts_col[:, k : k + 1].to_broadcast([P, P]), ident[:])
+            nc.tensor.transpose(ts_bank[:, block(k)], ts_col[:, k : k + 1].to_broadcast([P, P]), ident[:])
         ts_all = keep.tile([P, SLOTS], F32, name="ts_all")
         nc.vector.tensor_copy(ts_all[:], ts_bank[:])
 
         bank = bank_tile(1, [P, LANES, P])
         for t in range(LANES):
             nc.tensor.transpose(bank[:, t, :], vectors[:, t::LANES], ident[:])
-        by_row = keep.tile([P, 3, LANES], F32, name="by_row")
-        nc.vector.tensor_copy(by_row[:], bank[:, :, P - 3 :].rearrange("p t i -> p i t"))
-        us_t, la_t, wt_t = (by_row[:, i, :] for i in range(3))
+        by_row = keep.tile([P, VECTORS, LANES], F32, name="by_row")
+        nc.vector.tensor_copy(by_row[:], bank[:, :, first : P // 2].rearrange("p t i -> p i t"))
+        us_t, la_t, wt_t = (by_row[:, i, :] for i in range(VECTORS))
 
         neg_us = keep.tile([P, LANES], F32, name="neg_us")
         share = keep.tile([P, TABLES, LANES], F32, name="share")
-        weight = share[:, 2, :]
+        weight = share[:, STUDENT, :]
         nc.vector.tensor_scalar(neg_us[:], us_t, -1.0, None, ALU.mult)
         nc.vector.tensor_tensor(weight, wt_t, us_t, ALU.mult)
         nc.vector.scalar_tensor_tensor(share[:, 0, :], la_t, -1.0, weight, ALU.mult, ALU.mult)
@@ -123,29 +131,31 @@ def tile_attend_gkd2_pl_kernel(tc, xT, ws, wa, wb, us, ts, la, wt, offs, out_0, 
         x_words = x_pairs[:].bitcast(F32)
         xr_bf = keep.tile([P, D * LANES], BF16, name="xr_bf", align_bytes=64)
         xr_words = xr_bf[:].bitcast(F32).rearrange("p (j q u) -> p j q u", j=LANES, u=2)
-        for half in range(2):
-            bank = bank_tile(LANES + half, [P, LANES, P])
+        for pair in range(2):
+            bank = bank_tile(LANES + pair, [P, LANES, P])
             for i in range(LANES):
-                first = (LANES * half + i) * P
-                nc.tensor.transpose(bank[:, i, :], x_words[:, first : first + P], ident[:])
+                nc.tensor.transpose(bank[:, i, :], x_words[:, block(LANES * pair + i)], ident[:])
             nc.vector.tensor_copy(
-                xr_words[:, 2 * half : 2 * half + 2, :, :], bank[:].rearrange("p (j u) q -> p j q u", u=2)
+                xr_words[:, 2 * pair : 2 * pair + 2, :, :], bank[:].rearrange("p (j u) q -> p j q u", u=2)
             )
         xr_codes = keep.tile([P, D], U32, name="xr_codes", align_bytes=64)
         xr_scales = keep.tile([P, D], U8, name="xr_scales", align_bytes=64)
         nc.vector.quantize_mx(xr_codes[:].bitcast(E4M3), xr_scales[:], xr_bf[:])
+        xd = (xd_codes, xd_scales)
+        xr = (xr_codes, xr_scales)
 
         neg_max = keep.tile([P, TABLES, LANES], F32, name="neg_max")
         sums = {}
+        last_sums = {}
 
         def new_sum(n, t):
-            if n == 2:
+            if n == STUDENT:
                 sums[n, t] = keep.tile([P, 1], F32, name="sum", tag="sum%d" % t)[:]
-            elif t == 3:
-                sums[n, t] = sums[n, "last"][:, 1:2]
+            elif t == LANES - 1:
+                sums[n, t] = last_sums[n][:, 1:2]
             else:
                 held = keep.tile([P, 2], F32, name="sum", tag=plane_buffer(LANES * (n + 1) + t + 1), align_bytes=64)
-                sums[n, "last"] = held
+                last_sums[n] = held
                 sums[n, t] = held[:, 0:1]
             return sums[n, t]
 
@@ -154,12 +164,11 @@ def tile_attend_gkd2_pl_kernel(tc, xT, ws, wa, wb, us, ts, la, wt, offs, out_0, 
         e_b = keep.tile([P, LANES, SLOTS], F32, name="e_b")
         e_s = keep.tile([P, LANES, SLOTS], F32, name="e_s")
         exps = (mix, e_b, e_s)
+        left, right, every = slice(0, HALF), slice(HALF, SLOTS), slice(0, SLOTS)
+        halves = (left, right)
 
         def half_offsets(h):
             return offsets[:, h * (HALF // 16) : (h + 1) * (HALF // 16)]
-
-        def half_cols(h):
-            return slice(h * HALF, (h + 1) * HALF)
 
         def half_buffer(n, h):
             return "w_bf%d_%d" % (h, n)
@@ -170,26 +179,30 @@ def tile_attend_gkd2_pl_kernel(tc, xT, ws, wa, wb, us, ts, la, wt, offs, out_0, 
         def lanes_of(dense):
             return dense[:].bitcast(BF16).rearrange("p (j s) -> p j s", j=LANES)
 
+        def ahead_of_gather(dense, j):
+            return dense[:, j * HALF : j * HALF + 1]
+
         def gather(n, j, dense):
             nc.scalar.activation(lanes_of(dense)[:, j, :], planes[LANES * n + j][:].indirect(offsets[:]), ACT.Copy)
 
         def last_lane(n, dense):
-            halves = [
+            interleaved = [
                 keep.tile([P, HALF * LANES], BF16, name="w_bf", tag=half_buffer(n, h), align_bytes=64)
                 for h in range(2)
             ]
             codes = keep.tile([P, SLOTS], U32, name="w_codes%d" % n, align_bytes=64)
             scales = keep.tile([P, SLOTS], U8, name="w_scales%d" % n, align_bytes=64)
+            last = LANES - 1
             for h in range(2):
                 nc.scalar.activation(
-                    lanes_of(dense)[:, 3, half_cols(h)], planes[LANES * n + 3][:].indirect(half_offsets(h)), ACT.Copy
+                    lanes_of(dense)[:, last, halves[h]], planes[LANES * n + last][:].indirect(half_offsets(h)), ACT.Copy
                 )
                 nc.vector.tensor_copy(
-                    halves[h][:].rearrange("p (c i j) -> p c j i", i=RUN, j=LANES),
-                    lanes_of(dense)[:, :, half_cols(h)].rearrange("p j (c i) -> p c j i", i=RUN),
+                    interleaved[h][:].rearrange("p (c i j) -> p c j i", i=RUN, j=LANES),
+                    lanes_of(dense)[:, :, halves[h]].rearrange("p j (c i) -> p c j i", i=RUN),
                 )
             for h in range(2):
-                nc.vector.quantize_mx(codes[:, half_cols(h)].bitcast(E4M3), scales[:, half_cols(h)], halves[h][:])
+                nc.vector.quantize_mx(codes[:, halves[h]].bitcast(E4M3), scales[:, halves[h]], interleaved[h][:])
             return codes, scales
 
         def product(out, lhs, lhs_cols, rhs, rhs_cols, rhs_format=E4M3):
@@ -198,157 +211,130 @@ def tile_attend_gkd2_pl_kernel(tc, xT, ws, wa, wb, us, ts, la, wt, offs, out_0, 
                 rhs=rhs[0][:, rhs_cols].bitcast(rhs_format), rhs_scale=rhs[1][:, rhs_cols], start=True, stop=True,
             )
 
-        xd = (xd_codes, xd_scales)
-        xr = (xr_codes, xr_scales)
-
-        def block(i):
-            return slice(i * P, (i + 1) * P)
-
-        def row_scores(w, t, bank_number):
-            bank = bank_tile(bank_number, [P, SLOTS])
-            if t == 0:
-                for h in range(2):
-                    product(bank[:, half_cols(h)], xd, block(t), w, half_cols(h))
-            else:
-                product(bank[:], xd, block(t), w, slice(0, SLOTS))
+        def row_scores(w, t):
+            bank = bank_tile(t, [P, SLOTS])
+            for cols in halves if t == 0 else (every,):
+                product(bank[:, cols], xd, block(t), w, cols)
             return bank
 
-        def logits(t, bank, z):
-            nc.vector.scalar_tensor_tensor(z, bank[:], us_t[:, t : t + 1], ts_all[:], ALU.mult, ALU.mult)
+        def logits(t, scores, z, cols=every):
+            nc.vector.scalar_tensor_tensor(z, scores, us_t[:, t : t + 1], ts_all[:, cols], ALU.mult, ALU.mult)
 
-        def exponential(n, t, z, bias=None):
-            bias = neg_max[:, n, t : t + 1] if bias is None else bias
-            nc.vector.tensor_reduce(bias, z, mybir.AxisListType.X, ALU.max, negate=True)
-            nc.scalar.activation(
-                exps[n][:, t, :], z, ACT.Exp, bias=bias, scale=1.0,
-                accum_out=new_sum(n, t),
-            )
+        def maximum(z, negated):
+            nc.vector.tensor_reduce(negated, z, mybir.AxisListType.X, ALU.max, negate=True)
 
-        def turned_exponential(n, t, neg_z, bank):
-            nc.vector.tensor_scalar(
-                neg_z, bank[:], neg_us[:, t : t + 1], None, ALU.mult, ALU.min, accum_out=neg_max[:, n, t : t + 1]
-            )
-            nc.scalar.activation(
-                exps[n][:, t, :], neg_z, ACT.Exp, bias=neg_max[:, n, t : t + 1], scale=-1.0,
-                accum_out=new_sum(n, t),
-            )
+        def exponential(n, t, z, negated_max, sign=1.0):
+            nc.scalar.activation(exps[n][:, t, :], z, ACT.Exp, bias=negated_max, scale=sign, accum_out=new_sum(n, t))
 
         def invert(n, t):
             nc.vector.reciprocal(inv[:, n, t : t + 1], sums[n, t])
 
         coef = keep.tile([P, TABLES, LANES], F32, name="coef")
 
-        def factor(n, t):
-            invert(n, t)
-            nc.scalar.activation(coef[:, n, t : t + 1], inv[:, n, t : t + 1], ACT.Copy, scale=share[:, n, t : t + 1])
+        def coefficient(n, t, inverse):
+            nc.scalar.activation(coef[:, n, t : t + 1], inverse, ACT.Copy, scale=share[:, n, t : t + 1])
 
-        def add_term(n, t, lo=0, hi=SLOTS):
+        def add_term(n, t, factors, cols):
             nc.vector.scalar_tensor_tensor(
-                mix[:, t, lo:hi], exps[n][:, t, lo:hi], coef[:, n, t : t + 1], mix[:, t, lo:hi], ALU.mult, ALU.add
+                mix[:, t, cols], exps[n][:, t, cols], factors[:, t : t + 1], mix[:, t, cols], ALU.mult, ALU.add
             )
 
-        def scale_term(engine, n, t, inverse):
+        def scale_beside(n, t, inverse):
             e = exps[n]
-            engine.tensor_scalar(e[:, t, :], e[:, t, :], inverse, share[:, n, t : t + 1], ALU.mult, ALU.mult)
+            nc.gpsimd.tensor_scalar(e[:, t, :], e[:, t, :], inverse, share[:, n, t : t + 1], ALU.mult, ALU.mult)
+
+        def add_beside(t):
+            nc.gpsimd.tensor_tensor(mix[:, t, :], mix[:, t, :], e_b[:, t, :], ALU.add)
 
         def finish_teacher(n):
             late = keep.tile([P, LANES], F32, name="late", tag=half_buffer(n + 1, 1), align_bytes=64)
             if n == 0:
                 nc.vector.reciprocal(late[:, 1:2], sums[n, 1])
-            nc.vector.reciprocal(late[:, 2:4], sums[n, "last"][:])
+            nc.vector.reciprocal(late[:, 2:4], last_sums[n][:])
             if n == 0:
                 for t in range(1, LANES):
-                    scale_term(nc.gpsimd, n, t, late[:, t : t + 1])
+                    scale_beside(n, t, late[:, t : t + 1])
             else:
-                scale_term(nc.gpsimd, n, 2, late[:, 2:3])
-                nc.scalar.activation(coef[:, n, 3:4], late[:, 3:4], ACT.Copy, scale=share[:, n, 3:4])
+                scale_beside(n, 2, late[:, 2:3])
+                coefficient(n, 3, late[:, 3:4])
                 nc.scalar.activation(e_b[:, 3, :], e_b[:, 3, :], ACT.Copy, scale=coef[:, n, 3:4])
                 for t in (2, 3):
-                    nc.gpsimd.tensor_tensor(mix[:, t, :], mix[:, t, :], e_b[:, t, :], ALU.add)
-
-        def maximum(z, bias):
-            nc.vector.tensor_reduce(bias, z, mybir.AxisListType.X, ALU.max, negate=True)
-
-        def exp_of(n, t, z, bias):
-            nc.scalar.activation(exps[n][:, t, :], z, ACT.Exp, bias=bias, scale=1.0, accum_out=new_sum(n, t))
+                    add_beside(t)
 
         dense = new_dense()
         for j in range(LANES - 1):
             gather(0, j, dense)
         w = last_lane(0, dense)
-        for n in range(2):
+        for n in range(STUDENT):
             dense = new_dense()
             gather(n + 1, 0, dense)
             gather(n + 1, 1, dense)
-            banks = [row_scores(w, t, t) for t in range(LANES)]
+            banks = [row_scores(w, t) for t in range(LANES)]
             z = [quad.tile([P, SLOTS], F32, name="z") for t in range(LANES - 1)]
-            logits(0, banks[0], z[0][:])
-            logits(1, banks[1], z[1][:])
-            exponential(n, 0, z[0][:], dense[:, 2 * HALF : 2 * HALF + 1])
+            logits(0, banks[0][:], z[0][:])
+            logits(1, banks[1][:], z[1][:])
+            maximum(z[0][:], ahead_of_gather(dense, 2))
+            exponential(n, 0, z[0][:], ahead_of_gather(dense, 2))
             gather(n + 1, 2, dense)
-            logits(2, banks[2], z[2][:])
-            exponential(n, 1, z[1][:], dense[:, 3 * HALF : 3 * HALF + 1])
+            logits(2, banks[2][:], z[2][:])
+            maximum(z[1][:], ahead_of_gather(dense, 3))
+            exponential(n, 1, z[1][:], ahead_of_gather(dense, 3))
             invert(n, 0)
-            scale_term(nc.gpsimd, n, 0, inv[:, n, 0:1])
+            scale_beside(n, 0, inv[:, n, 0:1])
             if n == 1:
-                nc.gpsimd.tensor_tensor(mix[:, 0, :], mix[:, 0, :], e_b[:, 0, :], ALU.add)
+                add_beside(0)
             z.append(keep.tile([P, SLOTS], F32, name="z", tag=plane_buffer(LANES * (n + 1) + 1), align_bytes=64))
-            logits(3, banks[3], z[3][:])
-            maximum(z[2][:], neg_max[:, n, 2:3])
-            last_max = neg_max[:, n, 3:4]
-            maximum(z[3][:], last_max)
+            logits(3, banks[3][:], z[3][:])
+            for t in (2, 3):
+                maximum(z[t][:], neg_max[:, n, t : t + 1])
             if n == 1:
                 invert(n, 1)
                 nc.vector.tensor_tensor(coef[:, n, 1:2], inv[:, n, 1:2], share[:, n, 1:2], ALU.mult)
-                add_term(n, 1)
+                add_term(n, 1, coef[:, n, :], every)
             w = last_lane(n + 1, dense)
-            exp_of(n, 2, z[2][:], neg_max[:, n, 2:3])
-            exp_of(n, 3, z[3][:], last_max)
+            for t in (2, 3):
+                exponential(n, t, z[t][:], neg_max[:, n, t : t + 1])
             finish_teacher(n)
 
         z = [quad.tile([P, SLOTS], F32, name="z") for t in range(LANES)]
         for h in range(2):
             for t in range(2):
                 bank = bank_tile(LANES * (1 - h) + t, [P, HALF])
-                product(bank[:], xd, block(t), w, half_cols(h))
-                nc.vector.scalar_tensor_tensor(
-                    z[t][:, half_cols(h)], bank[:], us_t[:, t : t + 1], ts_all[:, half_cols(h)], ALU.mult, ALU.mult
-                )
-        logits(2, row_scores(w, 2, 2), z[2][:])
-        turned_in = []
-        for pair in range(2):
-            bank = bank_tile(3 + 3 * pair, [P, 2, P])
+                product(bank[:], xd, block(t), w, halves[h])
+                logits(t, bank[:], z[t][:, halves[h]], halves[h])
+        logits(2, row_scores(w, 2)[:], z[2][:])
+        scaled = []
+        for pair, bank_number in enumerate((3, 6)):
+            bank = bank_tile(bank_number, [P, 2, P])
             for i in range(2):
                 product(bank[:, i, :], w, block(2 * pair + i), xd, block(3))
             for i in range(2):
                 k = 2 * pair + i
-                scaled = quad.tile([P, P], F32, name="scaled")
-                nc.scalar.activation(scaled[:], bank[:, i, :], ACT.Copy, scale=ts_col[:, k : k + 1])
-                turned_in.append(scaled)
+                scaled.append(quad.tile([P, P], F32, name="scaled"))
+                nc.scalar.activation(scaled[k][:], bank[:, i, :], ACT.Copy, scale=ts_col[:, k : k + 1])
         turned = bank_tile(5, [P, SLOTS])
         for k in range(LANES):
-            nc.tensor.transpose(turned[:, block(k)], turned_in[k][:], ident[:])
-        exponential(2, 0, z[0][:])
-        exponential(2, 1, z[1][:])
-        exponential(2, 2, z[2][:])
-        factor(2, 0)
-        turned_exponential(2, 3, z[3][:], turned)
-        factor(2, 1)
-        add_term(2, 0, 0, HALF)
-        factor(2, 2)
-        add_term(2, 1, 0, HALF)
-        factor(2, 3)
-        add_term(2, 2, 0, HALF)
-        add_term(2, 3, 0, HALF)
+            nc.tensor.transpose(turned[:, block(k)], scaled[k][:], ident[:])
+        for t in range(LANES - 1):
+            maximum(z[t][:], neg_max[:, STUDENT, t : t + 1])
+            exponential(STUDENT, t, z[t][:], neg_max[:, STUDENT, t : t + 1])
+
+        def student_coefficient(t):
+            invert(STUDENT, t)
+            coefficient(STUDENT, t, inv[:, STUDENT, t : t + 1])
+
+        student_coefficient(0)
+        nc.vector.tensor_scalar(
+            z[3][:], turned[:], neg_us[:, 3:4], None, ALU.mult, ALU.min, accum_out=neg_max[:, STUDENT, 3:4]
+        )
+        exponential(STUDENT, 3, z[3][:], neg_max[:, STUDENT, 3:4], -1.0)
+        for t in range(LANES - 1):
+            student_coefficient(t + 1)
+            add_term(STUDENT, t, coef[:, STUDENT, :], left)
+        add_term(STUDENT, LANES - 1, coef[:, STUDENT, :], left)
         coef_late = keep.tile([P, LANES], F32, name="coef_late")
-        nc.scalar.copy(coef_late[:], coef[:, 2, :])
-
-        def late_term(t):
-            nc.vector.scalar_tensor_tensor(
-                mix[:, t, HALF:], e_s[:, t, HALF:], coef_late[:, t : t + 1], mix[:, t, HALF:], ALU.mult, ALU.add
-            )
-
-        late_term(0)
+        nc.scalar.copy(coef_late[:], coef[:, STUDENT, :])
+        add_term(STUDENT, 0, coef_late, right)
 
         g_bf = keep.tile([P, SLOTS * LANES], BF16, name="g_bf", align_bytes=64)
         g_codes = keep.tile([P, SLOTS], U32, name="g_codes", align_bytes=64)
@@ -380,33 +366,27 @@ def tile_attend_gkd2_pl_kernel(tc, xT, ws, wa, wb, us, ts, la, wt, offs, out_0, 
 
         round_g(0, HALF - BESIDE)
         round_g_beside(HALF - BESIDE, HALF)
-        late_term(1)
+        add_term(STUDENT, 1, coef_late, right)
         quantise_g(0, HALF)
-        late_term(2)
-        late_term(3)
+        add_term(STUDENT, 2, coef_late, right)
+        add_term(STUDENT, 3, coef_late, right)
         round_g(HALF, HALF + P)
         round_g(HALF + P, SLOTS - BESIDE)
         round_g_beside(SLOTS - BESIDE, SLOTS)
         quantise_g(HALF, HALF + P)
         quantise_g(HALF + P, SLOTS)
 
-        def gradient(j, cols, bank_number, engine, buffer=None):
+        def gradient(j, cols, bank_number, copy, buffer):
             width = cols.stop - cols.start
-            bank = psum.tile([P, width], F32, name="dw_sums", tag="bank%d" % bank_number)
-            nc.tensor.matmul_mx(
-                bank[:], lhsT=xr_codes[:, j * P : (j + 1) * P].bitcast(E4M3), lhsT_scale=xr_scales[:, j * P : (j + 1) * P],
-                rhs=g_codes[:, cols].bitcast(E5M2), rhs_scale=g_scales[:, cols], start=True, stop=True,
-            )
-            dw = keep.tile([P, width], F32, name="dw", tag=buffer or "dw%d_%d" % (j, cols.start))
-            if engine == "vector":
-                nc.vector.tensor_copy(dw[:], bank[:])
-            else:
-                nc.scalar.copy(dw[:], bank[:])
+            bank = bank_tile(bank_number, [P, width])
+            product(bank[:], xr, block(j), g, cols, E5M2)
+            dw = keep.tile([P, width], F32, name="dw", tag=buffer)
+            copy(dw[:], bank[:])
             return dw
 
         out_rows = out_0.rearrange("(q j) c -> q j c", j=LANES)
         sides = [
-            keep.tile([P, 2, 2, CHUNK, 2], BF16, name="rounded", tag=plane_buffer(4 * s), align_bytes=64)
+            keep.tile([P, 2, 2, CHUNK, 2], BF16, name="rounded", tag=plane_buffer(LANES * s), align_bytes=64)
             for s in range(2)
         ]
 
@@ -422,38 +402,39 @@ def tile_attend_gkd2_pl_kernel(tc, xT, ws, wa, wb, us, ts, la, wt, offs, out_0, 
         def side_of(j, s):
             return windows[j][:, 2 * s * CHUNK : 2 * (s + 1) * CHUNK].rearrange("p (c k) -> p c k", c=2)
 
-        one = keep.tile([P, 1], F32, name="one")
-        nc.gpsimd.memset(one[:], 1.0)
+        def new_one():
+            one = keep.tile([P, 1], F32, name="one")
+            nc.gpsimd.memset(one[:], 1.0)
+            return one
 
-        left, right, every = slice(0, HALF), slice(HALF, SLOTS), slice(0, SLOTS)
-        scalar_scatter(0, 0, gradient(0, left, 4, "scalar", "dw_chain")[:])
-        dw_1_left = gradient(1, left, 5, "scalar", "dw_chain")
-        dw_0_right = gradient(0, right, 6, "vector")
-        dw_1_right = gradient(1, right, 0, "vector")
-        dw_2 = gradient(2, every, 2, "vector", "dw0_256")
+        first_one = new_one()
+        scalar_scatter(0, 0, gradient(0, left, 4, nc.scalar.copy, "dw_chain")[:])
+        dw_1_left = gradient(1, left, 5, nc.scalar.copy, "dw_chain")
+        dw_0_right = gradient(0, right, 6, nc.vector.tensor_copy, "dw0_256")
+        dw_1_right = gradient(1, right, 0, nc.vector.tensor_copy, "dw1_256")
+        dw_2 = gradient(2, every, 2, nc.vector.tensor_copy, "dw0_256")
         nc.vector.tensor_copy(windows[0][:].indirect(half_offsets(1)), dw_0_right[:])
         store(0)
         scalar_scatter(1, 0, dw_1_left[:])
         scalar_scatter(1, 1, dw_1_right[:])
         store(1)
         for s in range(2):
-            nc.gpsimd.tensor_scalar(lane_of(0, s), side_of(0, s), one[:], one[:], ALU.mult, ALU.mult)
-        one = keep.tile([P, 1], F32, name="one")
-        nc.gpsimd.memset(one[:], 1.0)
+            nc.gpsimd.tensor_scalar(lane_of(0, s), side_of(0, s), first_one[:], first_one[:], ALU.mult, ALU.mult)
+        second_one = new_one()
         nc.vector.tensor_copy(windows[2][:].indirect(offsets[:]), dw_2[:])
         store(2)
-        dw_3 = gradient(3, every, 1, "scalar", "dw_chain")
-        scalar_scatter(3, 0, dw_3[:, left])
-        scalar_scatter(3, 1, dw_3[:, right])
+        dw_3 = gradient(3, every, 1, nc.scalar.copy, "dw_chain")
+        for h in range(2):
+            scalar_scatter(3, h, dw_3[:, halves[h]])
         store(3)
 
         for s in range(2):
-            nc.vector.tensor_scalar(lane_of(1, s), side_of(1, s), one[:], None, ALU.mult)
-        nc.vector.tensor_scalar(lane_of(2, 0), side_of(2, 0), one[:], None, ALU.mult)
+            nc.vector.tensor_scalar(lane_of(1, s), side_of(1, s), second_one[:], None, ALU.mult)
+        nc.vector.tensor_scalar(lane_of(2, 0), side_of(2, 0), second_one[:], None, ALU.mult)
         last_one = keep.tile([P, 1], F32, name="last_one", tag="dw_chain")
-        nc.vector.tensor_copy(last_one[:], one[:])
+        nc.vector.tensor_copy(last_one[:], second_one[:])
         for c in range(2):
-            nc.vector.tensor_scalar(lane_of(3, 0)[:, c, :], side_of(3, 0)[:, c, :], one[:], None, ALU.mult)
+            nc.vector.tensor_scalar(lane_of(3, 0)[:, c, :], side_of(3, 0)[:, c, :], second_one[:], None, ALU.mult)
         for c in range(2):
             nc.scalar.copy(lane_of(3, 1)[:, c, :], side_of(3, 1)[:, c, :])
             nc.scalar.activation(lane_of(2, 1)[:, c, :], side_of(2, 1)[:, c, :], ACT.Copy, scale=last_one[:])
@@ -466,32 +447,26 @@ def tile_attend_gkd2_pl_kernel(tc, xT, ws, wa, wb, us, ts, la, wt, offs, out_0, 
         o_scales = keep.tile([P, CHUNK], U8, name="o_scales", align_bytes=64)
         words = out_1[0].rearrange("p c l -> p (c l)").bitcast(I32)
 
-        def weave(engine, c):
+        def weave(copy, c):
             dst = woven[c // 2][:].bitcast(F32).rearrange("p (c k u) -> p c k u", c=2, u=2)[:, c % 2]
             src = sides[c // 2][:].rearrange("p c u k e -> p (c u k e)").bitcast(F32)
-            src = src.rearrange("p (c u k) -> p c k u", c=2, u=2)[:, c % 2]
-            if engine == "vector":
-                nc.vector.tensor_copy(dst, src)
-            else:
-                nc.scalar.copy(dst, src)
+            copy(dst, src.rearrange("p (c u k) -> p c k u", c=2, u=2)[:, c % 2])
 
-        def quantise_out(c, lo=0, hi=CHUNK):
-            cols = slice(c * CHUNK + lo, c * CHUNK + hi)
-            first = c % 2 * CHUNK
+        def quantise_out(c):
+            cols = slice(c * CHUNK, (c + 1) * CHUNK)
             nc.vector.quantize_mx(
-                o_codes[:, cols].bitcast(E4M3), o_scales[LANES * c :, lo:hi],
-                woven[c // 2][:, (first + lo) * LANES : (first + hi) * LANES],
+                o_codes[:, cols].bitcast(E4M3), o_scales[LANES * c :, :],
+                woven[c // 2][:, c % 2 * CHUNK * LANES : (c % 2 + 1) * CHUNK * LANES],
             )
             nc.sync.dma_start(words[:, cols], o_codes[:, cols].bitcast(I32))
 
-        weave("vector", 0)
-        weave("vector", 1)
+        weave(nc.vector.tensor_copy, 0)
+        weave(nc.vector.tensor_copy, 1)
         quantise_out(0)
-        weave("vector", 2)
-        weave("scalar", 3)
-        quantise_out(1)
-        quantise_out(2)
-        quantise_out(3)
+        weave(nc.vector.tensor_copy, 2)
+        weave(nc.scalar.copy, 3)
+        for c in range(1, CHUNKS):
+            quantise_out(c)
         for q in range(P // 32):
             queue = nc.scalar if q % 2 == 0 else nc.sync
             queue.dma_start(

@@ -193,13 +193,18 @@ def tile_attend_gkd2_pl_kernel(tc, xT, ws, wa, wb, us, ts, la, wt, offs, out_0, 
             codes = keep.tile([P, SLOTS], U32, name="w_codes%d" % n, align_bytes=64)
             scales = keep.tile([P, SLOTS], U8, name="w_scales%d" % n, align_bytes=64)
             last = LANES - 1
-            for h in range(2):
+            for lo, hi in ((k * P, (k + 1) * P) for k in range(LANES)):
                 nc.scalar.activation(
-                    lanes_of(dense)[:, last, halves[h]], planes[LANES * n + last][:].indirect(half_offsets(h)), ACT.Copy
+                    lanes_of(dense)[:, last, lo:hi],
+                    planes[LANES * n + last][:].indirect(offsets[:, lo // 16 : hi // 16]),
+                    ACT.Copy,
                 )
+                start = lo % HALF * LANES
                 nc.vector.tensor_copy(
-                    interleaved[h][:].rearrange("p (c i j) -> p c j i", i=RUN, j=LANES),
-                    lanes_of(dense)[:, :, halves[h]].rearrange("p j (c i) -> p c j i", i=RUN),
+                    interleaved[lo // HALF][:, start : start + (hi - lo) * LANES].rearrange(
+                        "p (c i j) -> p c j i", i=RUN, j=LANES
+                    ),
+                    lanes_of(dense)[:, :, lo:hi].rearrange("p j (c i) -> p c j i", i=RUN),
                 )
             for h in range(2):
                 nc.vector.quantize_mx(codes[:, halves[h]].bitcast(E4M3), scales[:, halves[h]], interleaved[h][:])
@@ -380,7 +385,7 @@ def tile_attend_gkd2_pl_kernel(tc, xT, ws, wa, wb, us, ts, la, wt, offs, out_0, 
             width = cols.stop - cols.start
             bank = bank_tile(bank_number, [P, width])
             product(bank[:], xr, block(j), g, cols, E5M2)
-            dw = keep.tile([P, width], F32, name="dw", tag=buffer)
+            dw = keep.tile([P, width], F32, name="dw", tag=buffer, align_bytes=64)
             copy(dw[:], bank[:])
             return dw
 
@@ -409,10 +414,10 @@ def tile_attend_gkd2_pl_kernel(tc, xT, ws, wa, wb, us, ts, la, wt, offs, out_0, 
 
         first_one = new_one()
         scalar_scatter(0, 0, gradient(0, left, 4, nc.scalar.copy, "dw_chain")[:])
-        dw_1_left = gradient(1, left, 5, nc.scalar.copy, "dw_chain")
+        dw_1_left = gradient(1, left, 5, nc.vector.tensor_copy, "g_bf")
         dw_0_right = gradient(0, right, 6, nc.vector.tensor_copy, "dw0_256")
         dw_1_right = gradient(1, right, 0, nc.vector.tensor_copy, "dw1_256")
-        dw_2 = gradient(2, every, 2, nc.vector.tensor_copy, "dw0_256")
+        dw_2 = gradient(2, every, 0, nc.vector.tensor_copy, "dw_2")
         nc.vector.tensor_copy(windows[0][:].indirect(half_offsets(1)), dw_0_right[:])
         store(0)
         scalar_scatter(1, 0, dw_1_left[:])
@@ -428,16 +433,18 @@ def tile_attend_gkd2_pl_kernel(tc, xT, ws, wa, wb, us, ts, la, wt, offs, out_0, 
             scalar_scatter(3, h, dw_3[:, halves[h]])
         store(3)
 
-        for s in range(2):
-            nc.vector.tensor_scalar(lane_of(1, s), side_of(1, s), second_one[:], None, ALU.mult)
+        nc.vector.tensor_scalar(lane_of(1, 0), side_of(1, 0), second_one[:], None, ALU.mult)
+        for c, cols in ((0, every), (1, left)):
+            nc.vector.tensor_scalar(lane_of(1, 1)[:, c, cols], side_of(1, 1)[:, c, cols], second_one[:], None, ALU.mult)
         nc.vector.tensor_scalar(lane_of(2, 0), side_of(2, 0), second_one[:], None, ALU.mult)
-        last_one = keep.tile([P, 1], F32, name="last_one", tag="dw_chain")
+        last_one = keep.tile([P, 1], F32, name="last_one", tag="dw_chain", align_bytes=64)
         nc.vector.tensor_copy(last_one[:], second_one[:])
         for c in range(2):
             nc.vector.tensor_scalar(lane_of(3, 0)[:, c, :], side_of(3, 0)[:, c, :], second_one[:], None, ALU.mult)
         for c in range(2):
             nc.scalar.copy(lane_of(3, 1)[:, c, :], side_of(3, 1)[:, c, :])
             nc.scalar.activation(lane_of(2, 1)[:, c, :], side_of(2, 1)[:, c, :], ACT.Copy, scale=last_one[:])
+        nc.scalar.activation(lane_of(1, 1)[:, 1, right], side_of(1, 1)[:, 1, right], ACT.Copy, scale=last_one[:])
 
         woven = [
             keep.tile([P, TOKENS // 2 * LANES], BF16, name="woven", tag=tag, align_bytes=64)

@@ -333,22 +333,54 @@ def tile_attend_gkd2_pl_kernel(tc, xT, ws, wa, wb, us, ts, la, wt, offs, out_0, 
             z[3][:], turned[:], neg_us[:, 3:4], None, ALU.mult, ALU.min, accum_out=neg_max[:, STUDENT, 3:4]
         )
         exponential(STUDENT, 3, z[3][:], neg_max[:, STUDENT, 3:4], -1.0)
+        third, fourth = block(2), block(3)
+        terms = keep.tile([P, LANES, P], F32, name="terms")
+        summed = bank_tile(2, [P, LANES, P])
+        for t in range(LANES):
+            nc.tensor.matmul(summed[:, t, :], mix[:, t, fourth], ident[:], start=t == 0, stop=False, is_transpose=True)
+
+        def add_turned(t):
+            nc.tensor.matmul(
+                summed[:, t, :], terms[:, t, :], ident[:], start=False, stop=t == LANES - 1, is_transpose=True
+            )
+
         for t in range(LANES - 1):
             student_coefficient(t + 1)
             add_term(STUDENT, t, coef[:, STUDENT, :], left)
-        add_term(STUDENT, LANES - 1, coef[:, STUDENT, :], left)
+            nc.vector.tensor_scalar(terms[:, t, :], e_s[:, t, fourth], coef[:, STUDENT, t : t + 1], None, ALU.mult)
+            add_turned(t)
+        nc.scalar.activation(terms[:, 3, :], e_s[:, 3, fourth], ACT.Copy, scale=coef[:, STUDENT, 3:4])
+        add_turned(3)
+        for k in range(2):
+            add_term(STUDENT, LANES - 1, coef[:, STUDENT, :], block(k))
         coef_late = keep.tile([P, LANES], F32, name="coef_late")
         nc.scalar.copy(coef_late[:], coef[:, STUDENT, :])
-        add_term(STUDENT, 0, coef_late, right)
 
-        g_bf = keep.tile([P, SLOTS * LANES], BF16, name="g_bf", align_bytes=64)
+        g_bf = [keep.tile([P, P * LANES], BF16, name="g_bf", tag="g_bf%d" % k, align_bytes=64) for k in range(LANES)]
+
+        def g_words(lo, hi):
+            return g_bf[lo // P][:, lo % P * LANES : (lo % P + hi - lo) * LANES]
+
         g_codes = keep.tile([P, SLOTS], U32, name="g_codes", align_bytes=64)
         g_scales = keep.tile([P, SLOTS], U8, name="g_scales", align_bytes=64)
         g = (g_codes, g_scales)
 
+        back = bank_tile(3, [P, 2, P])
+
+        def turn_back(u, buffer):
+            by_slot = keep.tile([P, 2 * P], BF16, name="by_slot", tag=buffer, align_bytes=64)
+            nc.scalar.activation(
+                by_slot[:].rearrange("s (p e) -> s p e", e=2),
+                summed[:].rearrange("s (u e) p -> s u p e", u=2)[:, u],
+                ACT.Copy, scale=ts_col[:, 3:4],
+            )
+            nc.tensor.transpose(back[:, u, :], by_slot[:].bitcast(F32), ident[:])
+
+        turn_back(0, "by_slot")
+
         def round_g(lo, hi):
             nc.vector.tensor_tensor(
-                g_bf[:, lo * LANES : hi * LANES].rearrange("p (c i t) -> p c t i", i=RUN, t=LANES),
+                g_words(lo, hi).rearrange("p (c i t) -> p c t i", i=RUN, t=LANES),
                 mix[:, :, lo:hi].rearrange("p t (c i) -> p c t i", i=RUN),
                 ts_bank[:, lo:hi].rearrange("p (c i) -> p c i", i=RUN).unsqueeze(2).to_broadcast(
                     [P, (hi - lo) // RUN, LANES, RUN]
@@ -358,7 +390,7 @@ def tile_attend_gkd2_pl_kernel(tc, xT, ws, wa, wb, us, ts, la, wt, offs, out_0, 
 
         def round_g_beside(lo, hi):
             nc.gpsimd.tensor_tensor(
-                g_bf[:, lo * LANES : hi * LANES].rearrange("p (s t) -> p s t", t=LANES),
+                g_words(lo, hi).rearrange("p (s t) -> p s t", t=LANES),
                 mix[:, :, lo:hi].rearrange("p t s -> p s t"),
                 ts_all[:, lo:hi].unsqueeze(2).to_broadcast([P, hi - lo, LANES]),
                 ALU.mult,
@@ -366,20 +398,8 @@ def tile_attend_gkd2_pl_kernel(tc, xT, ws, wa, wb, us, ts, la, wt, offs, out_0, 
 
         def quantise_g(lo, hi):
             nc.vector.quantize_mx(
-                g_codes[:, lo:hi].bitcast(E5M2), g_scales[:, lo:hi], g_bf[:, lo * LANES : hi * LANES]
+                g_codes[:, lo:hi].bitcast(E5M2), g_scales[:, lo:hi], g_words(lo, hi)
             )
-
-        round_g(0, HALF - BESIDE)
-        round_g_beside(HALF - BESIDE, HALF)
-        add_term(STUDENT, 1, coef_late, right)
-        quantise_g(0, HALF)
-        add_term(STUDENT, 2, coef_late, right)
-        add_term(STUDENT, 3, coef_late, right)
-        round_g(HALF, HALF + P)
-        round_g(HALF + P, SLOTS - BESIDE)
-        round_g_beside(SLOTS - BESIDE, SLOTS)
-        quantise_g(HALF, HALF + P)
-        quantise_g(HALF + P, SLOTS)
 
         def gradient(j, cols, bank_number, copy, buffer):
             width = cols.stop - cols.start
@@ -413,9 +433,32 @@ def tile_attend_gkd2_pl_kernel(tc, xT, ws, wa, wb, us, ts, la, wt, offs, out_0, 
             return one
 
         first_one = new_one()
-        scalar_scatter(0, 0, gradient(0, left, 4, nc.scalar.copy, "dw_chain")[:])
-        dw_1_left = gradient(1, left, 5, nc.vector.tensor_copy, "g_bf")
-        dw_0_right = gradient(0, right, 6, nc.vector.tensor_copy, "dw0_256")
+        round_g(0, P)
+        round_g(P, HALF - BESIDE)
+        round_g_beside(HALF - BESIDE, HALF)
+        dw_0_left = keep.tile([P, HALF], F32, name="dw", tag="dw_chain", align_bytes=64)
+        for k in range(2):
+            quantise_g(k * P, (k + 1) * P)
+            bank = bank_tile(4 + k, [P, P])
+            product(bank[:], xr, block(0), g, block(k), E5M2)
+            if k == 0:
+                turn_back(1, "g_bf0")
+            nc.scalar.copy(dw_0_left[:, block(k)], bank[:])
+        dw_1_left = gradient(1, left, 6, nc.scalar.copy, "dw_1_left")
+        scalar_scatter(0, 0, dw_0_left[:])
+        for t in range(LANES):
+            add_term(STUDENT, t, coef_late, third)
+        round_g(HALF, HALF + P - BESIDE // 2)
+        round_g_beside(HALF + P - BESIDE // 2, HALF + P)
+        nc.vector.tensor_copy(
+            g_bf[3][:].bitcast(F32).rearrange("p (s u) -> p s u", u=2), back[:].rearrange("p u s -> p s u")
+        )
+        bank = bank_tile(1, [P, HALF])
+        for k in range(2):
+            quantise_g(HALF + k * P, HALF + (k + 1) * P)
+            product(bank[:, block(k)], xr, block(0), g, block(2 + k), E5M2)
+        dw_0_right = keep.tile([P, HALF], F32, name="dw", tag="dw0_256", align_bytes=64)
+        nc.vector.tensor_copy(dw_0_right[:], bank[:])
         dw_1_right = gradient(1, right, 0, nc.vector.tensor_copy, "dw1_256")
         dw_2 = gradient(2, every, 0, nc.vector.tensor_copy, "dw_2")
         nc.vector.tensor_copy(windows[0][:].indirect(half_offsets(1)), dw_0_right[:])
@@ -428,7 +471,7 @@ def tile_attend_gkd2_pl_kernel(tc, xT, ws, wa, wb, us, ts, la, wt, offs, out_0, 
         second_one = new_one()
         nc.vector.tensor_copy(windows[2][:].indirect(offsets[:]), dw_2[:])
         store(2)
-        dw_3 = gradient(3, every, 1, nc.scalar.copy, "dw_chain")
+        dw_3 = gradient(3, every, 4, nc.scalar.copy, "dw_chain")
         for h in range(2):
             scalar_scatter(3, h, dw_3[:, halves[h]])
         store(3)

from contextlib import ExitStack

import concourse.mybir as mybir
from concourse.masks import make_identity

F32 = mybir.dt.float32
BF16 = mybir.dt.bfloat16
I32 = mybir.dt.int32
U32 = mybir.dt.uint32
U16 = mybir.dt.uint16
U8 = mybir.dt.uint8
E4M3 = mybir.dt.float8_e4m3fn_x4
E5M2 = mybir.dt.float8_e5m2_x4
ALU = mybir.AluOpType
ACT = mybir.ActivationFunctionType

P = 128
LANES = 4
D = 512
ROWS = 512
SLOTS = 512
TOKENS = 2048
TABLES = 3
STUDENT = 2
VECTORS = 3
HALF = SLOTS // 2
RUN = 4
PLANE_BUFFERS = 8
BESIDE = 64
CHUNK = 512
CHUNKS = TOKENS // CHUNK
TS_BANK = 7
FLOPS = 4 * 2 * D * ROWS * SLOTS


def tile_attend_gkd2_pl_kernel(tc, xT, ws, wa, wb, us, ts, la, wt, offs, out_0, out_1, out_2):
    nc = tc.nc
    with ExitStack() as ctx:
        keep = ctx.enter_context(tc.tile_pool(name="keep", bufs=1))
        work = ctx.enter_context(tc.tile_pool(name="work", bufs=2))
        quad = ctx.enter_context(tc.tile_pool(name="quad", bufs=LANES))
        psum = ctx.enter_context(tc.psum_pool(name="psum", bufs=1))

        def bank_tile(number, shape):
            return psum.tile(shape, F32, name="bank", tag="bank%d" % number)

        x_raw = keep.tile([P, LANES, ROWS], F32, name="x_raw", align_bytes=64)
        nc.sync.dma_start(x_raw[:], xT.rearrange("(p j) r -> p j r", j=LANES))
        offsets = keep.tile([P, SLOTS // 16], U16, name="offsets")
        nc.sync.dma_start(offsets[:], offs)
        ts_window = keep.tile([P, TOKENS], F32, name="ts_window", align_bytes=64)
        nc.sync.dma_start(ts_window[P - 1 : P, :], ts[0:1, :])

        nc.vector.memset(ts_window[0 : P - 1, :], 0.0)
        vectors = keep.tile([P, ROWS], F32, name="vectors")
        first = P // 2 - VECTORS
        nc.vector.memset(vectors[0:first, :], 0.0)
        nc.vector.memset(vectors[P // 2 :, :], 0.0)
        for i, src in enumerate((us, la, wt)):
            nc.sync.dma_start(vectors[first + i : first + i + 1, :], src.rearrange("r o -> o r"))

        ident = keep.tile([P, P], F32, name="ident")
        make_identity(nc, ident[:])

        def plane_buffer(i):
            return "plane%d" % (i % PLANE_BUFFERS)

        planes = []
        for table in (wa, wb, ws):
            table_rows = table.rearrange("(p j) c -> p j c", j=LANES)
            for j in range(LANES):
                plane = keep.tile([P, TOKENS], F32, name="plane", tag=plane_buffer(len(planes)), align_bytes=64)
                nc.sync.dma_start(plane[:], table_rows[:, j, :])
                planes.append(plane)

        windows = []
        for j in range(LANES - 1):
            window = keep.tile([P, TOKENS], F32, name="window%d" % j)
            nc.vector.memset(window[:], 0.0)
            windows.append(window)

        xd_bf = keep.tile([P, ROWS * LANES], BF16, name="xd_bf", align_bytes=64)
        nc.scalar.activation(
            xd_bf[:].rearrange("p (t q j) -> p q j t", t=LANES, j=LANES),
            x_raw[:].rearrange("p j (q t) -> p q j t", t=LANES),
            ACT.Copy,
        )
        x_pairs = keep.tile([P, LANES * ROWS], BF16, name="x_pairs")
        nc.vector.tensor_copy(
            x_pairs[:].rearrange("q (j u p e) -> q j u p e", j=LANES, u=2, e=2),
            x_raw[:].rearrange("q j (p u e) -> q j u p e", u=2, e=2),
        )
        xd_codes = keep.tile([P, ROWS], U32, name="xd_codes", align_bytes=64)
        xd_scales = keep.tile([P, ROWS], U8, name="xd_scales", align_bytes=64)
        nc.vector.quantize_mx(xd_codes[:].bitcast(E4M3), xd_scales[:], xd_bf[:])

        windows.append(keep.tile([P, TOKENS], F32, name="window", tag="xd_bf", align_bytes=64))
        nc.vector.memset(windows[LANES - 1][:], 0.0)

        def block(i):
            return slice(i * P, (i + 1) * P)

        ts_row = keep.tile([P, SLOTS], F32, name="ts_row")
        nc.vector.tensor_copy(ts_row[:], ts_window[:].indirect(offsets[:]))
        bank = bank_tile(0, [P, LANES, P])
        for k in range(LANES):
            nc.tensor.transpose(bank[:, k, :], ts_row[:, block(k)], ident[:])
        ts_col = keep.tile([P, LANES], F32, name="ts_col")
        nc.vector.tensor_copy(ts_col[:], bank[:, :, P - 1])
        ts_bank = bank_tile(TS_BANK, [P, SLOTS])
        for k in range(LANES):
            nc.tensor.transpose(ts_bank[:, block(k)], ts_col[:, k : k + 1].to_broadcast([P, P]), ident[:])
        ts_all = keep.tile([P, SLOTS], F32, name="ts_all")
        nc.vector.tensor_copy(ts_all[:], ts_bank[:])

        bank = bank_tile(1, [P, LANES, P])
        for t in range(LANES):
            nc.tensor.transpose(bank[:, t, :], vectors[:, t::LANES], ident[:])
        by_row = keep.tile([P, VECTORS, LANES], F32, name="by_row")
        nc.vector.tensor_copy(by_row[:], bank[:, :, first : P // 2].rearrange("p t i -> p i t"))
        us_t, la_t, wt_t = (by_row[:, i, :] for i in range(VECTORS))

        neg_us = keep.tile([P, LANES], F32, name="neg_us")
        share = keep.tile([P, TABLES, LANES], F32, name="share")
        weight = share[:, STUDENT, :]
        nc.vector.tensor_scalar(neg_us[:], us_t, -1.0, None, ALU.mult)
        nc.vector.tensor_tensor(weight, wt_t, us_t, ALU.mult)
        nc.vector.scalar_tensor_tensor(share[:, 0, :], la_t, -1.0, weight, ALU.mult, ALU.mult)
        nc.vector.scalar_tensor_tensor(share[:, 1, :], la_t, -1.0, weight, ALU.add, ALU.mult)

        x_words = x_pairs[:].bitcast(F32)
        xr_bf = keep.tile([P, D * LANES], BF16, name="xr_bf", align_bytes=64)
        xr_words = xr_bf[:].bitcast(F32).rearrange("p (j q u) -> p j q u", j=LANES, u=2)
        for pair in range(2):
            bank = bank_tile(LANES + pair, [P, LANES, P])
            for i in range(LANES):
                nc.tensor.transpose(bank[:, i, :], x_words[:, block(LANES * pair + i)], ident[:])
            nc.vector.tensor_copy(
                xr_words[:, 2 * pair : 2 * pair + 2, :, :], bank[:].rearrange("p (j u) q -> p j q u", u=2)
            )
        xr_codes = keep.tile([P, D], U32, name="xr_codes", align_bytes=64)
        xr_scales = keep.tile([P, D], U8, name="xr_scales", align_bytes=64)
        nc.vector.quantize_mx(xr_codes[:].bitcast(E4M3), xr_scales[:], xr_bf[:])
        xd = (xd_codes, xd_scales)
        xr = (xr_codes, xr_scales)

        neg_max = keep.tile([P, TABLES, LANES], F32, name="neg_max")
        sums = {}
        last_sums = {}

        def new_sum(n, t):
            if n == STUDENT:
                sums[n, t] = keep.tile([P, 1], F32, name="sum", tag="sum%d" % t)[:]
            elif t == LANES - 1:
                sums[n, t] = last_sums[n][:, 1:2]
            else:
                held = keep.tile([P, 2], F32, name="sum", tag=plane_buffer(LANES * (n + 1) + t + 1), align_bytes=64)
                last_sums[n] = held
                sums[n, t] = held[:, 0:1]
            return sums[n, t]

        inv = keep.tile([P, TABLES, LANES], F32, name="inv")
        mix = keep.tile([P, LANES, SLOTS], F32, name="mix")
        e_b = keep.tile([P, LANES, SLOTS], F32, name="e_b")
        e_s = keep.tile([P, LANES, SLOTS], F32, name="e_s")
        exps = (mix, e_b, e_s)
        left, right, every = slice(0, HALF), slice(HALF, SLOTS), slice(0, SLOTS)
        halves = (left, right)

        def half_offsets(h):
            return offsets[:, h * (HALF // 16) : (h + 1) * (HALF // 16)]

        def half_buffer(n, h):
            return "w_bf%d_%d" % (h, n)

        def new_dense():
            return work.tile([P, LANES * HALF], F32, name="dense")

        def lanes_of(dense):
            return dense[:].bitcast(BF16).rearrange("p (j s) -> p j s", j=LANES)

        def ahead_of_gather(dense, j):
            return dense[:, j * HALF : j * HALF + 1]

        def gather(n, j, dense):
            nc.scalar.activation(lanes_of(dense)[:, j, :], planes[LANES * n + j][:].indirect(offsets[:]), ACT.Copy)

        def last_lane(n, dense):
            interleaved = [
                keep.tile([P, HALF * LANES], BF16, name="w_bf", tag=half_buffer(n, h), align_bytes=64)
                for h in range(2)
            ]
            codes = keep.tile([P, SLOTS], U32, name="w_codes%d" % n, align_bytes=64)
            scales = keep.tile([P, SLOTS], U8, name="w_scales%d" % n, align_bytes=64)
            last = LANES - 1
            for lo, hi in ((k * P, (k + 1) * P) for k in range(LANES)):
                nc.scalar.activation(
                    lanes_of(dense)[:, last, lo:hi],
                    planes[LANES * n + last][:].indirect(offsets[:, lo // 16 : hi // 16]),
                    ACT.Copy,
                )
                start = lo % HALF * LANES
                nc.vector.tensor_copy(
                    interleaved[lo // HALF][:, start : start + (hi - lo) * LANES].rearrange(
                        "p (c i j) -> p c j i", i=RUN, j=LANES
                    ),
                    lanes_of(dense)[:, :, lo:hi].rearrange("p j (c i) -> p c j i", i=RUN),
                )
            for h in range(2):
                nc.vector.quantize_mx(codes[:, halves[h]].bitcast(E4M3), scales[:, halves[h]], interleaved[h][:])
            return codes, scales

        def product(out, lhs, lhs_cols, rhs, rhs_cols, rhs_format=E4M3):
            nc.tensor.matmul_mx(
                out, lhsT=lhs[0][:, lhs_cols].bitcast(E4M3), lhsT_scale=lhs[1][:, lhs_cols],
                rhs=rhs[0][:, rhs_cols].bitcast(rhs_format), rhs_scale=rhs[1][:, rhs_cols], start=True, stop=True,
            )

        def row_scores(w, t):
            bank = bank_tile(t, [P, SLOTS])
            for cols in halves if t == 0 else (every,):
                product(bank[:, cols], xd, block(t), w, cols)
            return bank

        def logits(t, scores, z, cols=every):
            nc.vector.scalar_tensor_tensor(z, scores, us_t[:, t : t + 1], ts_all[:, cols], ALU.mult, ALU.mult)

        def maximum(z, negated):
            nc.vector.tensor_reduce(negated, z, mybir.AxisListType.X, ALU.max, negate=True)

        def exponential(n, t, z, negated_max, sign=1.0):
            nc.scalar.activation(exps[n][:, t, :], z, ACT.Exp, bias=negated_max, scale=sign, accum_out=new_sum(n, t))

        def invert(n, t):
            nc.vector.reciprocal(inv[:, n, t : t + 1], sums[n, t])

        coef = keep.tile([P, TABLES, LANES], F32, name="coef")

        def coefficient(n, t, inverse):
            nc.scalar.activation(coef[:, n, t : t + 1], inverse, ACT.Copy, scale=share[:, n, t : t + 1])

        def add_term(n, t, factors, cols):
            nc.vector.scalar_tensor_tensor(
                mix[:, t, cols], exps[n][:, t, cols], factors[:, t : t + 1], mix[:, t, cols], ALU.mult, ALU.add
            )

        def scale_beside(n, t, inverse):
            e = exps[n]
            nc.gpsimd.tensor_scalar(e[:, t, :], e[:, t, :], inverse, share[:, n, t : t + 1], ALU.mult, ALU.mult)

        def add_beside(t):
            nc.gpsimd.tensor_tensor(mix[:, t, :], mix[:, t, :], e_b[:, t, :], ALU.add)

        def finish_teacher(n):
            late = keep.tile([P, LANES], F32, name="late", tag=half_buffer(n + 1, 1), align_bytes=64)
            if n == 0:
                nc.vector.reciprocal(late[:, 1:2], sums[n, 1])
            nc.vector.reciprocal(late[:, 2:4], last_sums[n][:])
            if n == 0:
                for t in range(1, LANES):
                    scale_beside(n, t, late[:, t : t + 1])
            else:
                scale_beside(n, 2, late[:, 2:3])
                coefficient(n, 3, late[:, 3:4])
                nc.scalar.activation(e_b[:, 3, :], e_b[:, 3, :], ACT.Copy, scale=coef[:, n, 3:4])
                for t in (2, 3):
                    add_beside(t)

        dense = new_dense()
        for j in range(LANES - 1):
            gather(0, j, dense)
        w = last_lane(0, dense)
        for n in range(STUDENT):
            dense = new_dense()
            gather(n + 1, 0, dense)
            gather(n + 1, 1, dense)
            banks = [row_scores(w, t) for t in range(LANES)]
            z = [quad.tile([P, SLOTS], F32, name="z") for t in range(LANES - 1)]
            logits(0, banks[0][:], z[0][:])
            logits(1, banks[1][:], z[1][:])
            maximum(z[0][:], ahead_of_gather(dense, 2))
            exponential(n, 0, z[0][:], ahead_of_gather(dense, 2))
            gather(n + 1, 2, dense)
            logits(2, banks[2][:], z[2][:])
            maximum(z[1][:], ahead_of_gather(dense, 3))
            exponential(n, 1, z[1][:], ahead_of_gather(dense, 3))
            invert(n, 0)
            scale_beside(n, 0, inv[:, n, 0:1])
            if n == 1:
                add_beside(0)
            z.append(keep.tile([P, SLOTS], F32, name="z", tag=plane_buffer(LANES * (n + 1) + 1), align_bytes=64))
            logits(3, banks[3][:], z[3][:])
            for t in (2, 3):
                maximum(z[t][:], neg_max[:, n, t : t + 1])
            if n == 1:
                invert(n, 1)
                nc.vector.tensor_tensor(coef[:, n, 1:2], inv[:, n, 1:2], share[:, n, 1:2], ALU.mult)
                add_term(n, 1, coef[:, n, :], every)
            w = last_lane(n + 1, dense)
            for t in (2, 3):
                exponential(n, t, z[t][:], neg_max[:, n, t : t + 1])
            finish_teacher(n)

        z = [quad.tile([P, SLOTS], F32, name="z") for t in range(LANES)]
        for h in range(2):
            for t in range(2):
                bank = bank_tile(LANES * (1 - h) + t, [P, HALF])
                product(bank[:], xd, block(t), w, halves[h])
                logits(t, bank[:], z[t][:, halves[h]], halves[h])
        logits(2, row_scores(w, 2)[:], z[2][:])
        scaled = []
        for pair, bank_number in enumerate((3, 6)):
            bank = bank_tile(bank_number, [P, 2, P])
            for i in range(2):
                product(bank[:, i, :], w, block(2 * pair + i), xd, block(3))
            for i in range(2):
                k = 2 * pair + i
                scaled.append(quad.tile([P, P], F32, name="scaled"))
                nc.scalar.activation(scaled[k][:], bank[:, i, :], ACT.Copy, scale=ts_col[:, k : k + 1])
        turned = bank_tile(5, [P, SLOTS])
        for k in range(LANES):
            nc.tensor.transpose(turned[:, block(k)], scaled[k][:], ident[:])
        for t in range(LANES - 1):
            maximum(z[t][:], neg_max[:, STUDENT, t : t + 1])
            exponential(STUDENT, t, z[t][:], neg_max[:, STUDENT, t : t + 1])

        def student_coefficient(t):
            invert(STUDENT, t)
            coefficient(STUDENT, t, inv[:, STUDENT, t : t + 1])

        student_coefficient(0)
        nc.vector.tensor_scalar(
            z[3][:], turned[:], neg_us[:, 3:4], None, ALU.mult, ALU.min, accum_out=neg_max[:, STUDENT, 3:4]
        )
        exponential(STUDENT, 3, z[3][:], neg_max[:, STUDENT, 3:4], -1.0)
        third, fourth = block(2), block(3)
        terms = keep.tile([P, LANES, P], F32, name="terms")
        summed = bank_tile(2, [P, LANES, P])
        for t in range(LANES):
            nc.tensor.matmul(summed[:, t, :], mix[:, t, fourth], ident[:], start=t == 0, stop=False, is_transpose=True)

        def add_turned(t):
            nc.tensor.matmul(
                summed[:, t, :], terms[:, t, :], ident[:], start=False, stop=t == LANES - 1, is_transpose=True
            )

        for t in range(LANES - 1):
            student_coefficient(t + 1)
            add_term(STUDENT, t, coef[:, STUDENT, :], left)
            nc.vector.tensor_scalar(terms[:, t, :], e_s[:, t, fourth], coef[:, STUDENT, t : t + 1], None, ALU.mult)
            add_turned(t)
        nc.scalar.activation(terms[:, 3, :], e_s[:, 3, fourth], ACT.Copy, scale=coef[:, STUDENT, 3:4])
        add_turned(3)
        for k in range(2):
            add_term(STUDENT, LANES - 1, coef[:, STUDENT, :], block(k))
        coef_late = keep.tile([P, LANES], F32, name="coef_late")
        nc.scalar.copy(coef_late[:], coef[:, STUDENT, :])

        g_bf = [keep.tile([P, P * LANES], BF16, name="g_bf", tag="g_bf%d" % k, align_bytes=64) for k in range(LANES)]

        def g_words(lo, hi):
            return g_bf[lo // P][:, lo % P * LANES : (lo % P + hi - lo) * LANES]

        g_codes = keep.tile([P, SLOTS], U32, name="g_codes", align_bytes=64)
        g_scales = keep.tile([P, SLOTS], U8, name="g_scales", align_bytes=64)
        g = (g_codes, g_scales)

        back = bank_tile(3, [P, 2, P])

        def turn_back(u, buffer):
            by_slot = keep.tile([P, 2 * P], BF16, name="by_slot", tag=buffer, align_bytes=64)
            nc.scalar.activation(
                by_slot[:].rearrange("s (p e) -> s p e", e=2),
                summed[:].rearrange("s (u e) p -> s u p e", u=2)[:, u],
                ACT.Copy, scale=ts_col[:, 3:4],
            )
            nc.tensor.transpose(back[:, u, :], by_slot[:].bitcast(F32), ident[:])

        turn_back(0, "by_slot")

        def round_g(lo, hi):
            nc.vector.tensor_tensor(
                g_words(lo, hi).rearrange("p (c i t) -> p c t i", i=RUN, t=LANES),
                mix[:, :, lo:hi].rearrange("p t (c i) -> p c t i", i=RUN),
                ts_bank[:, lo:hi].rearrange("p (c i) -> p c i", i=RUN).unsqueeze(2).to_broadcast(
                    [P, (hi - lo) // RUN, LANES, RUN]
                ),
                ALU.mult,
            )

        def round_g_beside(lo, hi):
            nc.gpsimd.tensor_tensor(
                g_words(lo, hi).rearrange("p (s t) -> p s t", t=LANES),
                mix[:, :, lo:hi].rearrange("p t s -> p s t"),
                ts_all[:, lo:hi].unsqueeze(2).to_broadcast([P, hi - lo, LANES]),
                ALU.mult,
            )

        def quantise_g(lo, hi):
            nc.vector.quantize_mx(
                g_codes[:, lo:hi].bitcast(E5M2), g_scales[:, lo:hi], g_words(lo, hi)
            )

        def gradient(j, cols, bank_number, copy, buffer):
            width = cols.stop - cols.start
            bank = bank_tile(bank_number, [P, width])
            product(bank[:], xr, block(j), g, cols, E5M2)
            dw = keep.tile([P, width], F32, name="dw", tag=buffer, align_bytes=64)
            copy(dw[:], bank[:])
            return dw

        out_rows = out_0.rearrange("(q j) c -> q j c", j=LANES)
        sides = [
            keep.tile([P, 2, 2, CHUNK, 2], BF16, name="rounded", tag=plane_buffer(LANES * s), align_bytes=64)
            for s in range(2)
        ]

        def lane_of(j, s):
            return sides[s][:, :, j // 2, :, j % 2]

        def scalar_scatter(j, h, dw):
            nc.scalar.activation(windows[j][:].indirect(half_offsets(h)), dw, ACT.Copy)

        def store(j):
            nc.sync.dma_start(out_rows[:, j, :], windows[j][:])

        def side_of(j, s):
            return windows[j][:, 2 * s * CHUNK : 2 * (s + 1) * CHUNK].rearrange("p (c k) -> p c k", c=2)

        def new_one():
            one = keep.tile([P, 1], F32, name="one")
            nc.gpsimd.memset(one[:], 1.0)
            return one

        first_one = new_one()
        round_g(0, P)
        round_g(P, HALF - BESIDE)
        round_g_beside(HALF - BESIDE, HALF)
        dw_0_left = keep.tile([P, HALF], F32, name="dw", tag="dw_chain", align_bytes=64)
        for k in range(2):
            quantise_g(k * P, (k + 1) * P)
            bank = bank_tile(4 + k, [P, P])
            product(bank[:], xr, block(0), g, block(k), E5M2)
            if k == 0:
                turn_back(1, "g_bf0")
            nc.scalar.copy(dw_0_left[:, block(k)], bank[:])
        dw_1_left = gradient(1, left, 6, nc.scalar.copy, "dw_1_left")
        scalar_scatter(0, 0, dw_0_left[:])
        for t in range(LANES):
            add_term(STUDENT, t, coef_late, third)
        round_g(HALF, HALF + P - BESIDE // 2)
        round_g_beside(HALF + P - BESIDE // 2, HALF + P)
        nc.vector.tensor_copy(
            g_bf[3][:].bitcast(F32).rearrange("p (s u) -> p s u", u=2), back[:].rearrange("p u s -> p s u")
        )
        bank = bank_tile(1, [P, HALF])
        for k in range(2):
            quantise_g(HALF + k * P, HALF + (k + 1) * P)
            product(bank[:, block(k)], xr, block(0), g, block(2 + k), E5M2)
        dw_0_right = keep.tile([P, HALF], F32, name="dw", tag="dw0_256", align_bytes=64)
        nc.vector.tensor_copy(dw_0_right[:], bank[:])
        dw_1_right = gradient(1, right, 0, nc.vector.tensor_copy, "dw1_256")
        dw_2 = gradient(2, every, 0, nc.vector.tensor_copy, "dw_2")
        nc.vector.tensor_copy(windows[0][:].indirect(half_offsets(1)), dw_0_right[:])
        store(0)
        scalar_scatter(1, 0, dw_1_left[:])
        scalar_scatter(1, 1, dw_1_right[:])
        store(1)
        for s in range(2):
            nc.gpsimd.tensor_scalar(lane_of(0, s), side_of(0, s), first_one[:], first_one[:], ALU.mult, ALU.mult)
        second_one = new_one()
        nc.vector.tensor_copy(windows[2][:].indirect(offsets[:]), dw_2[:])
        store(2)
        dw_3 = gradient(3, every, 4, nc.scalar.copy, "dw_chain")
        for h in range(2):
            scalar_scatter(3, h, dw_3[:, halves[h]])
        store(3)

        nc.vector.tensor_scalar(lane_of(1, 0), side_of(1, 0), second_one[:], None, ALU.mult)
        for c, cols in ((0, every), (1, left)):
            nc.vector.tensor_scalar(lane_of(1, 1)[:, c, cols], side_of(1, 1)[:, c, cols], second_one[:], None, ALU.mult)
        nc.vector.tensor_scalar(lane_of(2, 0), side_of(2, 0), second_one[:], None, ALU.mult)
        last_one = keep.tile([P, 1], F32, name="last_one", tag="dw_chain", align_bytes=64)
        nc.vector.tensor_copy(last_one[:], second_one[:])
        for c in range(2):
            nc.vector.tensor_scalar(lane_of(3, 0)[:, c, :], side_of(3, 0)[:, c, :], second_one[:], None, ALU.mult)
        for c in range(2):
            nc.scalar.copy(lane_of(3, 1)[:, c, :], side_of(3, 1)[:, c, :])
            nc.scalar.activation(lane_of(2, 1)[:, c, :], side_of(2, 1)[:, c, :], ACT.Copy, scale=last_one[:])
        nc.scalar.activation(lane_of(1, 1)[:, 1, right], side_of(1, 1)[:, 1, right], ACT.Copy, scale=last_one[:])

        woven = [
            keep.tile([P, TOKENS // 2 * LANES], BF16, name="woven", tag=tag, align_bytes=64)
            for tag in ("x_raw", "ts_window")
        ]
        o_codes = keep.tile([P, TOKENS], U32, name="o_codes", align_bytes=64)
        o_scales = keep.tile([P, CHUNK], U8, name="o_scales", align_bytes=64)
        words = out_1[0].rearrange("p c l -> p (c l)").bitcast(I32)

        def weave(copy, c):
            dst = woven[c // 2][:].bitcast(F32).rearrange("p (c k u) -> p c k u", c=2, u=2)[:, c % 2]
            src = sides[c // 2][:].rearrange("p c u k e -> p (c u k e)").bitcast(F32)
            copy(dst, src.rearrange("p (c u k) -> p c k u", c=2, u=2)[:, c % 2])

        def quantise_out(c):
            cols = slice(c * CHUNK, (c + 1) * CHUNK)
            nc.vector.quantize_mx(
                o_codes[:, cols].bitcast(E4M3), o_scales[LANES * c :, :],
                woven[c // 2][:, c % 2 * CHUNK * LANES : (c % 2 + 1) * CHUNK * LANES],
            )
            nc.sync.dma_start(words[:, cols], o_codes[:, cols].bitcast(I32))

        weave(nc.vector.tensor_copy, 0)
        weave(nc.vector.tensor_copy, 1)
        quantise_out(0)
        weave(nc.vector.tensor_copy, 2)
        weave(nc.scalar.copy, 3)
        for c in range(1, CHUNKS):
            quantise_out(c)
        for q in range(P // 32):
            queue = nc.scalar if q % 2 == 0 else nc.sync
            queue.dma_start(
                out_2[0, 4 * q : 4 * q + 4, :].bitcast(I32).rearrange("r (c k) -> c r k", c=CHUNKS),
                o_scales[32 * q : 32 * q + 16, :].bitcast(I32),
            )
